import numpy as np
import ml_dtypes


def mxq(x, axis, fmt="e4m3"):
    dtype, down = {"e4m3": (ml_dtypes.float8_e4m3fn, 7), "e5m2": (ml_dtypes.float8_e5m2, 14)}[fmt]
    v = np.moveaxis(np.asarray(x, np.float32).astype(ml_dtypes.bfloat16).astype(np.float64), axis, -1)
    blocks = v.reshape(v.shape[:-1] + (-1, 32))
    amax = np.abs(blocks).max(-1, keepdims=True)
    byte = np.maximum(np.where(amax > 0, np.frexp(amax)[1] - 1 + 127, 0) - down, 1)
    scale = np.exp2(byte - 127.0)
    codes = (blocks / scale).astype(np.float32).astype(dtype).astype(np.float64)
    return np.moveaxis((codes * scale).reshape(v.shape), -1, axis)


WIDE = False


def mx_kscale(k):
    if not WIDE:
        return np.ones(k)
    levels = np.array([10, -10, 5, -5, 0])
    if k % 512:
        return np.exp2(np.random.permutation(np.resize(levels, k // 32))).repeat(32)
    a = np.empty((k // 512, 16))
    for p in range(k // 512):
        a[p, :8] = np.random.permutation(np.resize(levels, 8))
        for g in range(8):
            far = levels[np.abs(levels - a[p, g]) >= 10]
            a[p, g + 8] = far[np.random.randint(len(far))]
    return np.exp2(a.ravel()).repeat(32)


def f64(x):
    return np.asarray(x).astype(np.float64)


def striped(idx):
    return np.tile(idx.reshape(-1, 16).T, (8, 1)).astype(np.uint16)


def unstriped(offs):
    return offs[:16].T.reshape(-1).astype(np.int64)


E2M1 = np.array([0.0, 0.5, 1.0, 1.5, 2.0, 3.0, 4.0, 6.0, -0.0, -0.5, -1.0, -1.5, -2.0, -3.0, -4.0, -6.0])


def pack_weight(w, fmt):
    k, n = w.shape
    w = f64(np.asarray(w, np.float32).astype(ml_dtypes.bfloat16)).reshape(k // 32, 32, n)
    amax = np.abs(w).max(1)
    if fmt == "e4m3":
        byte = np.frexp(amax)[1] - 1 + 127 - 7
    else:
        mant, ex = np.frexp(amax / 6.0)
        byte = np.where(mant > 0.5, ex, ex - 1) + 127
    byte = np.clip(np.where(amax > 0, byte, 1), 1, 254)
    scaled = (w * np.exp2(127.0 - byte)[:, None, :]).reshape(k, n).astype(np.float32)
    by_word = np.ascontiguousarray(scaled.reshape(k // 512, 128, 4, n).transpose(0, 1, 3, 2))
    if fmt == "e4m3":
        words = by_word.astype(ml_dtypes.float8_e4m3fn).view(np.uint8)
    else:
        c = by_word.astype(ml_dtypes.float4_e2m1fn).view(np.uint8) & 0xF
        words = (c[..., 0::2] | (c[..., 1::2] << 4)).reshape(k // 512, 128, 2 * n)
    return np.ascontiguousarray(words), np.ascontiguousarray(byte.astype(np.uint8).reshape(k // 512, 16, n))


def unpack_weight(words, scales, fmt):
    g, _, n = scales.shape
    words = np.ascontiguousarray(words).reshape(g, 128, n, -1)
    if fmt == "e4m3":
        vals = words.view(ml_dtypes.float8_e4m3fn).astype(np.float64)
    else:
        nib = np.empty((g, 128, n, 4), np.uint8)
        nib[..., 0::2] = words & 0xF
        nib[..., 1::2] = words >> 4
        vals = E2M1[nib]
    vals = vals * np.repeat(np.exp2(scales.astype(np.float64) - 127.0), 8, axis=1)[..., None]
    return vals.transpose(0, 1, 3, 2).reshape(g * 512, n)


def silu(v):
    return v / (1.0 + np.exp(-np.maximum(v, -700.0)))


K, T, E, C, N = 512, 2048, 8, 256, 128


def by_expert(wq, xq):
    return np.concatenate([wq[e].T @ xq[:, e * C:(e + 1) * C] for e in range(E)], axis=1)


def setup_inputs():
    n = np.random.standard_normal
    s = mx_kscale(K)[:, None]
    x = pack_weight(n((K, T)) * s, "e4m3")
    return {
        "x_words": x[0],
        "x_scales": x[1],
        "w": (n((E + 1, K, N)) / np.sqrt(K) / s[None]).astype(np.float32),
        "b": (0.3 * n((N, E + 1))).astype(np.float32),
        "gate": np.tile(np.random.uniform(0.2, 1.0, E * C), (N, 1)).astype(np.float32),
        "offs": striped(np.random.permutation(T)[:E * C]),
    }


def reference(x_words, x_scales, w, b, gate, offs):
    idx = unstriped(offs)
    wq = mxq(f64(w), 1, "e4m3")
    xs = unpack_weight(x_words, x_scales, "e4m3")
    ys = silu((wq[E].T @ xs) + f64(b)[:, E:])
    xq = unpack_weight(x_words, x_scales, "e4m3")[:, idx]
    y = by_expert(wq, xq)
    y = silu(y + np.repeat(f64(b)[:, :E], C, axis=1))
    out = ys
    out[:, idx] += f64(gate) * y
    return out

@@ -1,0 +1,156 @@
+from contextlib import ExitStack
+
+import concourse.mybir as mybir
+
+K, T, E, C, N = 512, 2048, 8, 256, 128
+FLOPS = 2 * K * N * (E * C + T)
+
+F32 = mybir.dt.float32
+BF16 = mybir.dt.bfloat16
+I32 = mybir.dt.int32
+U32 = mybir.dt.uint32
+U16 = mybir.dt.uint16
+U8 = mybir.dt.uint8
+FP8X4 = mybir.dt.float8_e4m3fn_x4
+SILU = mybir.ActivationFunctionType.Silu
+MULT = mybir.AluOpType.mult
+ADD = mybir.AluOpType.add
+
+P = 128
+PACK = 4
+BANK = 512
+HALF = T // 2
+EH = E // 2
+STORE_WIDTHS = (768, 640, 384, 256)
+
+
+def tile_moe_shr_lin_silu_kernel(tc, x_words, x_scales, w, b, gate, offs, out):
+    nc = tc.nc
+    with ExitStack() as ctx:
+        keep = ctx.enter_context(tc.tile_pool(name="keep", bufs=1))
+        psum = ctx.enter_context(tc.psum_pool(name="psum", bufs=1))
+
+        offsets = keep.tile([P, T // 16], U16, name="offsets")
+        nc.sync.dma_start(offsets[:], offs)
+
+        def half_list(h):
+            return offsets[:, h * HALF // 16 : (h + 1) * HALF // 16]
+
+        plane = keep.tile([P, T], U8, name="plane", align_bytes=64)
+        nc.vector.memset(plane[:].bitcast(I32), 0)
+        rows = x_scales[0].rearrange("(q r) t -> r q t", r=4)
+        for r in range(4):
+            nc.scalar.dma_start(plane[r:P:32, :].bitcast(I32), rows[r].bitcast(I32))
+
+        warm = keep.tile([P, 2], F32, name="warm")
+        nc.vector.memset(warm[:, 0:1], 0.0)
+        nc.scalar.activation(warm[:, 1:2], warm[:, 0:1], SILU)
+
+        bias = keep.tile([P, E + 1], F32, name="bias")
+        nc.gpsimd.dma_start(bias[:], b)
+
+        def load_w(first, count, tag):
+            raw = keep.tile([P, count, PACK, N], F32, name="raw%d" % first, tag=tag, align_bytes=64)
+            nc.sync.dma_start(raw[:], w[first : first + count].rearrange("e (p j) n -> p e j n", j=PACK))
+            return raw
+
+        def round_w(raw, count, tag):
+            grouped = keep.tile([P, count, N, PACK], BF16, name="grouped_" + tag, tag=tag, align_bytes=64)
+            for e in range(count):
+                nc.scalar.copy(
+                    grouped[:, e].rearrange("p (c i) j -> p c j i", i=4),
+                    raw[:, e].rearrange("p j (c i) -> p c j i", i=4),
+                )
+            return grouped
+
+        def quantize_w(grouped, first, count, tag):
+            codes = keep.tile([P, count * N], U32, name="codes_" + tag, tag=tag, align_bytes=64)
+            scales = keep.tile([P, count * N], U8, name="scales_" + tag, align_bytes=64)
+            nc.vector.quantize_mx(
+                out=codes[:].bitcast(FP8X4), scales=scales[:], in_=grouped[:, first : first + count].rearrange("p e n j -> p (e n j)")
+            )
+            return codes, scales
+
+        def gather_bytes(h):
+            got = keep.tile([P, HALF], U8, name="slot_bytes%d" % h, align_bytes=64)
+            nc.vector.tensor_copy(got[:], plane[:].indirect(half_list(h)))
+            return got
+
+        def gather_words(h, tag):
+            got = keep.tile([P, HALF], U32, name="slot_words%d" % h, tag=tag, align_bytes=64)
+            nc.vector.tensor_copy(got[:], words[:].bitcast(U32).indirect(half_list(h)))
+            return got
+
+        def routed(h, codes, scales, slot_words, slot_bytes, tag):
+            y = keep.tile([P, HALF], F32, name="y%d" % h, tag=tag, align_bytes=64)
+            for pair in range(EH // 2):
+                acc = psum.tile([P, BANK], F32, name="acc%d_%d" % (h, pair), tag="bank%d" % (2 * (1 - h) + pair))
+                for i in range(2):
+                    e = 2 * pair + i
+                    nc.tensor.matmul_mx(
+                        out=acc[:, i * C : (i + 1) * C],
+                        lhsT=codes[:, e * N : (e + 1) * N].bitcast(FP8X4),
+                        lhsT_scale=scales[:, e * N : (e + 1) * N],
+                        rhs=slot_words[:, e * C : (e + 1) * C].bitcast(FP8X4),
+                        rhs_scale=slot_bytes[:, e * C : (e + 1) * C],
+                        start=True,
+                        stop=True,
+                    )
+                for i in range(2):
+                    e = 2 * pair + i
+                    col = h * EH + e
+                    nc.scalar.activation(
+                        y[:, e * C : (e + 1) * C], acc[:, i * C : (i + 1) * C], SILU, bias=bias[:, col : col + 1]
+                    )
+            return y
+
+        def load_gate(h, tag):
+            g = keep.tile([P, HALF], F32, name="gate%d" % h, tag=tag, align_bytes=64)
+            nc.sync.dma_start(g[:], gate[:, h * HALF : (h + 1) * HALF])
+            return g
+
+        raw_a = load_w(EH, EH + 1, "raw_a")
+        words = keep.tile([P, T], I32, name="words", align_bytes=64)
+        nc.sync.dma_start(words[:], x_words[0].rearrange("p t r -> p (t r)").bitcast(I32))
+        raw_b = load_w(0, EH, "raw_b")
+
+        bytes_a = gather_bytes(1)
+        bytes_b = gather_bytes(0)
+        grouped_a = round_w(raw_a, EH + 1, "grouped_a")
+        codes_a, scales_a = quantize_w(grouped_a, 0, EH, "codes_a")
+        codes_s, scales_s = quantize_w(grouped_a, EH, 1, "codes_s")
+        gate_a = load_gate(1, "raw_a")
+        words_a = gather_words(1, "words_a")
+        words_b = gather_words(0, "grouped_a")
+        grouped_b = round_w(raw_b, EH, "grouped_b")
+        y_a = routed(1, codes_a, scales_a, words_a, bytes_a, "raw_b")
+        codes_b, scales_b = quantize_w(grouped_b, 0, EH, "codes_b")
+        gate_b = load_gate(0, "codes_a")
+
+        window = keep.tile([P, T], F32, name="window", tag="grouped_b", align_bytes=64)
+        nc.vector.tensor_tensor(window[:].indirect(half_list(1)), y_a[:], gate_a[:], MULT)
+
+        y_b = routed(0, codes_b, scales_b, words_b, bytes_b, "y_b")
+        nc.vector.tensor_tensor(window[:].indirect(half_list(0)), y_b[:], gate_b[:], MULT)
+
+        total = keep.tile([P, T], F32, name="total", align_bytes=64)
+        for c in range(T // BANK):
+            cols = slice(c * BANK, (c + 1) * BANK)
+            acc = psum.tile([P, BANK], F32, name="acc_s%d" % c, tag="bank%d" % c)
+            nc.tensor.matmul_mx(
+                out=acc[:],
+                lhsT=codes_s[:].bitcast(FP8X4),
+                lhsT_scale=scales_s[:],
+                rhs=words[:, cols].bitcast(FP8X4),
+                rhs_scale=plane[:, cols],
+                start=True,
+                stop=True,
+            )
+            nc.scalar.activation(total[:, cols], acc[:], SILU, bias=bias[:, E : E + 1])
+
+        start = 0
+        for width in STORE_WIDTHS:
+            cols = slice(start, start + width)
+            nc.vector.tensor_tensor(total[:, cols], total[:, cols], window[:, cols], ADD)
+            nc.sync.dma_start(out[:, cols], total[:, cols])
+            start = start + width

@@ -36,18 +36,19 @@ def tile_moe_shr_lin_silu_kernel(tc, x_words, x_scales, w, b, gate, offs, out):
         def half_list(h):
             return offsets[:, h * HALF // 16 : (h + 1) * HALF // 16]
 
+        bias = keep.tile([P, E + 1], F32, name="bias")
+        nc.sync.dma_start(bias[:], b)
+
         plane = keep.tile([P, T], U8, name="plane", align_bytes=64)
         nc.vector.memset(plane[:].bitcast(I32), 0)
         rows = x_scales[0].rearrange("(q r) t -> r q t", r=4)
         for r in range(4):
-            nc.scalar.dma_start(plane[r:P:32, :].bitcast(I32), rows[r].bitcast(I32))
+            nc.sync.dma_start(plane[r:P:32, :].bitcast(I32), rows[r].bitcast(I32))
 
         warm = keep.tile([P, 2], F32, name="warm")
         nc.vector.memset(warm[:, 0:1], 0.0)
         nc.scalar.activation(warm[:, 1:2], warm[:, 0:1], SILU)
 
-        bias = keep.tile([P, E + 1], F32, name="bias")
-        nc.gpsimd.dma_start(bias[:], b)
 
         def load_w(first, count, tag):
             raw = keep.tile([P, count, PACK, N], F32, name="raw%d" % first, tag=tag, align_bytes=64)

@@ -21,7 +21,7 @@ PACK = 4
 BANK = 512
 HALF = T // 2
 EH = E // 2
-STORE_WIDTHS = (768, 640, 384, 256)
+STORE_WIDTHS = (512, 512, 512, 512)
 
 
 def tile_moe_shr_lin_silu_kernel(tc, x_words, x_scales, w, b, gate, offs, out):
@@ -53,14 +53,14 @@ def tile_moe_shr_lin_silu_kernel(tc, x_words, x_scales, w, b, gate, offs, out):
         def load_w(first, count, tag):
             raw = keep.tile([P, count, PACK, N], F32, name="raw%d" % first, tag=tag, align_bytes=64)
             nc.sync.dma_start(raw[:], w[first : first + count].rearrange("e (p j) n -> p e j n", j=PACK))
-            return raw
+            return [raw[:, e] for e in range(count)]
 
-        def round_w(raw, count, tag):
-            grouped = keep.tile([P, count, N, PACK], BF16, name="grouped_" + tag, tag=tag, align_bytes=64)
-            for e in range(count):
+        def round_w(raws, tag):
+            grouped = keep.tile([P, len(raws), N, PACK], BF16, name="grouped_" + tag, tag=tag, align_bytes=64)
+            for e, raw in enumerate(raws):
                 nc.scalar.copy(
                     grouped[:, e].rearrange("p (c i) j -> p c j i", i=4),
-                    raw[:, e].rearrange("p j (c i) -> p c j i", i=4),
+                    raw.rearrange("p j (c i) -> p c j i", i=4),
                 )
             return grouped
 
@@ -85,7 +85,7 @@ def tile_moe_shr_lin_silu_kernel(tc, x_words, x_scales, w, b, gate, offs, out):
         def routed(h, codes, scales, slot_words, slot_bytes, tag):
             y = keep.tile([P, HALF], F32, name="y%d" % h, tag=tag, align_bytes=64)
             for pair in range(EH // 2):
-                acc = psum.tile([P, BANK], F32, name="acc%d_%d" % (h, pair), tag="bank%d" % (2 * (1 - h) + pair))
+                acc = psum.tile([P, BANK], F32, name="acc%d_%d" % (h, pair))
                 for i in range(2):
                     e = 2 * pair + i
                     nc.tensor.matmul_mx(
@@ -110,34 +110,36 @@ def tile_moe_shr_lin_silu_kernel(tc, x_words, x_scales, w, b, gate, offs, out):
             nc.sync.dma_start(g[:], gate[:, h * HALF : (h + 1) * HALF])
             return g
 
-        raw_a = load_w(EH, EH + 1, "raw_a")
+        raw_a = load_w(0, EH, "raw_a")
         words = keep.tile([P, T], I32, name="words", align_bytes=64)
         nc.sync.dma_start(words[:], x_words[0].rearrange("p t r -> p (t r)").bitcast(I32))
-        raw_b = load_w(0, EH, "raw_b")
+        raw_b = load_w(EH, 2, "raw_b1") + load_w(EH + 2, 2, "raw_b2")
 
-        bytes_a = gather_bytes(1)
-        bytes_b = gather_bytes(0)
-        grouped_a = round_w(raw_a, EH + 1, "grouped_a")
+        bytes_a = gather_bytes(0)
+        bytes_b = gather_bytes(1)
+        grouped_a = round_w(raw_a, "grouped_a")
         codes_a, scales_a = quantize_w(grouped_a, 0, EH, "codes_a")
-        codes_s, scales_s = quantize_w(grouped_a, EH, 1, "codes_s")
-        gate_a = load_gate(1, "raw_a")
-        words_a = gather_words(1, "words_a")
-        words_b = gather_words(0, "grouped_a")
-        grouped_b = round_w(raw_b, EH, "grouped_b")
-        y_a = routed(1, codes_a, scales_a, words_a, bytes_a, "raw_b")
+        gate_a = load_gate(0, "raw_a")
+        words_a = gather_words(0, "words_a")
+        words_b = gather_words(1, "grouped_a")
+        grouped_b = round_w(raw_b, "grouped_b")
+        y_a = routed(0, codes_a, scales_a, words_a, bytes_a, "raw_b2")
         codes_b, scales_b = quantize_w(grouped_b, 0, EH, "codes_b")
-        gate_b = load_gate(0, "codes_a")
+        gate_b = load_gate(1, "codes_a")
+        raw_s = load_w(E, 1, "raw_b1")
 
-        window = keep.tile([P, T], F32, name="window", tag="grouped_b", align_bytes=64)
-        nc.vector.tensor_tensor(window[:].indirect(half_list(1)), y_a[:], gate_a[:], MULT)
+        window = keep.tile([P, T], F32, name="window", align_bytes=64)
+        nc.vector.tensor_tensor(window[:].indirect(half_list(0)), y_a[:], gate_a[:], MULT)
 
-        y_b = routed(0, codes_b, scales_b, words_b, bytes_b, "y_b")
-        nc.vector.tensor_tensor(window[:].indirect(half_list(0)), y_b[:], gate_b[:], MULT)
+        grouped_s = round_w(raw_s, "grouped_s")
+        codes_s, scales_s = quantize_w(grouped_s, 0, 1, "raw_a")
+        y_b = routed(1, codes_b, scales_b, words_b, bytes_b, "raw_b1")
+        nc.vector.tensor_tensor(window[:].indirect(half_list(1)), y_b[:], gate_b[:], MULT)
 
         total = keep.tile([P, T], F32, name="total", align_bytes=64)
         for c in range(T // BANK):
             cols = slice(c * BANK, (c + 1) * BANK)
-            acc = psum.tile([P, BANK], F32, name="acc_s%d" % c, tag="bank%d" % c)
+            acc = psum.tile([P, BANK], F32, name="acc_s%d" % c)
             nc.tensor.matmul_mx(
                 out=acc[:],
                 lhsT=codes_s[:].bitcast(FP8X4),

@@ -17,143 +17,153 @@ MULT = mybir.AluOpType.mult
 ADD = mybir.AluOpType.add
 
 P = 128
+QUADRANT = 32
+SCALE_ROWS = 4
 PACK = 4
+RUN = 4
+LIST_COLUMN = 16
 BANK = 512
-HALF = T // 2
-EH = E // 2
-STORE_WIDTHS = (512, 512, 512, 512)
+PAIR = BANK // C
+HALF_SLOTS = E * C // 2
+HALF_EXPERTS = E // 2
+ALIGN = 64
+STORE_WIDTHS = (256, 384, 384, 384, 384, 256)
+assert sum(STORE_WIDTHS) == T
 
 
 def tile_moe_shr_lin_silu_kernel(tc, x_words, x_scales, w, b, gate, offs, out):
     nc = tc.nc
     with ExitStack() as ctx:
-        keep = ctx.enter_context(tc.tile_pool(name="keep", bufs=1))
+        sbuf = ctx.enter_context(tc.tile_pool(name="sbuf", bufs=1))
         psum = ctx.enter_context(tc.psum_pool(name="psum", bufs=1))
 
-        offsets = keep.tile([P, T // 16], U16, name="offsets")
+        offsets = sbuf.tile([P, E * C // LIST_COLUMN], U16, name="offsets")
         nc.sync.dma_start(offsets[:], offs)
 
-        def half_list(h):
-            return offsets[:, h * HALF // 16 : (h + 1) * HALF // 16]
+        def half_list(half):
+            columns = HALF_SLOTS // LIST_COLUMN
+            return offsets[:, half * columns : (half + 1) * columns]
 
-        bias = keep.tile([P, E + 1], F32, name="bias")
+        bias = sbuf.tile([P, E + 1], F32, name="bias")
         nc.sync.dma_start(bias[:], b)
 
-        plane = keep.tile([P, T], U8, name="plane", align_bytes=64)
-        nc.vector.memset(plane[:].bitcast(I32), 0)
-        rows = x_scales[0].rearrange("(q r) t -> r q t", r=4)
-        for r in range(4):
-            nc.sync.dma_start(plane[r:P:32, :].bitcast(I32), rows[r].bitcast(I32))
+        token_scales = sbuf.tile([P, T], U8, name="token_scales", align_bytes=ALIGN)
+        nc.vector.memset(token_scales[:].bitcast(I32), 0)
+        scale_rows = x_scales[0].rearrange("(q r) t -> r q t", r=SCALE_ROWS)
+        for r in range(SCALE_ROWS):
+            nc.sync.dma_start(token_scales[r:P:QUADRANT, :].bitcast(I32), scale_rows[r].bitcast(I32))
 
-        warm = keep.tile([P, 2], F32, name="warm")
-        nc.vector.memset(warm[:, 0:1], 0.0)
-        nc.scalar.activation(warm[:, 1:2], warm[:, 0:1], SILU)
-
+        warm_up = sbuf.tile([P, 2], F32, name="warm_up")
+        nc.vector.memset(warm_up[:, 0:1], 0.0)
+        nc.scalar.activation(warm_up[:, 1:2], warm_up[:, 0:1], SILU)
 
         def load_w(first, count, tag):
-            raw = keep.tile([P, count, PACK, N], F32, name="raw%d" % first, tag=tag, align_bytes=64)
+            raw = sbuf.tile([P, count, PACK, N], F32, name="w_raw%d" % first, tag=tag, align_bytes=ALIGN)
             nc.sync.dma_start(raw[:], w[first : first + count].rearrange("e (p j) n -> p e j n", j=PACK))
             return [raw[:, e] for e in range(count)]
 
         def round_w(raws, tag):
-            grouped = keep.tile([P, len(raws), N, PACK], BF16, name="grouped_" + tag, tag=tag, align_bytes=64)
+            rounded = sbuf.tile([P, len(raws), N, PACK], BF16, name=tag, tag=tag, align_bytes=ALIGN)
             for e, raw in enumerate(raws):
                 nc.scalar.copy(
-                    grouped[:, e].rearrange("p (c i) j -> p c j i", i=4),
-                    raw.rearrange("p j (c i) -> p c j i", i=4),
+                    rounded[:, e].rearrange("p (c i) j -> p c j i", i=RUN),
+                    raw.rearrange("p j (c i) -> p c j i", i=RUN),
                 )
-            return grouped
+            return rounded
 
-        def quantize_w(grouped, first, count, tag):
-            codes = keep.tile([P, count * N], U32, name="codes_" + tag, tag=tag, align_bytes=64)
-            scales = keep.tile([P, count * N], U8, name="scales_" + tag, align_bytes=64)
+        def quantize_w(rounded, count, name, tag):
+            codes = sbuf.tile([P, count * N], U32, name="w_words_" + name, tag=tag, align_bytes=ALIGN)
+            scales = sbuf.tile([P, count * N], U8, name="w_scales_" + name, align_bytes=ALIGN)
             nc.vector.quantize_mx(
-                out=codes[:].bitcast(FP8X4), scales=scales[:], in_=grouped[:, first : first + count].rearrange("p e n j -> p (e n j)")
+                out=codes[:].bitcast(FP8X4), scales=scales[:], in_=rounded[:].rearrange("p e n j -> p (e n j)")
             )
             return codes, scales
 
-        def gather_bytes(h):
-            got = keep.tile([P, HALF], U8, name="slot_bytes%d" % h, align_bytes=64)
-            nc.vector.tensor_copy(got[:], plane[:].indirect(half_list(h)))
-            return got
+        def gather_scales(half):
+            slot_scales = sbuf.tile([P, HALF_SLOTS], U8, name="slot_scales%d" % half, align_bytes=ALIGN)
+            nc.vector.tensor_copy(slot_scales[:], token_scales[:].indirect(half_list(half)))
+            return slot_scales
 
-        def gather_words(h, tag):
-            got = keep.tile([P, HALF], U32, name="slot_words%d" % h, tag=tag, align_bytes=64)
-            nc.vector.tensor_copy(got[:], words[:].bitcast(U32).indirect(half_list(h)))
-            return got
+        def gather_words(half, tag):
+            slot_words = sbuf.tile([P, HALF_SLOTS], U32, name="slot_words%d" % half, tag=tag, align_bytes=ALIGN)
+            nc.vector.tensor_copy(slot_words[:], token_words[:].bitcast(U32).indirect(half_list(half)))
+            return slot_words
 
-        def routed(h, codes, scales, slot_words, slot_bytes, tag):
-            y = keep.tile([P, HALF], F32, name="y%d" % h, tag=tag, align_bytes=64)
-            for pair in range(EH // 2):
-                acc = psum.tile([P, BANK], F32, name="acc%d_%d" % (h, pair))
-                for i in range(2):
-                    e = 2 * pair + i
+        def routed(half, w_words, w_scales, slot_words, slot_scales, tag):
+            y = sbuf.tile([P, HALF_SLOTS], F32, name="y%d" % half, tag=tag, align_bytes=ALIGN)
+            for pair in range(HALF_EXPERTS // PAIR):
+                acc = psum.tile([P, BANK], F32, name="routed_sums%d_%d" % (half, pair))
+                for i in range(PAIR):
+                    e = PAIR * pair + i
                     nc.tensor.matmul_mx(
                         out=acc[:, i * C : (i + 1) * C],
-                        lhsT=codes[:, e * N : (e + 1) * N].bitcast(FP8X4),
-                        lhsT_scale=scales[:, e * N : (e + 1) * N],
+                        lhsT=w_words[:, e * N : (e + 1) * N].bitcast(FP8X4),
+                        lhsT_scale=w_scales[:, e * N : (e + 1) * N],
                         rhs=slot_words[:, e * C : (e + 1) * C].bitcast(FP8X4),
-                        rhs_scale=slot_bytes[:, e * C : (e + 1) * C],
+                        rhs_scale=slot_scales[:, e * C : (e + 1) * C],
                         start=True,
                         stop=True,
                     )
-                for i in range(2):
-                    e = 2 * pair + i
-                    col = h * EH + e
+                for i in range(PAIR):
+                    e = PAIR * pair + i
+                    column = half * HALF_EXPERTS + e
                     nc.scalar.activation(
-                        y[:, e * C : (e + 1) * C], acc[:, i * C : (i + 1) * C], SILU, bias=bias[:, col : col + 1]
+                        y[:, e * C : (e + 1) * C],
+                        acc[:, i * C : (i + 1) * C],
+                        SILU,
+                        bias=bias[:, column : column + 1],
                     )
             return y
 
-        def load_gate(h, tag):
-            g = keep.tile([P, HALF], F32, name="gate%d" % h, tag=tag, align_bytes=64)
-            nc.sync.dma_start(g[:], gate[:, h * HALF : (h + 1) * HALF])
-            return g
+        def load_gate(half, tag):
+            gate_half = sbuf.tile([P, HALF_SLOTS], F32, name="gate%d" % half, tag=tag, align_bytes=ALIGN)
+            nc.sync.dma_start(gate_half[:], gate[:, half * HALF_SLOTS : (half + 1) * HALF_SLOTS])
+            return gate_half
 
-        raw_a = load_w(0, EH, "raw_a")
-        words = keep.tile([P, T], I32, name="words", align_bytes=64)
-        nc.sync.dma_start(words[:], x_words[0].rearrange("p t r -> p (t r)").bitcast(I32))
-        raw_b = load_w(EH, 2, "raw_b1") + load_w(EH + 2, 2, "raw_b2")
+        raw0 = load_w(0, PAIR, "raw_e0") + load_w(PAIR, PAIR, "raw_e2")
+        token_words = sbuf.tile([P, T], I32, name="token_words", align_bytes=ALIGN)
+        nc.sync.dma_start(token_words[:], x_words[0].rearrange("p t r -> p (t r)").bitcast(I32))
+        raw1 = load_w(HALF_EXPERTS, PAIR, "raw_e4") + load_w(HALF_EXPERTS + PAIR, PAIR, "raw_e6")
 
-        bytes_a = gather_bytes(0)
-        bytes_b = gather_bytes(1)
-        grouped_a = round_w(raw_a, "grouped_a")
-        codes_a, scales_a = quantize_w(grouped_a, 0, EH, "codes_a")
-        gate_a = load_gate(0, "raw_a")
-        words_a = gather_words(0, "words_a")
-        words_b = gather_words(1, "grouped_a")
-        grouped_b = round_w(raw_b, "grouped_b")
-        y_a = routed(0, codes_a, scales_a, words_a, bytes_a, "raw_b2")
-        codes_b, scales_b = quantize_w(grouped_b, 0, EH, "codes_b")
-        gate_b = load_gate(1, "codes_a")
-        raw_s = load_w(E, 1, "raw_b1")
+        slot_scales0 = gather_scales(0)
+        slot_scales1 = gather_scales(1)
+        rounded0 = round_w(raw0, "rounded0")
+        w_words0, w_scales0 = quantize_w(rounded0, HALF_EXPERTS, "0", "w_words0")
+        gate0 = load_gate(0, "raw_e2")
+        slot_words0 = gather_words(0, "slot_words0")
+        slot_words1 = gather_words(1, "rounded0")
+        rounded1 = round_w(raw1, "rounded1")
+        y0 = routed(0, w_words0, w_scales0, slot_words0, slot_scales0, "raw_e6")
+        w_words1, w_scales1 = quantize_w(rounded1, HALF_EXPERTS, "1", "w_words1")
+        gate1 = load_gate(1, "w_words0")
+        raw_shared = load_w(E, 1, "raw_e4")
 
-        window = keep.tile([P, T], F32, name="window", align_bytes=64)
-        nc.vector.tensor_tensor(window[:].indirect(half_list(0)), y_a[:], gate_a[:], MULT)
+        routed_out = sbuf.tile([P, T], F32, name="routed_out", align_bytes=ALIGN)
+        nc.vector.tensor_tensor(routed_out[:].indirect(half_list(0)), y0[:], gate0[:], MULT)
 
-        grouped_s = round_w(raw_s, "grouped_s")
-        codes_s, scales_s = quantize_w(grouped_s, 0, 1, "raw_a")
-        y_b = routed(1, codes_b, scales_b, words_b, bytes_b, "raw_b1")
-        nc.vector.tensor_tensor(window[:].indirect(half_list(1)), y_b[:], gate_b[:], MULT)
+        rounded_shared = round_w(raw_shared, "rounded_shared")
+        w_words_shared, w_scales_shared = quantize_w(rounded_shared, 1, "shared", "raw_e2")
+        y1 = routed(1, w_words1, w_scales1, slot_words1, slot_scales1, "raw_e4")
+        nc.vector.tensor_tensor(routed_out[:].indirect(half_list(1)), y1[:], gate1[:], MULT)
 
-        total = keep.tile([P, T], F32, name="total", align_bytes=64)
+        total = sbuf.tile([P, T], F32, name="total", align_bytes=ALIGN)
         for c in range(T // BANK):
             cols = slice(c * BANK, (c + 1) * BANK)
-            acc = psum.tile([P, BANK], F32, name="acc_s%d" % c)
+            acc = psum.tile([P, BANK], F32, name="shared_sums%d" % c)
             nc.tensor.matmul_mx(
                 out=acc[:],
-                lhsT=codes_s[:].bitcast(FP8X4),
-                lhsT_scale=scales_s[:],
-                rhs=words[:, cols].bitcast(FP8X4),
-                rhs_scale=plane[:, cols],
+                lhsT=w_words_shared[:].bitcast(FP8X4),
+                lhsT_scale=w_scales_shared[:],
+                rhs=token_words[:, cols].bitcast(FP8X4),
+                rhs_scale=token_scales[:, cols],
                 start=True,
                 stop=True,
             )
             nc.scalar.activation(total[:, cols], acc[:], SILU, bias=bias[:, E : E + 1])
 
-        start = 0
+        first = 0
         for width in STORE_WIDTHS:
-            cols = slice(start, start + width)
-            nc.vector.tensor_tensor(total[:, cols], total[:, cols], window[:, cols], ADD)
+            cols = slice(first, first + width)
+            nc.vector.tensor_tensor(total[:, cols], total[:, cols], routed_out[:, cols], ADD)
             nc.sync.dma_start(out[:, cols], total[:, cols])
-            start = start + width
+            first = first + width

@@ -19,6 +19,7 @@ ADD = mybir.AluOpType.add
 P = 128
 QUADRANT = 32
 SCALE_ROWS = 4
+SPREAD = 8
 PACK = 4
 RUN = 4
 LIST_COLUMN = 16
@@ -47,11 +48,17 @@ def tile_moe_shr_lin_silu_kernel(tc, x_words, x_scales, w, b, gate, offs, out):
         bias = sbuf.tile([P, E + 1], F32, name="bias")
         nc.sync.dma_start(bias[:], b)
 
-        token_scales = sbuf.tile([P, T], U8, name="token_scales", align_bytes=ALIGN)
-        nc.vector.memset(token_scales[:].bitcast(I32), 0)
-        scale_rows = x_scales[0].rearrange("(q r) t -> r q t", r=SCALE_ROWS)
-        for r in range(SCALE_ROWS):
-            nc.sync.dma_start(token_scales[r:P:QUADRANT, :].bitcast(I32), scale_rows[r].bitcast(I32))
+        spread_scales = sbuf.tile([P, T], U8, name="spread_scales", align_bytes=ALIGN)
+        nc.vector.memset(spread_scales[:].bitcast(I32), 0)
+        nc.sync.dma_start(spread_scales[0:P:SPREAD, :].bitcast(I32), x_scales[0].bitcast(I32))
+
+        def to_scale_tile(spread, name):
+            scales = sbuf.tile([P, spread.shape[1]], U8, name=name, align_bytes=ALIGN)
+            for r in range(SCALE_ROWS):
+                nc.sync.dma_start(
+                    scales[r:P:QUADRANT, :].bitcast(I32), spread[SPREAD * r : P : QUADRANT, :].bitcast(I32)
+                )
+            return scales
 
         warm_up = sbuf.tile([P, 2], F32, name="warm_up")
         nc.vector.memset(warm_up[:, 0:1], 0.0)
@@ -80,9 +87,9 @@ def tile_moe_shr_lin_silu_kernel(tc, x_words, x_scales, w, b, gate, offs, out):
             return codes, scales
 
         def gather_scales(half):
-            slot_scales = sbuf.tile([P, HALF_SLOTS], U8, name="slot_scales%d" % half, align_bytes=ALIGN)
-            nc.vector.tensor_copy(slot_scales[:], token_scales[:].indirect(half_list(half)))
-            return slot_scales
+            picked = sbuf.tile([P, HALF_SLOTS], U8, name="picked_scales%d" % half, align_bytes=ALIGN)
+            nc.vector.tensor_copy(picked[:], spread_scales[:].indirect(half_list(half)))
+            return to_scale_tile(picked[:], "slot_scales%d" % half)
 
         def gather_words(half, tag):
             slot_words = sbuf.tile([P, HALF_SLOTS], U32, name="slot_words%d" % half, tag=tag, align_bytes=ALIGN)
@@ -137,6 +144,7 @@ def tile_moe_shr_lin_silu_kernel(tc, x_words, x_scales, w, b, gate, offs, out):
         w_words1, w_scales1 = quantize_w(rounded1, HALF_EXPERTS, "1", "w_words1")
         gate1 = load_gate(1, "w_words0")
         raw_shared = load_w(E, 1, "raw_e4")
+        token_scales = to_scale_tile(spread_scales[:], "token_scales")
 
         routed_out = sbuf.tile([P, T], F32, name="routed_out", align_bytes=ALIGN)
         nc.vector.tensor_tensor(routed_out[:].indirect(half_list(0)), y0[:], gate0[:], MULT)

@@ -19,7 +19,7 @@ ADD = mybir.AluOpType.add
 P = 128
 QUADRANT = 32
 SCALE_ROWS = 4
-SPREAD = 8
+FIRST_ROW = 112
 PACK = 4
 RUN = 4
 LIST_COLUMN = 16
@@ -38,6 +38,10 @@ def tile_moe_shr_lin_silu_kernel(tc, x_words, x_scales, w, b, gate, offs, out):
         sbuf = ctx.enter_context(tc.tile_pool(name="sbuf", bufs=1))
         psum = ctx.enter_context(tc.psum_pool(name="psum", bufs=1))
 
+        spread_scales = sbuf.tile([P, T], U8, name="spread_scales", align_bytes=ALIGN)
+        nc.sync.dma_start(spread_scales[FIRST_ROW:P, :].bitcast(I32), x_scales[0].bitcast(I32))
+        nc.vector.memset(spread_scales[0:FIRST_ROW, :].bitcast(I32), 0)
+
         offsets = sbuf.tile([P, E * C // LIST_COLUMN], U16, name="offsets")
         nc.sync.dma_start(offsets[:], offs)
 
@@ -45,18 +49,12 @@ def tile_moe_shr_lin_silu_kernel(tc, x_words, x_scales, w, b, gate, offs, out):
             columns = HALF_SLOTS // LIST_COLUMN
             return offsets[:, half * columns : (half + 1) * columns]
 
-        bias = sbuf.tile([P, E + 1], F32, name="bias")
-        nc.sync.dma_start(bias[:], b)
-
-        spread_scales = sbuf.tile([P, T], U8, name="spread_scales", align_bytes=ALIGN)
-        nc.vector.memset(spread_scales[:].bitcast(I32), 0)
-        nc.sync.dma_start(spread_scales[0:P:SPREAD, :].bitcast(I32), x_scales[0].bitcast(I32))
 
         def to_scale_tile(spread, name):
             scales = sbuf.tile([P, spread.shape[1]], U8, name=name, align_bytes=ALIGN)
             for r in range(SCALE_ROWS):
                 nc.sync.dma_start(
-                    scales[r:P:QUADRANT, :].bitcast(I32), spread[SPREAD * r : P : QUADRANT, :].bitcast(I32)
+                    scales[r:P:QUADRANT, :].bitcast(I32), spread[FIRST_ROW + r : P : SCALE_ROWS, :].bitcast(I32)
                 )
             return scales
 
@@ -127,17 +125,20 @@ def tile_moe_shr_lin_silu_kernel(tc, x_words, x_scales, w, b, gate, offs, out):
             nc.sync.dma_start(gate_half[:], gate[:, half * HALF_SLOTS : (half + 1) * HALF_SLOTS])
             return gate_half
 
-        raw0 = load_w(0, PAIR, "raw_e0") + load_w(PAIR, PAIR, "raw_e2")
         token_words = sbuf.tile([P, T], I32, name="token_words", align_bytes=ALIGN)
         nc.sync.dma_start(token_words[:], x_words[0].rearrange("p t r -> p (t r)").bitcast(I32))
+        raw0 = load_w(0, PAIR, "raw_e0") + load_w(PAIR, PAIR, "raw_e2")
         raw1 = load_w(HALF_EXPERTS, PAIR, "raw_e4") + load_w(HALF_EXPERTS + PAIR, PAIR, "raw_e6")
+
+        bias = sbuf.tile([P, E + 1], F32, name="bias")
+        nc.sync.dma_start(bias[:], b)
 
         slot_scales0 = gather_scales(0)
         slot_scales1 = gather_scales(1)
+        slot_words0 = gather_words(0, "slot_words0")
         rounded0 = round_w(raw0, "rounded0")
         w_words0, w_scales0 = quantize_w(rounded0, HALF_EXPERTS, "0", "w_words0")
         gate0 = load_gate(0, "raw_e2")
-        slot_words0 = gather_words(0, "slot_words0")
         slot_words1 = gather_words(1, "rounded0")
         rounded1 = round_w(raw1, "rounded1")
         y0 = routed(0, w_words0, w_scales0, slot_words0, slot_scales0, "raw_e6")

@@ -45,13 +45,16 @@ def tile_moe_shr_lin_silu_kernel(tc, x_words, x_scales, w, b, gate, offs, out):
         offsets = sbuf.tile([P, E * C // LIST_COLUMN], U16, name="offsets")
         nc.sync.dma_start(offsets[:], offs)
 
+        def slot_list(first, count):
+            return offsets[:, first // LIST_COLUMN : (first + count) // LIST_COLUMN]
+
         def half_list(half):
             columns = HALF_SLOTS // LIST_COLUMN
             return offsets[:, half * columns : (half + 1) * columns]
 
 
-        def to_scale_tile(spread, name):
-            scales = sbuf.tile([P, spread.shape[1]], U8, name=name, align_bytes=ALIGN)
+        def to_scale_tile(spread, name, tag):
+            scales = sbuf.tile([P, spread.shape[1]], U8, name=name, tag=tag, align_bytes=ALIGN)
             for r in range(SCALE_ROWS):
                 nc.sync.dma_start(
                     scales[r:P:QUADRANT, :].bitcast(I32), spread[FIRST_ROW + r : P : SCALE_ROWS, :].bitcast(I32)
@@ -67,8 +70,8 @@ def tile_moe_shr_lin_silu_kernel(tc, x_words, x_scales, w, b, gate, offs, out):
             nc.sync.dma_start(raw[:], w[first : first + count].rearrange("e (p j) n -> p e j n", j=PACK))
             return [raw[:, e] for e in range(count)]
 
-        def round_w(raws, tag):
-            rounded = sbuf.tile([P, len(raws), N, PACK], BF16, name=tag, tag=tag, align_bytes=ALIGN)
+        def round_w(raws, name, tag):
+            rounded = sbuf.tile([P, len(raws), N, PACK], BF16, name=name, tag=tag, align_bytes=ALIGN)
             for e, raw in enumerate(raws):
                 nc.scalar.copy(
                     rounded[:, e].rearrange("p (c i) j -> p c j i", i=RUN),
@@ -85,19 +88,18 @@ def tile_moe_shr_lin_silu_kernel(tc, x_words, x_scales, w, b, gate, offs, out):
             return codes, scales
 
         def gather_scales(half):
-            picked = sbuf.tile([P, HALF_SLOTS], U8, name="picked_scales%d" % half, align_bytes=ALIGN)
+            picked = sbuf.tile([P, HALF_SLOTS], U8, name="picked_scales%d" % half, tag="picked%d" % half, align_bytes=ALIGN)
             nc.vector.tensor_copy(picked[:], spread_scales[:].indirect(half_list(half)))
-            return to_scale_tile(picked[:], "slot_scales%d" % half)
+            return to_scale_tile(picked[:], "slot_scales%d" % half, "slot_scales%d" % half)
 
         def gather_words(half, tag):
             slot_words = sbuf.tile([P, HALF_SLOTS], U32, name="slot_words%d" % half, tag=tag, align_bytes=ALIGN)
             nc.vector.tensor_copy(slot_words[:], token_words[:].bitcast(U32).indirect(half_list(half)))
             return slot_words
 
-        def routed(half, w_words, w_scales, slot_words, slot_scales, tag):
-            y = sbuf.tile([P, HALF_SLOTS], F32, name="y%d" % half, tag=tag, align_bytes=ALIGN)
-            for pair in range(HALF_EXPERTS // PAIR):
-                acc = psum.tile([P, BANK], F32, name="routed_sums%d_%d" % (half, pair))
+        def routed(first, count, w_words, w_scales, slot_words, slot_scales, y):
+            for pair in range(count // PAIR):
+                acc = psum.tile([P, BANK], F32, name="routed_sums%d" % (first + PAIR * pair))
                 for i in range(PAIR):
                     e = PAIR * pair + i
                     nc.tensor.matmul_mx(
@@ -111,49 +113,53 @@ def tile_moe_shr_lin_silu_kernel(tc, x_words, x_scales, w, b, gate, offs, out):
                     )
                 for i in range(PAIR):
                     e = PAIR * pair + i
-                    column = half * HALF_EXPERTS + e
                     nc.scalar.activation(
                         y[:, e * C : (e + 1) * C],
                         acc[:, i * C : (i + 1) * C],
                         SILU,
-                        bias=bias[:, column : column + 1],
+                        bias=bias[:, first + e : first + e + 1],
                     )
-            return y
 
-        def load_gate(half, tag):
-            gate_half = sbuf.tile([P, HALF_SLOTS], F32, name="gate%d" % half, tag=tag, align_bytes=ALIGN)
-            nc.sync.dma_start(gate_half[:], gate[:, half * HALF_SLOTS : (half + 1) * HALF_SLOTS])
-            return gate_half
+        def load_gate(first, count, tag):
+            gate_part = sbuf.tile([P, count * C], F32, name="gate%d" % first, tag=tag, align_bytes=ALIGN)
+            nc.sync.dma_start(gate_part[:], gate[:, first * C : (first + count) * C])
+            return gate_part
 
+        def scatter(first, count, y, gate_part):
+            nc.vector.tensor_tensor(routed_out[:].indirect(slot_list(first * C, count * C)), y[:], gate_part[:], MULT)
+
+        raw01 = load_w(0, PAIR, "raw01")
         token_words = sbuf.tile([P, T], I32, name="token_words", align_bytes=ALIGN)
         nc.sync.dma_start(token_words[:], x_words[0].rearrange("p t r -> p (t r)").bitcast(I32))
-        raw0 = load_w(0, PAIR, "raw_e0") + load_w(PAIR, PAIR, "raw_e2")
-        raw1 = load_w(HALF_EXPERTS, PAIR, "raw_e4") + load_w(HALF_EXPERTS + PAIR, PAIR, "raw_e6")
-
+        raw23 = load_w(2, PAIR, "raw23")
+        raw45 = load_w(4, PAIR, "raw45")
+        raw67 = load_w(6, PAIR, "raw67")
         bias = sbuf.tile([P, E + 1], F32, name="bias")
         nc.sync.dma_start(bias[:], b)
 
         slot_scales0 = gather_scales(0)
         slot_scales1 = gather_scales(1)
         slot_words0 = gather_words(0, "slot_words0")
-        rounded0 = round_w(raw0, "rounded0")
+        rounded0 = round_w(raw01 + raw23, "rounded0", "rounded0")
         w_words0, w_scales0 = quantize_w(rounded0, HALF_EXPERTS, "0", "w_words0")
-        gate0 = load_gate(0, "raw_e2")
+        gate_first = load_gate(0, PAIR, "raw01")
         slot_words1 = gather_words(1, "rounded0")
-        rounded1 = round_w(raw1, "rounded1")
-        y0 = routed(0, w_words0, w_scales0, slot_words0, slot_scales0, "raw_e6")
+        rounded1 = round_w(raw45 + raw67, "rounded1", "rounded1")
         w_words1, w_scales1 = quantize_w(rounded1, HALF_EXPERTS, "1", "w_words1")
-        gate1 = load_gate(1, "w_words0")
-        raw_shared = load_w(E, 1, "raw_e4")
-        token_scales = to_scale_tile(spread_scales[:], "token_scales")
+        y_first = sbuf.tile([P, PAIR * C], F32, name="y_first", tag="raw67", align_bytes=ALIGN)
+        routed(0, PAIR, w_words0, w_scales0, slot_words0, slot_scales0, y_first)
+        raw_shared = load_w(E, 1, "raw45")
+        gate_rest = load_gate(PAIR, E - PAIR, "raw23")
+        routed_out = sbuf.tile([P, 2 * T], F32, name="routed_out", align_bytes=ALIGN)
+        scatter(0, PAIR, y_first, gate_first)
 
-        routed_out = sbuf.tile([P, T], F32, name="routed_out", align_bytes=ALIGN)
-        nc.vector.tensor_tensor(routed_out[:].indirect(half_list(0)), y0[:], gate0[:], MULT)
-
-        rounded_shared = round_w(raw_shared, "rounded_shared")
-        w_words_shared, w_scales_shared = quantize_w(rounded_shared, 1, "shared", "raw_e2")
-        y1 = routed(1, w_words1, w_scales1, slot_words1, slot_scales1, "raw_e4")
-        nc.vector.tensor_tensor(routed_out[:].indirect(half_list(1)), y1[:], gate1[:], MULT)
+        token_scales = to_scale_tile(spread_scales[:], "token_scales", "rounded1")
+        rounded_shared = round_w(raw_shared, "rounded_shared", "rounded_shared")
+        w_words_shared, w_scales_shared = quantize_w(rounded_shared, 1, "shared", "raw01")
+        y_rest = sbuf.tile([P, (E - PAIR) * C], F32, name="y_rest", tag="raw45", align_bytes=ALIGN)
+        routed(PAIR, PAIR, w_words0[:, PAIR * N :], w_scales0[:, PAIR * N :], slot_words0[:, BANK:], slot_scales0[:, BANK:], y_rest)
+        routed(HALF_EXPERTS, HALF_EXPERTS, w_words1, w_scales1, slot_words1, slot_scales1, y_rest[:, BANK:])
+        scatter(PAIR, E - PAIR, y_rest, gate_rest)
 
         total = sbuf.tile([P, T], F32, name="total", align_bytes=ALIGN)
         for c in range(T // BANK):

@@ -36,6 +36,7 @@ def tile_moe_shr_lin_silu_kernel(tc, x_words, x_scales, w, b, gate, offs, out):
     nc = tc.nc
     with ExitStack() as ctx:
         sbuf = ctx.enter_context(tc.tile_pool(name="sbuf", bufs=1))
+        reused = ctx.enter_context(tc.tile_pool(name="reused", bufs=1))
         psum = ctx.enter_context(tc.psum_pool(name="psum", bufs=1))
 
         spread_scales = sbuf.tile([P, T], U8, name="spread_scales", align_bytes=ALIGN)
@@ -53,8 +54,7 @@ def tile_moe_shr_lin_silu_kernel(tc, x_words, x_scales, w, b, gate, offs, out):
             return offsets[:, half * columns : (half + 1) * columns]
 
 
-        def to_scale_tile(spread, name, tag):
-            scales = sbuf.tile([P, spread.shape[1]], U8, name=name, tag=tag, align_bytes=ALIGN)
+        def to_scale_tile(spread, scales):
             for r in range(SCALE_ROWS):
                 nc.sync.dma_start(
                     scales[r:P:QUADRANT, :].bitcast(I32), spread[FIRST_ROW + r : P : SCALE_ROWS, :].bitcast(I32)
@@ -65,120 +65,166 @@ def tile_moe_shr_lin_silu_kernel(tc, x_words, x_scales, w, b, gate, offs, out):
         nc.vector.memset(warm_up[:, 0:1], 0.0)
         nc.scalar.activation(warm_up[:, 1:2], warm_up[:, 0:1], SILU)
 
-        def load_w(first, count, tag):
-            raw = sbuf.tile([P, count, PACK, N], F32, name="w_raw%d" % first, tag=tag, align_bytes=ALIGN)
+        def placed(name, shape, dtype, at):
+            if at is None:
+                return sbuf.tile(shape, dtype, name=name, align_bytes=ALIGN)
+            return reused.tile(shape, dtype, name=name, offset=at, align_bytes=ALIGN)
+
+        def load_w(first, count, at):
+            raw = placed("w_raw%d" % first, [P, count, PACK, N], F32, at)
             nc.sync.dma_start(raw[:], w[first : first + count].rearrange("e (p j) n -> p e j n", j=PACK))
             return [raw[:, e] for e in range(count)]
 
-        def round_w(raws, name, tag):
-            rounded = sbuf.tile([P, len(raws), N, PACK], BF16, name=name, tag=tag, align_bytes=ALIGN)
-            for e, raw in enumerate(raws):
-                nc.scalar.copy(
-                    rounded[:, e].rearrange("p (c i) j -> p c j i", i=RUN),
-                    raw.rearrange("p j (c i) -> p c j i", i=RUN),
-                )
-            return rounded
+        def round_into(rounded, i, raw):
+            nc.scalar.copy(
+                rounded[:, i].rearrange("p (c i) j -> p c j i", i=RUN),
+                raw.rearrange("p j (c i) -> p c j i", i=RUN),
+            )
 
-        def quantize_w(rounded, count, name, tag):
-            codes = sbuf.tile([P, count * N], U32, name="w_words_" + name, tag=tag, align_bytes=ALIGN)
-            scales = sbuf.tile([P, count * N], U8, name="w_scales_" + name, align_bytes=ALIGN)
+        def quantize_w(rounded, count, name, at):
+            codes = placed("w_words_" + name, [P, count * N], U32, at)
+            scales = placed("w_scales_" + name, [P, count * N], U8, None)
             nc.vector.quantize_mx(
                 out=codes[:].bitcast(FP8X4), scales=scales[:], in_=rounded[:].rearrange("p e n j -> p (e n j)")
             )
-            return codes, scales
+            return [(codes[:, i * N : (i + 1) * N], scales[:, i * N : (i + 1) * N]) for i in range(count)]
 
-        def gather_scales(half):
-            picked = sbuf.tile([P, HALF_SLOTS], U8, name="picked_scales%d" % half, tag="picked%d" % half, align_bytes=ALIGN)
+        def gather_scales(half, at):
+            picked = placed("picked_scales%d" % half, [P, HALF_SLOTS], U8, at)
             nc.vector.tensor_copy(picked[:], spread_scales[:].indirect(half_list(half)))
-            return to_scale_tile(picked[:], "slot_scales%d" % half, "slot_scales%d" % half)
+            return picked
 
-        def gather_words(half, tag):
-            slot_words = sbuf.tile([P, HALF_SLOTS], U32, name="slot_words%d" % half, tag=tag, align_bytes=ALIGN)
-            nc.vector.tensor_copy(slot_words[:], token_words[:].bitcast(U32).indirect(half_list(half)))
-            return slot_words
-
-        def routed(first, count, w_words, w_scales, slot_words, slot_scales, y):
-            for pair in range(count // PAIR):
-                acc = psum.tile([P, BANK], F32, name="routed_sums%d" % (first + PAIR * pair))
-                for i in range(PAIR):
-                    e = PAIR * pair + i
-                    nc.tensor.matmul_mx(
-                        out=acc[:, i * C : (i + 1) * C],
-                        lhsT=w_words[:, e * N : (e + 1) * N].bitcast(FP8X4),
-                        lhsT_scale=w_scales[:, e * N : (e + 1) * N],
-                        rhs=slot_words[:, e * C : (e + 1) * C].bitcast(FP8X4),
-                        rhs_scale=slot_scales[:, e * C : (e + 1) * C],
-                        start=True,
-                        stop=True,
-                    )
-                for i in range(PAIR):
-                    e = PAIR * pair + i
-                    nc.scalar.activation(
-                        y[:, e * C : (e + 1) * C],
-                        acc[:, i * C : (i + 1) * C],
-                        SILU,
-                        bias=bias[:, first + e : first + e + 1],
-                    )
-
-        def load_gate(first, count, tag):
-            gate_part = sbuf.tile([P, count * C], F32, name="gate%d" % first, tag=tag, align_bytes=ALIGN)
+        def load_gate(first, count, at):
+            gate_part = placed("gate%d" % first, [P, count * C], F32, at)
             nc.sync.dma_start(gate_part[:], gate[:, first * C : (first + count) * C])
             return gate_part
 
-        def scatter(first, count, y, gate_part):
-            nc.vector.tensor_tensor(routed_out[:].indirect(slot_list(first * C, count * C)), y[:], gate_part[:], MULT)
+        def gather_words(first, count, at):
+            slot_words = placed("slot_words%d" % first, [P, count * C], U32, at)
+            nc.vector.tensor_copy(slot_words[:], token_words[:].bitcast(U32).indirect(slot_list(first * C, count * C)))
+            return slot_words
 
-        raw01 = load_w(0, PAIR, "raw01")
-        token_words = sbuf.tile([P, T], I32, name="token_words", align_bytes=ALIGN)
-        nc.sync.dma_start(token_words[:], x_words[0].rearrange("p t r -> p (t r)").bitcast(I32))
-        raw23 = load_w(2, PAIR, "raw23")
-        raw45 = load_w(4, PAIR, "raw45")
-        raw67 = load_w(6, PAIR, "raw67")
-        bias = sbuf.tile([P, E + 1], F32, name="bias")
-        nc.sync.dma_start(bias[:], b)
-
-        slot_scales0 = gather_scales(0)
-        slot_scales1 = gather_scales(1)
-        slot_words0 = gather_words(0, "slot_words0")
-        rounded0 = round_w(raw01 + raw23, "rounded0", "rounded0")
-        w_words0, w_scales0 = quantize_w(rounded0, HALF_EXPERTS, "0", "w_words0")
-        gate_first = load_gate(0, PAIR, "raw01")
-        slot_words1 = gather_words(1, "rounded0")
-        rounded1 = round_w(raw45 + raw67, "rounded1", "rounded1")
-        w_words1, w_scales1 = quantize_w(rounded1, HALF_EXPERTS, "1", "w_words1")
-        y_first = sbuf.tile([P, PAIR * C], F32, name="y_first", tag="raw67", align_bytes=ALIGN)
-        routed(0, PAIR, w_words0, w_scales0, slot_words0, slot_scales0, y_first)
-        raw_shared = load_w(E, 1, "raw45")
-        gate_rest = load_gate(PAIR, E - PAIR, "raw23")
-        routed_out = sbuf.tile([P, 2 * T], F32, name="routed_out", align_bytes=ALIGN)
-        scatter(0, PAIR, y_first, gate_first)
-
-        token_scales = to_scale_tile(spread_scales[:], "token_scales", "rounded1")
-        rounded_shared = round_w(raw_shared, "rounded_shared", "rounded_shared")
-        w_words_shared, w_scales_shared = quantize_w(rounded_shared, 1, "shared", "raw01")
-        y_rest = sbuf.tile([P, (E - PAIR) * C], F32, name="y_rest", tag="raw45", align_bytes=ALIGN)
-        routed(PAIR, PAIR, w_words0[:, PAIR * N :], w_scales0[:, PAIR * N :], slot_words0[:, BANK:], slot_scales0[:, BANK:], y_rest)
-        routed(HALF_EXPERTS, HALF_EXPERTS, w_words1, w_scales1, slot_words1, slot_scales1, y_rest[:, BANK:])
-        scatter(PAIR, E - PAIR, y_rest, gate_rest)
-
-        total = sbuf.tile([P, T], F32, name="total", align_bytes=ALIGN)
-        for c in range(T // BANK):
-            cols = slice(c * BANK, (c + 1) * BANK)
-            acc = psum.tile([P, BANK], F32, name="shared_sums%d" % c)
+        def sums(acc, stationary, words, slot_scales):
             nc.tensor.matmul_mx(
-                out=acc[:],
-                lhsT=w_words_shared[:].bitcast(FP8X4),
-                lhsT_scale=w_scales_shared[:],
-                rhs=token_words[:, cols].bitcast(FP8X4),
-                rhs_scale=token_scales[:, cols],
+                out=acc,
+                lhsT=stationary[0].bitcast(FP8X4),
+                lhsT_scale=stationary[1],
+                rhs=words.bitcast(FP8X4),
+                rhs_scale=slot_scales,
                 start=True,
                 stop=True,
             )
-            nc.scalar.activation(total[:, cols], acc[:], SILU, bias=bias[:, E : E + 1])
 
-        first = 0
-        for width in STORE_WIDTHS:
-            cols = slice(first, first + width)
-            nc.vector.tensor_tensor(total[:, cols], total[:, cols], routed_out[:, cols], ADD)
+        def silu(result, acc, e):
+            nc.scalar.activation(result, acc, SILU, bias=bias[:, e : e + 1])
+
+        def bank(name, tag):
+            return psum.tile([P, BANK], F32, name=name, tag=tag)
+
+        def product(name, y, gate_part, width, at):
+            gated = placed(name, [P, width], F32, at)
+            nc.gpsimd.tensor_tensor(gated[:], y, gate_part, MULT)
+            return gated
+
+        def add(name, gated, ys, width, at):
+            both = placed(name, [P, width], F32, at)
+            nc.gpsimd.tensor_tensor(both[:], gated[:], ys, ADD)
+            return both
+
+        def scatter_copy(first, count, both):
+            nc.vector.tensor_copy(total[:].indirect(slot_list(first * C, count * C)), both[:])
+
+        left, right = slice(0, C), slice(C, 2 * C)
+        token_words = sbuf.tile([P, T], I32, name="token_words", align_bytes=ALIGN)
+        nc.sync.dma_start(token_words[:], x_words[0].rearrange("p t r -> p (t r)").bitcast(I32))
+        raw7 = load_w(7, 1, 4096)
+        raw8 = load_w(8, 1, 30720)
+        raw56 = load_w(5, 2, 38912)
+        raw4 = load_w(4, 1, 8192)
+        bias = sbuf.tile([P, E + 1], F32, name="bias")
+        nc.sync.dma_start(bias[:], b)
+
+        picked_high = gather_scales(1, None)
+        scales_high = to_scale_tile(picked_high[:], placed("scales_high", [P, HALF_SLOTS], U8, None))
+        words67 = gather_words(6, 2, None)
+        words45 = gather_words(4, 2, None)
+        rounded78 = placed("rounded78", [P, 2, N, PACK], BF16, None)
+        rounded56 = placed("rounded56", [P, 2, N, PACK], BF16, None)
+        rounded4 = placed("rounded4", [P, 1, N, PACK], BF16, None)
+        rounded_low = placed("rounded_low", [P, HALF_EXPERTS, N, PACK], BF16, 73728)
+        round_into(rounded78, 0, raw7[0])
+        gate67 = load_gate(6, 2, 3072)
+        raw3 = load_w(3, 1, 5120)
+        round_into(rounded78, 1, raw8[0])
+        raw_low = load_w(0, 3, 31744) + raw3
+        w7, w_shared = quantize_w(rounded78, 2, "78", None)
+        words01 = gather_words(0, 2, 29696)
+        round_into(rounded56, 0, raw56[0])
+        round_into(rounded56, 1, raw56[1])
+        gate45 = load_gate(4, 2, 37888)
+        gate_low = load_gate(0, HALF_EXPERTS, 40960)
+        w5, w6 = quantize_w(rounded56, 2, "56", None)
+        round_into(rounded4, 0, raw4[0])
+        w4 = quantize_w(rounded4, 1, "4", None)[0]
+        picked_low = gather_scales(0, 8192)
+        scales_low = to_scale_tile(picked_low[:], placed("scales_low", [P, HALF_SLOTS], U8, None))
+        words23 = gather_words(2, 2, 9216)
+
+        total = sbuf.tile([P, T], F32, name="total", align_bytes=ALIGN)
+        y67 = placed("y67", [P, 4, C], F32, None)
+        acc_y7, acc_ys7, acc6 = bank("acc_y7", "bank0"), bank("acc_ys7", "bank1"), bank("acc6", "bank2")
+        sums(acc_y7[:, left], w7, words67[:, right], scales_high[:, 3 * C :])
+        sums(acc_ys7[:, left], w_shared, words67[:, right], scales_high[:, 3 * C :])
+        silu(y67[:, 0], acc_y7[:, left], 7)
+        silu(y67[:, 1], acc_ys7[:, left], E)
+        sums(acc6[:, left], w6, words67[:, left], scales_high[:, 2 * C : 3 * C])
+        sums(acc6[:, right], w_shared, words67[:, left], scales_high[:, 2 * C : 3 * C])
+        silu(y67[:, 2], acc6[:, left], 6)
+        silu(y67[:, 3], acc6[:, right], E)
+        y45 = placed("y45", [P, BANK], F32, None)
+        acc_y45, acc_ys45 = bank("acc_y45", "bank3"), bank("acc_ys45", "bank4")
+        sums(acc_y45[:, right], w5, words45[:, right], scales_high[:, C : 2 * C])
+        sums(acc_y45[:, left], w4, words45[:, left], scales_high[:, :C])
+        sums(acc_ys45[:], w_shared, words45[:], scales_high[:, : 2 * C])
+        silu(y45[:, left], acc_y45[:, left], 4)
+        silu(y45[:, right], acc_y45[:, right], 5)
+        ys45 = placed("ys45", [P, BANK], F32, None)
+        silu(ys45[:], acc_ys45[:], E)
+
+        gated7 = product("gated7", y67[:, 0], gate67[:, right], C, 57344)
+        both7 = add("both7", gated7, y67[:, 1], C, None)
+        scatter_copy(7, 1, both7)
+        both456 = placed("both456", [P, 3 * C], F32, None)
+        gated6 = product("gated6", y67[:, 2], gate67[:, left], C, 57344 + 512)
+        nc.gpsimd.tensor_tensor(both456[:, BANK:], gated6[:], y67[:, 3], ADD)
+        gated45 = product("gated45", y45[:], gate45[:], BANK, 57344 + 1024)
+        for e in range(HALF_EXPERTS):
+            round_into(rounded_low, e, raw_low[e])
+        w_low = quantize_w(rounded_low, HALF_EXPERTS, "low", None)
+        nc.gpsimd.tensor_tensor(both456[:, :BANK], gated45[:], ys45[:], ADD)
+        scatter_copy(4, 3, both456)
+
+        y_both = placed("y_low", [P, 2 * HALF_SLOTS], F32, 65600)
+        y_low = y_both[:, :HALF_SLOTS]
+        ys_low = y_both[:, HALF_SLOTS:]
+        gated_low = placed("gated_low", [P, HALF_SLOTS], F32, None)
+        for pair, words in enumerate((words01, words23)):
+            cols = slice(pair * BANK, (pair + 1) * BANK)
+            acc = bank("acc_y%d" % pair, "bank%d" % (5 + pair))
+            for i, side in enumerate((left, right)):
+                e = PAIR * pair + i
+                sums(acc[:, side], w_low[e], words[:, side], scales_low[:, e * C : (e + 1) * C])
+            for i, side in enumerate((left, right)):
+                e = PAIR * pair + i
+                silu(y_low[:, e * C : (e + 1) * C], acc[:, side], e)
+            nc.gpsimd.tensor_tensor(gated_low[:, cols], y_low[:, cols], gate_low[:, cols], MULT)
+        for pair, words in enumerate((words01, words23)):
+            cols = slice(pair * BANK, (pair + 1) * BANK)
+            acc = bank("acc_ys%d" % pair, ("bank7", "bank0")[pair])
+            sums(acc[:], w_shared, words[:], scales_low[:, cols])
+            silu(ys_low[:, cols], acc[:], E)
+        nc.vector.tensor_tensor(total[:].indirect(slot_list(0, HALF_SLOTS)), gated_low[:], ys_low, ADD)
+
+        for half in range(2):
+            cols = slice(half * T // 2, (half + 1) * T // 2)
             nc.sync.dma_start(out[:, cols], total[:, cols])
-            first = first + width

@@ -138,9 +138,9 @@ def tile_moe_shr_lin_silu_kernel(tc, x_words, x_scales, w, b, gate, offs, out):
         token_words = sbuf.tile([P, T], I32, name="token_words", align_bytes=ALIGN)
         nc.sync.dma_start(token_words[:], x_words[0].rearrange("p t r -> p (t r)").bitcast(I32))
         raw7 = load_w(7, 1, 4096)
-        raw8 = load_w(8, 1, 30720)
+        raw8 = load_w(8, 1, 32768)
         raw56 = load_w(5, 2, 38912)
-        raw4 = load_w(4, 1, 8192)
+        raw4 = load_w(4, 1, 12288)
         bias = sbuf.tile([P, E + 1], F32, name="bias")
         nc.sync.dma_start(bias[:], b)
 
@@ -154,11 +154,11 @@ def tile_moe_shr_lin_silu_kernel(tc, x_words, x_scales, w, b, gate, offs, out):
         rounded_low = placed("rounded_low", [P, HALF_EXPERTS, N, PACK], BF16, 73728)
         round_into(rounded78, 0, raw7[0])
         gate67 = load_gate(6, 2, 3072)
-        raw3 = load_w(3, 1, 5120)
+        raw01 = load_w(0, 2, 5120)
         round_into(rounded78, 1, raw8[0])
-        raw_low = load_w(0, 3, 31744) + raw3
+        raw_low = raw01 + load_w(2, 2, 29696)
         w7, w_shared = quantize_w(rounded78, 2, "78", None)
-        words01 = gather_words(0, 2, 29696)
+        words01 = gather_words(0, 2, 33856)
         round_into(rounded56, 0, raw56[0])
         round_into(rounded56, 1, raw56[1])
         gate45 = load_gate(4, 2, 37888)
@@ -166,43 +166,41 @@ def tile_moe_shr_lin_silu_kernel(tc, x_words, x_scales, w, b, gate, offs, out):
         w5, w6 = quantize_w(rounded56, 2, "56", None)
         round_into(rounded4, 0, raw4[0])
         w4 = quantize_w(rounded4, 1, "4", None)[0]
-        picked_low = gather_scales(0, 8192)
+        picked_low = gather_scales(0, 12288)
         scales_low = to_scale_tile(picked_low[:], placed("scales_low", [P, HALF_SLOTS], U8, None))
-        words23 = gather_words(2, 2, 9216)
+        words23 = gather_words(2, 2, 13312)
 
-        total = sbuf.tile([P, T], F32, name="total", align_bytes=ALIGN)
-        y67 = placed("y67", [P, 4, C], F32, None)
-        acc_y7, acc_ys7, acc6 = bank("acc_y7", "bank0"), bank("acc_ys7", "bank1"), bank("acc6", "bank2")
+        total = placed("total", [P, T], F32, 31744 - 8192 + 64 - 2048)
+        y67 = placed("y67", [P, BANK], F32, None)
+        ys67 = placed("ys67", [P, BANK], F32, None)
+        gated67 = placed("gated67", [P, BANK], F32, None)
+        acc_y7, acc_y6, acc_ys67 = bank("acc_y7", "bank0"), bank("acc_y6", "bank1"), bank("acc_ys67", "bank2")
         sums(acc_y7[:, left], w7, words67[:, right], scales_high[:, 3 * C :])
-        sums(acc_ys7[:, left], w_shared, words67[:, right], scales_high[:, 3 * C :])
-        silu(y67[:, 0], acc_y7[:, left], 7)
-        silu(y67[:, 1], acc_ys7[:, left], E)
-        sums(acc6[:, left], w6, words67[:, left], scales_high[:, 2 * C : 3 * C])
-        sums(acc6[:, right], w_shared, words67[:, left], scales_high[:, 2 * C : 3 * C])
-        silu(y67[:, 2], acc6[:, left], 6)
-        silu(y67[:, 3], acc6[:, right], E)
-        y45 = placed("y45", [P, BANK], F32, None)
+        sums(acc_ys67[:], w_shared, words67[:], scales_high[:, 2 * C :])
+        sums(acc_y6[:, left], w6, words67[:, left], scales_high[:, 2 * C : 3 * C])
+        silu(y67[:, right], acc_y7[:, left], 7)
+        nc.gpsimd.tensor_tensor(gated67[:, right], y67[:, right], gate67[:, right], MULT)
+        silu(y67[:, left], acc_y6[:, left], 6)
+        nc.gpsimd.tensor_tensor(gated67[:, left], y67[:, left], gate67[:, left], MULT)
+        silu(ys67[:], acc_ys67[:], E)
+        for e in range(HALF_EXPERTS):
+            round_into(rounded_low, e, raw_low[e])
+        w_low = quantize_w(rounded_low, HALF_EXPERTS, "low", None)
+        both67 = add("both67", gated67, ys67[:], BANK, None)
+        scatter_copy(6, 2, both67)
+
+        y45 = placed("y45", [P, BANK], F32, 29760)
+        ys45 = placed("ys45", [P, BANK], F32, 31808)
         acc_y45, acc_ys45 = bank("acc_y45", "bank3"), bank("acc_ys45", "bank4")
         sums(acc_y45[:, right], w5, words45[:, right], scales_high[:, C : 2 * C])
         sums(acc_y45[:, left], w4, words45[:, left], scales_high[:, :C])
         sums(acc_ys45[:], w_shared, words45[:], scales_high[:, : 2 * C])
         silu(y45[:, left], acc_y45[:, left], 4)
         silu(y45[:, right], acc_y45[:, right], 5)
-        ys45 = placed("ys45", [P, BANK], F32, None)
         silu(ys45[:], acc_ys45[:], E)
-
-        gated7 = product("gated7", y67[:, 0], gate67[:, right], C, 57344)
-        both7 = add("both7", gated7, y67[:, 1], C, None)
-        scatter_copy(7, 1, both7)
-        both456 = placed("both456", [P, 3 * C], F32, None)
-        gated6 = product("gated6", y67[:, 2], gate67[:, left], C, 57344 + 512)
-        nc.gpsimd.tensor_tensor(both456[:, BANK:], gated6[:], y67[:, 3], ADD)
-        gated45 = product("gated45", y45[:], gate45[:], BANK, 57344 + 1024)
-        for e in range(HALF_EXPERTS):
-            round_into(rounded_low, e, raw_low[e])
-        w_low = quantize_w(rounded_low, HALF_EXPERTS, "low", None)
-        nc.gpsimd.tensor_tensor(both456[:, :BANK], gated45[:], ys45[:], ADD)
-        scatter_copy(4, 3, both456)
+        gated45 = product("gated45", y45[:], gate45[:], BANK, 75776)
+        both45 = add("both45", gated45, ys45[:], BANK, None)
+        scatter_copy(4, 2, both45)
 
         y_both = placed("y_low", [P, 2 * HALF_SLOTS], F32, 65600)
         y_low = y_both[:, :HALF_SLOTS]

@@ -140,23 +140,24 @@ def tile_moe_shr_lin_silu_kernel(tc, x_words, x_scales, w, b, gate, offs, out):
         raw7 = load_w(7, 1, 4096)
         raw8 = load_w(8, 1, 32768)
         raw56 = load_w(5, 2, 38912)
-        raw4 = load_w(4, 1, 12288)
+        raw4 = load_w(4, 1, 73728)
         bias = sbuf.tile([P, E + 1], F32, name="bias")
         nc.sync.dma_start(bias[:], b)
 
         picked_high = gather_scales(1, None)
         scales_high = to_scale_tile(picked_high[:], placed("scales_high", [P, HALF_SLOTS], U8, None))
-        words67 = gather_words(6, 2, None)
-        words45 = gather_words(4, 2, None)
+        words_high = gather_words(4, 4, None)
+        words45, words67 = words_high[:, :BANK], words_high[:, BANK:]
         rounded78 = placed("rounded78", [P, 2, N, PACK], BF16, None)
         rounded56 = placed("rounded56", [P, 2, N, PACK], BF16, None)
         rounded4 = placed("rounded4", [P, 1, N, PACK], BF16, None)
-        rounded_low = placed("rounded_low", [P, HALF_EXPERTS, N, PACK], BF16, 73728)
+        rounded01 = placed("rounded01", [P, 2, N, PACK], BF16, 49152)
+        rounded23 = placed("rounded23", [P, 2, N, PACK], BF16, 57344)
         round_into(rounded78, 0, raw7[0])
         gate67 = load_gate(6, 2, 3072)
         raw01 = load_w(0, 2, 5120)
         round_into(rounded78, 1, raw8[0])
-        raw_low = raw01 + load_w(2, 2, 29696)
+        raw23 = load_w(2, 2, 29696)
         w7, w_shared = quantize_w(rounded78, 2, "78", None)
         words01 = gather_words(0, 2, 33856)
         round_into(rounded56, 0, raw56[0])
@@ -166,46 +167,49 @@ def tile_moe_shr_lin_silu_kernel(tc, x_words, x_scales, w, b, gate, offs, out):
         w5, w6 = quantize_w(rounded56, 2, "56", None)
         round_into(rounded4, 0, raw4[0])
         w4 = quantize_w(rounded4, 1, "4", None)[0]
-        picked_low = gather_scales(0, 12288)
+        picked_low = gather_scales(0, 73728)
         scales_low = to_scale_tile(picked_low[:], placed("scales_low", [P, HALF_SLOTS], U8, None))
-        words23 = gather_words(2, 2, 13312)
+        words23 = gather_words(2, 2, 74752)
 
-        total = placed("total", [P, T], F32, 31744 - 8192 + 64 - 2048)
         y67 = placed("y67", [P, BANK], F32, None)
         ys67 = placed("ys67", [P, BANK], F32, None)
-        gated67 = placed("gated67", [P, BANK], F32, None)
+        gated67 = placed("gated67", [P, BANK], F32, 65536)
         acc_y7, acc_y6, acc_ys67 = bank("acc_y7", "bank0"), bank("acc_y6", "bank1"), bank("acc_ys67", "bank2")
         sums(acc_y7[:, left], w7, words67[:, right], scales_high[:, 3 * C :])
-        sums(acc_ys67[:], w_shared, words67[:], scales_high[:, 2 * C :])
+        sums(acc_ys67[:], w_shared, words67, scales_high[:, 2 * C :])
         sums(acc_y6[:, left], w6, words67[:, left], scales_high[:, 2 * C : 3 * C])
         silu(y67[:, right], acc_y7[:, left], 7)
         nc.gpsimd.tensor_tensor(gated67[:, right], y67[:, right], gate67[:, right], MULT)
         silu(y67[:, left], acc_y6[:, left], 6)
         nc.gpsimd.tensor_tensor(gated67[:, left], y67[:, left], gate67[:, left], MULT)
         silu(ys67[:], acc_ys67[:], E)
-        for e in range(HALF_EXPERTS):
-            round_into(rounded_low, e, raw_low[e])
-        w_low = quantize_w(rounded_low, HALF_EXPERTS, "low", None)
+        round_into(rounded01, 0, raw01[0])
+        round_into(rounded01, 1, raw01[1])
         both67 = add("both67", gated67, ys67[:], BANK, None)
+        w_low = quantize_w(rounded01, 2, "01", 65536)
+        total = placed("total", [P, T], F32, 9152)
         scatter_copy(6, 2, both67)
 
-        y45 = placed("y45", [P, BANK], F32, 29760)
-        ys45 = placed("ys45", [P, BANK], F32, 31808)
+        y45 = placed("y45", [P, BANK], F32, None)
+        ys45 = placed("ys45", [P, BANK], F32, None)
         acc_y45, acc_ys45 = bank("acc_y45", "bank3"), bank("acc_ys45", "bank4")
         sums(acc_y45[:, right], w5, words45[:, right], scales_high[:, C : 2 * C])
         sums(acc_y45[:, left], w4, words45[:, left], scales_high[:, :C])
-        sums(acc_ys45[:], w_shared, words45[:], scales_high[:, : 2 * C])
+        sums(acc_ys45[:], w_shared, words45, scales_high[:, : 2 * C])
         silu(y45[:, left], acc_y45[:, left], 4)
         silu(y45[:, right], acc_y45[:, right], 5)
         silu(ys45[:], acc_ys45[:], E)
-        gated45 = product("gated45", y45[:], gate45[:], BANK, 75776)
-        both45 = add("both45", gated45, ys45[:], BANK, None)
+        round_into(rounded23, 0, raw23[0])
+        round_into(rounded23, 1, raw23[1])
+        gated45 = product("gated45", y45[:], gate45[:], BANK, 49152)
+        both45 = add("both45", gated45, ys45[:], BANK, 31808)
+        w_low = w_low + quantize_w(rounded23, 2, "23", 49152)
         scatter_copy(4, 2, both45)
 
-        y_both = placed("y_low", [P, 2 * HALF_SLOTS], F32, 65600)
+        y_both = placed("y_low", [P, 2 * HALF_SLOTS], F32, 23616)
         y_low = y_both[:, :HALF_SLOTS]
         ys_low = y_both[:, HALF_SLOTS:]
-        gated_low = placed("gated_low", [P, HALF_SLOTS], F32, None)
+        gated_low = placed("gated_low", [P, HALF_SLOTS], F32, 57344)
         for pair, words in enumerate((words01, words23)):
             cols = slice(pair * BANK, (pair + 1) * BANK)
             acc = bank("acc_y%d" % pair, "bank%d" % (5 + pair))

@@ -13,6 +13,7 @@ U16 = mybir.dt.uint16
 U8 = mybir.dt.uint8
 FP8X4 = mybir.dt.float8_e4m3fn_x4
 SILU = mybir.ActivationFunctionType.Silu
+COPY = mybir.ActivationFunctionType.Copy
 MULT = mybir.AluOpType.mult
 ADD = mybir.AluOpType.add
 
@@ -24,9 +25,6 @@ PACK = 4
 RUN = 4
 LIST_COLUMN = 16
 BANK = 512
-PAIR = BANK // C
-HALF_SLOTS = E * C // 2
-HALF_EXPERTS = E // 2
 ALIGN = 64
 STORE_WIDTHS = (256, 384, 384, 384, 384, 256)
 assert sum(STORE_WIDTHS) == T
@@ -39,38 +37,15 @@ def tile_moe_shr_lin_silu_kernel(tc, x_words, x_scales, w, b, gate, offs, out):
         reused = ctx.enter_context(tc.tile_pool(name="reused", bufs=1))
         psum = ctx.enter_context(tc.psum_pool(name="psum", bufs=1))
 
-        spread_scales = sbuf.tile([P, T], U8, name="spread_scales", align_bytes=ALIGN)
-        nc.sync.dma_start(spread_scales[FIRST_ROW:P, :].bitcast(I32), x_scales[0].bitcast(I32))
-        nc.vector.memset(spread_scales[0:FIRST_ROW, :].bitcast(I32), 0)
-
-        offsets = sbuf.tile([P, E * C // LIST_COLUMN], U16, name="offsets")
-        nc.sync.dma_start(offsets[:], offs)
-
-        def slot_list(first, count):
-            return offsets[:, first // LIST_COLUMN : (first + count) // LIST_COLUMN]
-
-        def half_list(half):
-            columns = HALF_SLOTS // LIST_COLUMN
-            return offsets[:, half * columns : (half + 1) * columns]
-
-
-        def to_scale_tile(spread, scales):
-            for r in range(SCALE_ROWS):
-                nc.sync.dma_start(
-                    scales[r:P:QUADRANT, :].bitcast(I32), spread[FIRST_ROW + r : P : SCALE_ROWS, :].bitcast(I32)
-                )
-            return scales
-
-        warm_up = sbuf.tile([P, 2], F32, name="warm_up")
-        nc.vector.memset(warm_up[:, 0:1], 0.0)
-        nc.scalar.activation(warm_up[:, 1:2], warm_up[:, 0:1], SILU)
-
-        def placed(name, shape, dtype, at):
+        def placed(name, shape, dtype, at=None):
             if at is None:
                 return sbuf.tile(shape, dtype, name=name, align_bytes=ALIGN)
             return reused.tile(shape, dtype, name=name, offset=at, align_bytes=ALIGN)
 
-        def load_w(first, count, at):
+        def slot_list(first, count):
+            return offsets[:, first // LIST_COLUMN : (first + count) // LIST_COLUMN]
+
+        def load_w(first, count, at=None):
             raw = placed("w_raw%d" % first, [P, count, PACK, N], F32, at)
             nc.sync.dma_start(raw[:], w[first : first + count].rearrange("e (p j) n -> p e j n", j=PACK))
             return [raw[:, e] for e in range(count)]
@@ -81,36 +56,38 @@ def tile_moe_shr_lin_silu_kernel(tc, x_words, x_scales, w, b, gate, offs, out):
                 raw.rearrange("p j (c i) -> p c j i", i=RUN),
             )
 
-        def quantize_w(rounded, count, name, at):
+        def quantize_w(rounded, count, name, at=None):
             codes = placed("w_words_" + name, [P, count * N], U32, at)
-            scales = placed("w_scales_" + name, [P, count * N], U8, None)
+            scales = placed("w_scales_" + name, [P, count * N], U8)
             nc.vector.quantize_mx(
                 out=codes[:].bitcast(FP8X4), scales=scales[:], in_=rounded[:].rearrange("p e n j -> p (e n j)")
             )
             return [(codes[:, i * N : (i + 1) * N], scales[:, i * N : (i + 1) * N]) for i in range(count)]
 
-        def gather_scales(half, at):
-            picked = placed("picked_scales%d" % half, [P, HALF_SLOTS], U8, at)
-            nc.vector.tensor_copy(picked[:], spread_scales[:].indirect(half_list(half)))
+        def gather_scales(first, count, at=None):
+            picked = placed("picked_scales%d" % first, [P, count * C], U8, at)
+            nc.vector.tensor_copy(picked[:], spread_scales[:].indirect(slot_list(first * C, count * C)))
             return picked
 
-        def load_gate(first, count, at):
-            gate_part = placed("gate%d" % first, [P, count * C], F32, at)
-            nc.sync.dma_start(gate_part[:], gate[:, first * C : (first + count) * C])
-            return gate_part
+        def move_scales(picked, first, count):
+            for r in range(SCALE_ROWS):
+                nc.sync.dma_start(
+                    slot_scales[r:P:QUADRANT, first * C : (first + count) * C].bitcast(I32),
+                    picked[FIRST_ROW + r : P : SCALE_ROWS, :].bitcast(I32),
+                )
 
-        def gather_words(first, count, at):
-            slot_words = placed("slot_words%d" % first, [P, count * C], U32, at)
-            nc.vector.tensor_copy(slot_words[:], token_words[:].bitcast(U32).indirect(slot_list(first * C, count * C)))
-            return slot_words
+        def gather_words(first, count, at=None):
+            words = placed("slot_words%d" % first, [P, count * C], U32, at)
+            nc.vector.tensor_copy(words[:], token_words[:].bitcast(U32).indirect(slot_list(first * C, count * C)))
+            return [words[:, i * C : (i + 1) * C] for i in range(count)], words
 
-        def sums(acc, stationary, words, slot_scales):
+        def sums(acc, stationary, words, scales):
             nc.tensor.matmul_mx(
                 out=acc,
                 lhsT=stationary[0].bitcast(FP8X4),
                 lhsT_scale=stationary[1],
                 rhs=words.bitcast(FP8X4),
-                rhs_scale=slot_scales,
+                rhs_scale=scales,
                 start=True,
                 stop=True,
             )
@@ -118,115 +95,125 @@ def tile_moe_shr_lin_silu_kernel(tc, x_words, x_scales, w, b, gate, offs, out):
         def silu(result, acc, e):
             nc.scalar.activation(result, acc, SILU, bias=bias[:, e : e + 1])
 
-        def bank(name, tag):
-            return psum.tile([P, BANK], F32, name=name, tag=tag)
+        def bank(name, number):
+            return psum.tile([P, BANK], F32, name=name, tag="bank%d" % number)
 
-        def product(name, y, gate_part, width, at):
-            gated = placed(name, [P, width], F32, at)
-            nc.gpsimd.tensor_tensor(gated[:], y, gate_part, MULT)
-            return gated
-
-        def add(name, gated, ys, width, at):
-            both = placed(name, [P, width], F32, at)
-            nc.gpsimd.tensor_tensor(both[:], gated[:], ys, ADD)
-            return both
-
-        def scatter_copy(first, count, both):
-            nc.vector.tensor_copy(total[:].indirect(slot_list(first * C, count * C)), both[:])
+        def slots(first, count=1):
+            return slice(first * C, (first + count) * C)
 
         left, right = slice(0, C), slice(C, 2 * C)
-        token_words = sbuf.tile([P, T], I32, name="token_words", align_bytes=ALIGN)
-        nc.sync.dma_start(token_words[:], x_words[0].rearrange("p t r -> p (t r)").bitcast(I32))
-        raw7 = load_w(7, 1, 4096)
-        raw8 = load_w(8, 1, 32768)
-        raw56 = load_w(5, 2, 38912)
-        raw4 = load_w(4, 1, 73728)
+
+        spread_scales = placed("spread_scales", [P, T], U8)
+        nc.sync.dma_start(spread_scales[FIRST_ROW:P, :].bitcast(I32), x_scales[0].bitcast(I32))
+        nc.vector.memset(spread_scales[0:FIRST_ROW, :].bitcast(I32), 0)
+        offsets = sbuf.tile([P, E * C // LIST_COLUMN], U16, name="offsets")
+        nc.sync.dma_start(offsets[:], offs)
+        warm_up = sbuf.tile([P, 2], F32, name="warm_up")
+        nc.vector.memset(warm_up[:, 0:1], 0.0)
+        nc.scalar.activation(warm_up[:, 1:2], warm_up[:, 0:1], SILU)
         bias = sbuf.tile([P, E + 1], F32, name="bias")
-        nc.sync.dma_start(bias[:], b)
+        nc.gpsimd.dma_start(bias[:], b)
+        window_s = placed("window_s", [P, T], F32)
+        nc.gpsimd.memset(window_s[:], 0.0)
+        window_v = placed("window_v", [P, T], F32)
 
-        picked_high = gather_scales(1, None)
-        scales_high = to_scale_tile(picked_high[:], placed("scales_high", [P, HALF_SLOTS], U8, None))
-        words_high = gather_words(4, 4, None)
-        words45, words67 = words_high[:, :BANK], words_high[:, BANK:]
-        rounded78 = placed("rounded78", [P, 2, N, PACK], BF16, None)
-        rounded56 = placed("rounded56", [P, 2, N, PACK], BF16, None)
-        rounded4 = placed("rounded4", [P, 1, N, PACK], BF16, None)
-        rounded01 = placed("rounded01", [P, 2, N, PACK], BF16, 49152)
-        rounded23 = placed("rounded23", [P, 2, N, PACK], BF16, 57344)
-        round_into(rounded78, 0, raw7[0])
-        gate67 = load_gate(6, 2, 3072)
-        raw01 = load_w(0, 2, 5120)
-        round_into(rounded78, 1, raw8[0])
-        raw23 = load_w(2, 2, 29696)
-        w7, w_shared = quantize_w(rounded78, 2, "78", None)
-        words01 = gather_words(0, 2, 33856)
-        round_into(rounded56, 0, raw56[0])
-        round_into(rounded56, 1, raw56[1])
-        gate45 = load_gate(4, 2, 37888)
-        gate_low = load_gate(0, HALF_EXPERTS, 40960)
-        w5, w6 = quantize_w(rounded56, 2, "56", None)
-        round_into(rounded4, 0, raw4[0])
-        w4 = quantize_w(rounded4, 1, "4", None)[0]
-        picked_low = gather_scales(0, 73728)
-        scales_low = to_scale_tile(picked_low[:], placed("scales_low", [P, HALF_SLOTS], U8, None))
-        words23 = gather_words(2, 2, 74752)
+        token_words = placed("token_words", [P, T], I32)
+        token_scales = placed("token_scales", [P, T], U8)
+        slot_scales = placed("slot_scales", [P, T], U8)
+        words_hbm = x_words[0].rearrange("p t r -> p (t r)").bitcast(I32)
+        raw8 = load_w(8, 1)
+        raw01 = load_w(0, 2)
+        raw45 = load_w(4, 2)
+        raw67 = load_w(6, 2)
+        for r in range(SCALE_ROWS):
+            nc.sync.dma_start(token_scales[r:P:QUADRANT, :].bitcast(I32), x_scales[0, r:16:SCALE_ROWS, :].bitcast(I32))
+        nc.sync.dma_start(token_words[:, : T // 2], words_hbm[:, : T // 2])
+        nc.sync.dma_start(token_words[:, T // 2 :], words_hbm[:, T // 2 :])
+        raw23 = load_w(2, 2)
 
-        y67 = placed("y67", [P, BANK], F32, None)
-        ys67 = placed("ys67", [P, BANK], F32, None)
-        gated67 = placed("gated67", [P, BANK], F32, 65536)
-        acc_y7, acc_y6, acc_ys67 = bank("acc_y7", "bank0"), bank("acc_y6", "bank1"), bank("acc_ys67", "bank2")
-        sums(acc_y7[:, left], w7, words67[:, right], scales_high[:, 3 * C :])
-        sums(acc_ys67[:], w_shared, words67, scales_high[:, 2 * C :])
-        sums(acc_y6[:, left], w6, words67[:, left], scales_high[:, 2 * C : 3 * C])
-        silu(y67[:, right], acc_y7[:, left], 7)
-        nc.gpsimd.tensor_tensor(gated67[:, right], y67[:, right], gate67[:, right], MULT)
-        silu(y67[:, left], acc_y6[:, left], 6)
-        nc.gpsimd.tensor_tensor(gated67[:, left], y67[:, left], gate67[:, left], MULT)
-        silu(ys67[:], acc_ys67[:], E)
-        round_into(rounded01, 0, raw01[0])
-        round_into(rounded01, 1, raw01[1])
-        both67 = add("both67", gated67, ys67[:], BANK, None)
-        w_low = quantize_w(rounded01, 2, "01", 65536)
-        total = placed("total", [P, T], F32, 9152)
-        scatter_copy(6, 2, both67)
+        picked = placed("picked", [P, T], U8)
 
-        y45 = placed("y45", [P, BANK], F32, None)
-        ys45 = placed("ys45", [P, BANK], F32, None)
-        acc_y45, acc_ys45 = bank("acc_y45", "bank3"), bank("acc_ys45", "bank4")
-        sums(acc_y45[:, right], w5, words45[:, right], scales_high[:, C : 2 * C])
-        sums(acc_y45[:, left], w4, words45[:, left], scales_high[:, :C])
-        sums(acc_ys45[:], w_shared, words45, scales_high[:, : 2 * C])
-        silu(y45[:, left], acc_y45[:, left], 4)
-        silu(y45[:, right], acc_y45[:, right], 5)
-        silu(ys45[:], acc_ys45[:], E)
+        def gather_bytes(first):
+            nc.vector.tensor_copy(picked[:, first : first + T // 2], spread_scales[:].indirect(slot_list(first, T // 2)))
+
+        rounded8 = placed("rounded8", [P, 1, N, PACK], BF16)
+        rounded0145 = placed("rounded0145", [P, 4, N, PACK], BF16)
+        rounded67 = placed("rounded67", [P, 2, N, PACK], BF16)
+        rounded23 = placed("rounded23", [P, 2, N, PACK], BF16)
+        gather_bytes(0)
+        round_into(rounded8, 0, raw8[0])
+        (w8,) = quantize_w(rounded8, 1, "8")
+        gather_bytes(T // 2)
+        move_scales(picked, 0, E)
+        gate_low = placed("gate_low", [P, 4 * C], F32)
+        nc.sync.dma_start(gate_low[:], gate[:, slots(0, 4)])
+        gate_high = placed("gate_high", [P, 4 * C], F32)
+        nc.sync.dma_start(gate_high[:], gate[:, slots(4, 4)])
+        round_into(rounded0145, 0, raw01[0])
+        round_into(rounded0145, 1, raw01[1])
+        round_into(rounded0145, 2, raw45[0])
+        round_into(rounded0145, 3, raw45[1])
+        w0, w1, w4, w5 = quantize_w(rounded0145, 4, "0145")
+
+        def shared_tokens(quarter):
+            cols = slice(quarter * BANK, (quarter + 1) * BANK)
+            acc = bank("acc_tokens%d" % quarter, quarter)
+            sums(acc[:], w8, token_words[:, cols].bitcast(U32), token_scales[:, cols])
+            silu(window_v[:, cols], acc[:], E)
+
+        round_into(rounded67, 0, raw67[0])
+        round_into(rounded67, 1, raw67[1])
+        w6, w7 = quantize_w(rounded67, 2, "67")
+        shared_tokens(0)
+        shared_tokens(1)
+        shared_tokens(2)
+        shared_tokens(3)
         round_into(rounded23, 0, raw23[0])
         round_into(rounded23, 1, raw23[1])
-        gated45 = product("gated45", y45[:], gate45[:], BANK, 49152)
-        both45 = add("both45", gated45, ys45[:], BANK, 31808)
-        w_low = w_low + quantize_w(rounded23, 2, "23", 49152)
-        scatter_copy(4, 2, both45)
 
-        y_both = placed("y_low", [P, 2 * HALF_SLOTS], F32, 23616)
-        y_low = y_both[:, :HALF_SLOTS]
-        ys_low = y_both[:, HALF_SLOTS:]
-        gated_low = placed("gated_low", [P, HALF_SLOTS], F32, 57344)
-        for pair, words in enumerate((words01, words23)):
-            cols = slice(pair * BANK, (pair + 1) * BANK)
-            acc = bank("acc_y%d" % pair, "bank%d" % (5 + pair))
-            for i, side in enumerate((left, right)):
-                e = PAIR * pair + i
-                sums(acc[:, side], w_low[e], words[:, side], scales_low[:, e * C : (e + 1) * C])
-            for i, side in enumerate((left, right)):
-                e = PAIR * pair + i
-                silu(y_low[:, e * C : (e + 1) * C], acc[:, side], e)
-            nc.gpsimd.tensor_tensor(gated_low[:, cols], y_low[:, cols], gate_low[:, cols], MULT)
-        for pair, words in enumerate((words01, words23)):
-            cols = slice(pair * BANK, (pair + 1) * BANK)
-            acc = bank("acc_ys%d" % pair, ("bank7", "bank0")[pair])
-            sums(acc[:], w_shared, words[:], scales_low[:, cols])
-            silu(ys_low[:, cols], acc[:], E)
-        nc.vector.tensor_tensor(total[:].indirect(slot_list(0, HALF_SLOTS)), gated_low[:], ys_low, ADD)
+        gated = placed("gated", [P, T], F32)
+        y = placed("y", [P, T], F32)
+        ys = placed("ys", [P, 4 * C], F32)
 
-        for half in range(2):
-            cols = slice(half * T // 2, (half + 1) * T // 2)
+        def product(first, count, gate_part):
+            nc.vector.tensor_tensor(gated[:, slots(first, count)], y[:, slots(first, count)], gate_part, MULT)
+
+        def scalar_scatter(first, count):
+            nc.scalar.activation(window_s[:].indirect(slot_list(first, count)), gated[:, first : first + count], COPY)
+
+        def pair(first, number, stationary, words):
+            acc = bank("acc%d" % first, number)
+            for i, side in enumerate((left, right)):
+                sums(acc[:, side], stationary[i], words[i], slot_scales[:, slots(first + i)])
+            for i, side in enumerate((left, right)):
+                silu(y[:, slots(first + i)], acc[:, side], first + i)
+
+        x01, x01_tile = gather_words(0, 2)
+        pair(0, 4, (w0, w1), x01)
+        x_high, x_high_tile = gather_words(4, 4)
+        pair(4, 5, (w4, w5), x_high[:2])
+        pair(6, 6, (w6, w7), x_high[2:])
+        x23, x23_tile = gather_words(2, 2)
+        w2, w3 = quantize_w(rounded23, 2, "23")
+        product(0, 2, gate_low[:, slots(0, 2)])
+        acc_s45 = bank("acc_s45", 7)
+        sums(acc_s45[:], w8, x_high_tile[:, :BANK], slot_scales[:, slots(4, 2)])
+        silu(ys[:, :BANK], acc_s45[:], E)
+        product(4, 4, gate_high[:])
+        pair(2, 0, (w2, w3), x23)
+        product(2, 2, gate_low[:, slots(2, 2)])
+        acc_s67 = bank("acc_s67", 1)
+        sums(acc_s67[:], w8, x_high_tile[:, BANK:], slot_scales[:, slots(6, 2)])
+        silu(ys[:, BANK:], acc_s67[:], E)
+        scalar_scatter(0, 384)
+        nc.vector.tensor_tensor(window_v[:].indirect(slot_list(4 * C, 4 * C)), gated[:, slots(4, 4)], ys[:], ADD)
+        scalar_scatter(384, 384)
+        scalar_scatter(768, 256)
+
+        total = placed("total", [P, T], F32)
+        first = 0
+        for width in STORE_WIDTHS:
+            cols = slice(first, first + width)
+            nc.vector.tensor_tensor(total[:, cols], window_v[:, cols], window_s[:, cols], ADD)
             nc.sync.dma_start(out[:, cols], total[:, cols])
+            first = first + width

@@ -102,6 +102,7 @@ def tile_moe_shr_lin_silu_kernel(tc, x_words, x_scales, w, b, gate, offs, out):
             return slice(first * C, (first + count) * C)
 
         left, right = slice(0, C), slice(C, 2 * C)
+        SPLIT = 1152
 
         spread_scales = placed("spread_scales", [P, T], U8)
         nc.sync.dma_start(spread_scales[FIRST_ROW:P, :].bitcast(I32), x_scales[0].bitcast(I32))
@@ -173,7 +174,7 @@ def tile_moe_shr_lin_silu_kernel(tc, x_words, x_scales, w, b, gate, offs, out):
 
         gated = placed("gated", [P, T], F32)
         y = placed("y", [P, T], F32)
-        ys = placed("ys", [P, 4 * C], F32)
+        ys = placed("ys", [P, T - SPLIT], F32)
 
         def product(first, count, gate_part):
             nc.vector.tensor_tensor(gated[:, slots(first, count)], y[:, slots(first, count)], gate_part, MULT)
@@ -195,20 +196,22 @@ def tile_moe_shr_lin_silu_kernel(tc, x_words, x_scales, w, b, gate, offs, out):
         pair(6, 6, (w6, w7), x_high[2:])
         x23, x23_tile = gather_words(2, 2)
         w2, w3 = quantize_w(rounded23, 2, "23")
-        product(0, 2, gate_low[:, slots(0, 2)])
+        product(1, 1, gate_low[:, slots(1)])
+        nc.vector.tensor_tensor(window_s[:].indirect(slot_list(0, C)), y[:, slots(0)], gate_low[:, slots(0)], MULT)
         acc_s45 = bank("acc_s45", 7)
-        sums(acc_s45[:], w8, x_high_tile[:, :BANK], slot_scales[:, slots(4, 2)])
-        silu(ys[:, :BANK], acc_s45[:], E)
+        sums(acc_s45[:, :128], w8, x_high_tile[:, 128:C], slot_scales[:, SPLIT : 5 * C])
+        sums(acc_s45[:, 128:384], w8, x_high[1], slot_scales[:, slots(5)])
+        silu(ys[:, :384], acc_s45[:, :384], E)
         product(4, 4, gate_high[:])
         pair(2, 0, (w2, w3), x23)
         product(2, 2, gate_low[:, slots(2, 2)])
         acc_s67 = bank("acc_s67", 1)
         sums(acc_s67[:], w8, x_high_tile[:, BANK:], slot_scales[:, slots(6, 2)])
-        silu(ys[:, BANK:], acc_s67[:], E)
-        scalar_scatter(0, 384)
-        nc.vector.tensor_tensor(window_v[:].indirect(slot_list(4 * C, 4 * C)), gated[:, slots(4, 4)], ys[:], ADD)
-        scalar_scatter(384, 384)
-        scalar_scatter(768, 256)
+        silu(ys[:, 384:], acc_s67[:], E)
+        scalar_scatter(C, C)
+        nc.vector.tensor_tensor(window_v[:].indirect(slot_list(SPLIT, T - SPLIT)), gated[:, SPLIT:], ys[:], ADD)
+        scalar_scatter(2 * C, 384)
+        scalar_scatter(2 * C + 384, C)
 
         total = placed("total", [P, T], F32)
         first = 0

@@ -122,14 +122,14 @@ def tile_moe_shr_lin_silu_kernel(tc, x_words, x_scales, w, b, gate, offs, out):
         token_scales = placed("token_scales", [P, T], U8)
         slot_scales = placed("slot_scales", [P, T], U8)
         words_hbm = x_words[0].rearrange("p t r -> p (t r)").bitcast(I32)
+        for r in range(SCALE_ROWS):
+            nc.sync.dma_start(token_scales[r:P:QUADRANT, :].bitcast(I32), x_scales[0, r:16:SCALE_ROWS, :].bitcast(I32))
         raw8 = load_w(8, 1)
         raw01 = load_w(0, 2)
         raw45 = load_w(4, 2)
-        raw67 = load_w(6, 2)
-        for r in range(SCALE_ROWS):
-            nc.sync.dma_start(token_scales[r:P:QUADRANT, :].bitcast(I32), x_scales[0, r:16:SCALE_ROWS, :].bitcast(I32))
         nc.sync.dma_start(token_words[:, : T // 2], words_hbm[:, : T // 2])
         nc.sync.dma_start(token_words[:, T // 2 :], words_hbm[:, T // 2 :])
+        raw67 = load_w(6, 2)
         raw23 = load_w(2, 2)
 
         picked = placed("picked", [P, T], U8)
@@ -139,8 +139,7 @@ def tile_moe_shr_lin_silu_kernel(tc, x_words, x_scales, w, b, gate, offs, out):
 
         rounded8 = placed("rounded8", [P, 1, N, PACK], BF16)
         rounded0145 = placed("rounded0145", [P, 4, N, PACK], BF16)
-        rounded67 = placed("rounded67", [P, 2, N, PACK], BF16)
-        rounded23 = placed("rounded23", [P, 2, N, PACK], BF16)
+        rounded_late = placed("rounded_late", [P, 4, N, PACK], BF16)
         gather_bytes(0)
         round_into(rounded8, 0, raw8[0])
         (w8,) = quantize_w(rounded8, 1, "8")
@@ -162,15 +161,10 @@ def tile_moe_shr_lin_silu_kernel(tc, x_words, x_scales, w, b, gate, offs, out):
             sums(acc[:], w8, token_words[:, cols].bitcast(U32), token_scales[:, cols])
             silu(window_v[:, cols], acc[:], E)
 
-        round_into(rounded67, 0, raw67[0])
-        round_into(rounded67, 1, raw67[1])
-        w6, w7 = quantize_w(rounded67, 2, "67")
-        shared_tokens(0)
-        shared_tokens(1)
-        shared_tokens(2)
-        shared_tokens(3)
-        round_into(rounded23, 0, raw23[0])
-        round_into(rounded23, 1, raw23[1])
+        for quarter in range(3):
+            shared_tokens(quarter)
+        for i, raw in enumerate(raw67 + raw23):
+            round_into(rounded_late, i, raw)
 
         gated = placed("gated", [P, T], F32)
         y = placed("y", [P, T], F32)
@@ -193,18 +187,19 @@ def tile_moe_shr_lin_silu_kernel(tc, x_words, x_scales, w, b, gate, offs, out):
         pair(0, 4, (w0, w1), x01)
         x_high, x_high_tile = gather_words(4, 4)
         pair(4, 5, (w4, w5), x_high[:2])
-        pair(6, 6, (w6, w7), x_high[2:])
         x23, x23_tile = gather_words(2, 2)
-        w2, w3 = quantize_w(rounded23, 2, "23")
+        w6, w7, w2, w3 = quantize_w(rounded_late, 4, "late")
         product(1, 1, gate_low[:, slots(1)])
         nc.vector.tensor_tensor(window_s[:].indirect(slot_list(0, C)), y[:, slots(0)], gate_low[:, slots(0)], MULT)
+        shared_tokens(3)
+        pair(6, 6, (w6, w7), x_high[2:])
+        product(4, 4, gate_high[:])
+        pair(2, 0, (w2, w3), x23)
+        product(2, 2, gate_low[:, slots(2, 2)])
         acc_s45 = bank("acc_s45", 7)
         sums(acc_s45[:, :128], w8, x_high_tile[:, 128:C], slot_scales[:, SPLIT : 5 * C])
         sums(acc_s45[:, 128:384], w8, x_high[1], slot_scales[:, slots(5)])
         silu(ys[:, :384], acc_s45[:, :384], E)
-        product(4, 4, gate_high[:])
-        pair(2, 0, (w2, w3), x23)
-        product(2, 2, gate_low[:, slots(2, 2)])
         acc_s67 = bank("acc_s67", 1)
         sums(acc_s67[:], w8, x_high_tile[:, BANK:], slot_scales[:, slots(6, 2)])
         silu(ys[:, 384:], acc_s67[:], E)

@@ -20,12 +20,14 @@ ADD = mybir.AluOpType.add
 P = 128
 QUADRANT = 32
 SCALE_ROWS = 4
-FIRST_ROW = 112
 PACK = 4
 RUN = 4
 LIST_COLUMN = 16
 BANK = 512
 ALIGN = 64
+FIRST_ROW = 112
+RAW67, RAW01, RAW23 = 0, 6144, 16384
+SPLIT = 704
 STORE_WIDTHS = (256, 384, 384, 384, 384, 256)
 assert sum(STORE_WIDTHS) == T
 
@@ -42,6 +44,9 @@ def tile_moe_shr_lin_silu_kernel(tc, x_words, x_scales, w, b, gate, offs, out):
                 return sbuf.tile(shape, dtype, name=name, align_bytes=ALIGN)
             return reused.tile(shape, dtype, name=name, offset=at, align_bytes=ALIGN)
 
+        def slots(first, count=1):
+            return slice(first * C, (first + count) * C)
+
         def slot_list(first, count):
             return offsets[:, first // LIST_COLUMN : (first + count) // LIST_COLUMN]
 
@@ -50,36 +55,39 @@ def tile_moe_shr_lin_silu_kernel(tc, x_words, x_scales, w, b, gate, offs, out):
             nc.sync.dma_start(raw[:], w[first : first + count].rearrange("e (p j) n -> p e j n", j=PACK))
             return [raw[:, e] for e in range(count)]
 
-        def round_into(rounded, i, raw):
+        def load_gate(first, count, at=None):
+            part = placed("gate%d" % first, [P, count * C], F32, at)
+            nc.sync.dma_start(part[:], gate[:, slots(first, count)])
+            return part
+
+        def round_on_scalar(rounded, i, raw):
             nc.scalar.copy(
                 rounded[:, i].rearrange("p (c i) j -> p c j i", i=RUN),
                 raw.rearrange("p j (c i) -> p c j i", i=RUN),
             )
 
-        def quantize_w(rounded, count, name, at=None):
+        def round_on_gpsimd(rounded, i, raw):
+            nc.gpsimd.tensor_scalar(rounded[:, i], raw.rearrange("p j n -> p n j"), 1.0, 0.0, MULT, ADD)
+
+        def quantize_w(rounded, first, count, name, at=None):
             codes = placed("w_words_" + name, [P, count * N], U32, at)
             scales = placed("w_scales_" + name, [P, count * N], U8)
             nc.vector.quantize_mx(
-                out=codes[:].bitcast(FP8X4), scales=scales[:], in_=rounded[:].rearrange("p e n j -> p (e n j)")
+                out=codes[:].bitcast(FP8X4),
+                scales=scales[:],
+                in_=rounded[:, first : first + count].rearrange("p e n j -> p (e n j)"),
             )
             return [(codes[:, i * N : (i + 1) * N], scales[:, i * N : (i + 1) * N]) for i in range(count)]
 
         def gather_scales(first, count, at=None):
-            picked = placed("picked_scales%d" % first, [P, count * C], U8, at)
-            nc.vector.tensor_copy(picked[:], spread_scales[:].indirect(slot_list(first * C, count * C)))
+            picked = placed("slot_scales%d" % first, [P, count * C], U8, at)
+            nc.vector.tensor_copy(picked[:], token_scales[:].indirect(slot_list(first * C, count * C)))
             return picked
 
-        def move_scales(picked, first, count):
-            for r in range(SCALE_ROWS):
-                nc.sync.dma_start(
-                    slot_scales[r:P:QUADRANT, first * C : (first + count) * C].bitcast(I32),
-                    picked[FIRST_ROW + r : P : SCALE_ROWS, :].bitcast(I32),
-                )
-
         def gather_words(first, count, at=None):
-            words = placed("slot_words%d" % first, [P, count * C], U32, at)
-            nc.vector.tensor_copy(words[:], token_words[:].bitcast(U32).indirect(slot_list(first * C, count * C)))
-            return [words[:, i * C : (i + 1) * C] for i in range(count)], words
+            picked = placed("slot_words%d" % first, [P, count * C], U32, at)
+            nc.vector.tensor_copy(picked[:], token_words[:].bitcast(U32).indirect(slot_list(first * C, count * C)))
+            return picked
 
         def sums(acc, stationary, words, scales):
             nc.tensor.matmul_mx(
@@ -98,17 +106,19 @@ def tile_moe_shr_lin_silu_kernel(tc, x_words, x_scales, w, b, gate, offs, out):
         def bank(name, number):
             return psum.tile([P, BANK], F32, name=name, tag="bank%d" % number)
 
-        def slots(first, count=1):
-            return slice(first * C, (first + count) * C)
+        def scalar_scatter(first, count):
+            nc.scalar.activation(window_s[:].indirect(slot_list(first, count)), gated[:, first : first + count], COPY)
 
-        left, right = slice(0, C), slice(C, 2 * C)
-        SPLIT = 1152
-
+        token_scales = placed("token_scales", [P, T], U8)
+        nc.gpsimd.memset(token_scales[:].bitcast(I32), 0)
         spread_scales = placed("spread_scales", [P, T], U8)
         nc.sync.dma_start(spread_scales[FIRST_ROW:P, :].bitcast(I32), x_scales[0].bitcast(I32))
         nc.vector.memset(spread_scales[0:FIRST_ROW, :].bitcast(I32), 0)
         offsets = sbuf.tile([P, E * C // LIST_COLUMN], U16, name="offsets")
         nc.sync.dma_start(offsets[:], offs)
+        raw8 = load_w(8, 1)
+        for r in range(SCALE_ROWS):
+            nc.sync.dma_start(token_scales[r:P:QUADRANT, :].bitcast(I32), x_scales[0, r:16:SCALE_ROWS, :].bitcast(I32))
         warm_up = sbuf.tile([P, 2], F32, name="warm_up")
         nc.vector.memset(warm_up[:, 0:1], 0.0)
         nc.scalar.activation(warm_up[:, 1:2], warm_up[:, 0:1], SILU)
@@ -118,42 +128,33 @@ def tile_moe_shr_lin_silu_kernel(tc, x_words, x_scales, w, b, gate, offs, out):
         nc.gpsimd.memset(window_s[:], 0.0)
         window_v = placed("window_v", [P, T], F32)
 
+        raw67 = load_w(6, 2, RAW67)
         token_words = placed("token_words", [P, T], I32)
-        token_scales = placed("token_scales", [P, T], U8)
-        slot_scales = placed("slot_scales", [P, T], U8)
         words_hbm = x_words[0].rearrange("p t r -> p (t r)").bitcast(I32)
-        for r in range(SCALE_ROWS):
-            nc.sync.dma_start(token_scales[r:P:QUADRANT, :].bitcast(I32), x_scales[0, r:16:SCALE_ROWS, :].bitcast(I32))
-        raw8 = load_w(8, 1)
-        raw01 = load_w(0, 2)
-        raw45 = load_w(4, 2)
         nc.sync.dma_start(token_words[:, : T // 2], words_hbm[:, : T // 2])
+        raw5 = load_w(5, 1)
         nc.sync.dma_start(token_words[:, T // 2 :], words_hbm[:, T // 2 :])
-        raw67 = load_w(6, 2)
-        raw23 = load_w(2, 2)
+        gate7 = load_gate(7, 1)
+        raw4 = load_w(4, 1)
+        raw01 = load_w(0, 2, RAW01)
+        raw23 = load_w(2, 2, RAW23)
 
-        picked = placed("picked", [P, T], U8)
-
-        def gather_bytes(first):
-            nc.vector.tensor_copy(picked[:, first : first + T // 2], spread_scales[:].indirect(slot_list(first, T // 2)))
-
-        rounded8 = placed("rounded8", [P, 1, N, PACK], BF16)
-        rounded0145 = placed("rounded0145", [P, 4, N, PACK], BF16)
-        rounded_late = placed("rounded_late", [P, 4, N, PACK], BF16)
-        gather_bytes(0)
-        round_into(rounded8, 0, raw8[0])
-        (w8,) = quantize_w(rounded8, 1, "8")
-        gather_bytes(T // 2)
-        move_scales(picked, 0, E)
-        gate_low = placed("gate_low", [P, 4 * C], F32)
-        nc.sync.dma_start(gate_low[:], gate[:, slots(0, 4)])
-        gate_high = placed("gate_high", [P, 4 * C], F32)
-        nc.sync.dma_start(gate_high[:], gate[:, slots(4, 4)])
-        round_into(rounded0145, 0, raw01[0])
-        round_into(rounded0145, 1, raw01[1])
-        round_into(rounded0145, 2, raw45[0])
-        round_into(rounded0145, 3, raw45[1])
-        w0, w1, w4, w5 = quantize_w(rounded0145, 4, "0145")
+        picked = placed("picked", [P, 4 * C], U8)
+        nc.vector.tensor_copy(picked[:], spread_scales[:].indirect(slot_list(0, 4 * C)))
+        scales03 = placed("slot_scales0", [P, 4 * C], U8)
+        for r in range(SCALE_ROWS):
+            nc.sync.dma_start(
+                scales03[r:P:QUADRANT, :].bitcast(I32), picked[FIRST_ROW + r : P : SCALE_ROWS, :].bitcast(I32)
+            )
+        scales67 = gather_scales(6, 2)
+        rounded867 = placed("rounded867", [P, 3, N, PACK], BF16)
+        for i, raw in enumerate(raw8 + raw67):
+            round_on_scalar(rounded867, i, raw)
+        w8, w6, w7 = quantize_w(rounded867, 0, 3, "867")
+        scales45 = gather_scales(4, 2, RAW67)
+        rounded5 = placed("rounded5", [P, 1, N, PACK], BF16)
+        round_on_scalar(rounded5, 0, raw5[0])
+        (w5,) = quantize_w(rounded5, 0, 1, "5")
 
         def shared_tokens(quarter):
             cols = slice(quarter * BANK, (quarter + 1) * BANK)
@@ -161,52 +162,62 @@ def tile_moe_shr_lin_silu_kernel(tc, x_words, x_scales, w, b, gate, offs, out):
             sums(acc[:], w8, token_words[:, cols].bitcast(U32), token_scales[:, cols])
             silu(window_v[:, cols], acc[:], E)
 
-        for quarter in range(3):
-            shared_tokens(quarter)
-        for i, raw in enumerate(raw67 + raw23):
-            round_into(rounded_late, i, raw)
-
-        gated = placed("gated", [P, T], F32)
-        y = placed("y", [P, T], F32)
-        ys = placed("ys", [P, T - SPLIT], F32)
+        def expert(e, number, stationary, words, scales):
+            acc = bank("acc%d" % e, number)
+            sums(acc[:, :C], stationary, words[:, slots(e % 2)], scales)
+            silu(y[:, slots(e)], acc[:, :C], e)
 
         def product(first, count, gate_part):
             nc.vector.tensor_tensor(gated[:, slots(first, count)], y[:, slots(first, count)], gate_part, MULT)
 
-        def scalar_scatter(first, count):
-            nc.scalar.activation(window_s[:].indirect(slot_list(first, count)), gated[:, first : first + count], COPY)
+        y = placed("y", [P, T], F32)
+        gated = placed("gated", [P, T], F32)
+        for quarter in range(4):
+            shared_tokens(quarter)
+        words67 = gather_words(6, 2)
+        expert(7, 4, w7, words67, scales67[:, slots(1)])
+        expert(6, 5, w6, words67, scales67[:, slots(0)])
+        words45 = gather_words(4, 2)
+        expert(5, 7, w5, words45, scales45[:, slots(1)])
+        words03 = gather_words(0, 4)
+        words01, words23 = words03[:, slots(0, 2)], words03[:, slots(2, 2)]
 
-        def pair(first, number, stationary, words):
-            acc = bank("acc%d" % first, number)
-            for i, side in enumerate((left, right)):
-                sums(acc[:, side], stationary[i], words[i], slot_scales[:, slots(first + i)])
-            for i, side in enumerate((left, right)):
-                silu(y[:, slots(first + i)], acc[:, side], first + i)
+        rounded04 = placed("rounded04", [P, 5, N, PACK], BF16)
+        for i, raw in enumerate(raw4 + raw01):
+            round_on_gpsimd(rounded04, i, raw)
+        gated7 = placed("gated7", [P, C], F32, RAW01 + 1024)
+        nc.gpsimd.tensor_tensor(gated7[:], y[:, slots(7)], gate7[:], MULT)
+        round_on_gpsimd(rounded04, 3, raw23[0])
+        round_on_scalar(rounded04, 4, raw23[1])
+        nc.scalar.activation(window_s[:].indirect(slot_list(7 * C, C)), gated7[:], COPY)
+        gate56 = load_gate(5, 2, RAW01 - 1024)
+        gate04 = load_gate(0, 5, RAW01 + 3072)
+        w4, w0, w1, w2 = quantize_w(rounded04, 0, 4, "4012")
+        (w3,) = quantize_w(rounded04, 4, 1, "3", RAW23)
 
-        x01, x01_tile = gather_words(0, 2)
-        pair(0, 4, (w0, w1), x01)
-        x_high, x_high_tile = gather_words(4, 4)
-        pair(4, 5, (w4, w5), x_high[:2])
-        x23, x23_tile = gather_words(2, 2)
-        w6, w7, w2, w3 = quantize_w(rounded_late, 4, "late")
-        product(1, 1, gate_low[:, slots(1)])
-        nc.vector.tensor_tensor(window_s[:].indirect(slot_list(0, C)), y[:, slots(0)], gate_low[:, slots(0)], MULT)
-        shared_tokens(3)
-        pair(6, 6, (w6, w7), x_high[2:])
-        product(4, 4, gate_high[:])
-        pair(2, 0, (w2, w3), x23)
-        product(2, 2, gate_low[:, slots(2, 2)])
-        acc_s45 = bank("acc_s45", 7)
-        sums(acc_s45[:, :128], w8, x_high_tile[:, 128:C], slot_scales[:, SPLIT : 5 * C])
-        sums(acc_s45[:, 128:384], w8, x_high[1], slot_scales[:, slots(5)])
-        silu(ys[:, :384], acc_s45[:, :384], E)
-        acc_s67 = bank("acc_s67", 1)
-        sums(acc_s67[:], w8, x_high_tile[:, BANK:], slot_scales[:, slots(6, 2)])
-        silu(ys[:, 384:], acc_s67[:], E)
-        scalar_scatter(C, C)
-        nc.vector.tensor_tensor(window_v[:].indirect(slot_list(SPLIT, T - SPLIT)), gated[:, SPLIT:], ys[:], ADD)
-        scalar_scatter(2 * C, 384)
-        scalar_scatter(2 * C + 384, C)
+        ys = placed("ys", [P, SPLIT], F32)
+        acc_shared = bank("acc_shared01", 0)
+        sums(acc_shared[:], w8, words01, scales03[:, slots(0, 2)])
+        silu(ys[:, :BANK], acc_shared[:], E)
+        acc_rest = bank("acc_shared2", 1)
+        sums(acc_rest[:, :128], w8, words23[:, :128], scales03[:, BANK : BANK + 128])
+        sums(acc_rest[:, 128:192], w8, words23[:, 128:192], scales03[:, BANK + 128 : SPLIT])
+        silu(ys[:, BANK:], acc_rest[:, : SPLIT - BANK], E)
+        expert(0, 2, w0, words01, scales03[:, slots(0)])
+        expert(1, 3, w1, words01, scales03[:, slots(1)])
+        expert(2, 4, w2, words23, scales03[:, slots(2)])
+        expert(3, 5, w3, words23, scales03[:, slots(3)])
+
+        expert(4, 6, w4, words45, scales45[:, slots(0)])
+
+        product(5, 1, gate56[:, slots(0)])
+        nc.vector.tensor_tensor(window_s[:].indirect(slot_list(6 * C, C)), y[:, slots(6)], gate56[:, slots(1)], MULT)
+        product(0, 3, gate04[:, slots(0, 3)])
+        product(3, 2, gate04[:, slots(3, 2)])
+        scalar_scatter(5 * C, C)
+        nc.vector.tensor_tensor(window_v[:].indirect(slot_list(0, SPLIT)), gated[:, :SPLIT], ys[:], ADD)
+        scalar_scatter(SPLIT, 288)
+        scalar_scatter(SPLIT + 288, 288)
 
         total = placed("total", [P, T], F32)
         first = 0

@@ -26,7 +26,7 @@ LIST_COLUMN = 16
 BANK = 512
 ALIGN = 64
 FIRST_ROW = 112
-RAW67, RAW01, RAW23 = 0, 6144, 16384
+RAW67, RAW01, GATE7, Y7 = 0, 6144, 16384, 18432
 SPLIT = 704
 STORE_WIDTHS = (256, 384, 384, 384, 384, 256)
 assert sum(STORE_WIDTHS) == T
@@ -65,6 +65,9 @@ def tile_moe_shr_lin_silu_kernel(tc, x_words, x_scales, w, b, gate, offs, out):
                 rounded[:, i].rearrange("p (c i) j -> p c j i", i=RUN),
                 raw.rearrange("p j (c i) -> p c j i", i=RUN),
             )
+
+        def round_on_vector(rounded, i, raw):
+            nc.vector.tensor_copy(rounded[:, i], raw.rearrange("p j n -> p n j"))
 
         def round_on_gpsimd(rounded, i, raw):
             nc.gpsimd.tensor_scalar(rounded[:, i], raw.rearrange("p j n -> p n j"), 1.0, 0.0, MULT, ADD)
@@ -134,24 +137,24 @@ def tile_moe_shr_lin_silu_kernel(tc, x_words, x_scales, w, b, gate, offs, out):
         nc.sync.dma_start(token_words[:, : T // 2], words_hbm[:, : T // 2])
         raw5 = load_w(5, 1)
         nc.sync.dma_start(token_words[:, T // 2 :], words_hbm[:, T // 2 :])
-        gate7 = load_gate(7, 1)
+        gate7 = load_gate(7, 1, GATE7)
         raw4 = load_w(4, 1)
         raw01 = load_w(0, 2, RAW01)
-        raw23 = load_w(2, 2, RAW23)
+        raw23 = load_w(2, 2)
 
-        picked = placed("picked", [P, 4 * C], U8)
-        nc.vector.tensor_copy(picked[:], spread_scales[:].indirect(slot_list(0, 4 * C)))
-        scales03 = placed("slot_scales0", [P, 4 * C], U8)
+        picked = placed("picked", [P, 5 * C], U8)
+        nc.vector.tensor_copy(picked[:], spread_scales[:].indirect(slot_list(0, 5 * C)))
+        scales03 = placed("slot_scales0", [P, 5 * C], U8)
         for r in range(SCALE_ROWS):
             nc.sync.dma_start(
                 scales03[r:P:QUADRANT, :].bitcast(I32), picked[FIRST_ROW + r : P : SCALE_ROWS, :].bitcast(I32)
             )
-        scales67 = gather_scales(6, 2)
+        scales5 = gather_scales(5, 1)
         rounded867 = placed("rounded867", [P, 3, N, PACK], BF16)
         for i, raw in enumerate(raw8 + raw67):
             round_on_scalar(rounded867, i, raw)
         w8, w6, w7 = quantize_w(rounded867, 0, 3, "867")
-        scales45 = gather_scales(4, 2, RAW67)
+        scales67 = gather_scales(6, 2, RAW67)
         rounded5 = placed("rounded5", [P, 1, N, PACK], BF16)
         round_on_scalar(rounded5, 0, raw5[0])
         (w5,) = quantize_w(rounded5, 0, 1, "5")
@@ -165,12 +168,13 @@ def tile_moe_shr_lin_silu_kernel(tc, x_words, x_scales, w, b, gate, offs, out):
         def expert(e, number, stationary, words, scales):
             acc = bank("acc%d" % e, number)
             sums(acc[:, :C], stationary, words[:, slots(e % 2)], scales)
-            silu(y[:, slots(e)], acc[:, :C], e)
+            silu(y7[:] if e == 7 else y[:, slots(e)], acc[:, :C], e)
 
         def product(first, count, gate_part):
             nc.vector.tensor_tensor(gated[:, slots(first, count)], y[:, slots(first, count)], gate_part, MULT)
 
-        y = placed("y", [P, T], F32)
+        y = placed("y", [P, 7 * C], F32)
+        y7 = placed("y7", [P, C], F32, Y7)
         gated = placed("gated", [P, T], F32)
         for quarter in range(4):
             shared_tokens(quarter)
@@ -178,22 +182,23 @@ def tile_moe_shr_lin_silu_kernel(tc, x_words, x_scales, w, b, gate, offs, out):
         expert(7, 4, w7, words67, scales67[:, slots(1)])
         expert(6, 5, w6, words67, scales67[:, slots(0)])
         words45 = gather_words(4, 2)
-        expert(5, 7, w5, words45, scales45[:, slots(1)])
+        expert(5, 7, w5, words45, scales5[:])
         words03 = gather_words(0, 4)
         words01, words23 = words03[:, slots(0, 2)], words03[:, slots(2, 2)]
 
-        rounded04 = placed("rounded04", [P, 5, N, PACK], BF16)
+        rounded04 = placed("rounded04", [P, 4, N, PACK], BF16)
         for i, raw in enumerate(raw4 + raw01):
             round_on_gpsimd(rounded04, i, raw)
         gated7 = placed("gated7", [P, C], F32, RAW01 + 1024)
-        nc.gpsimd.tensor_tensor(gated7[:], y[:, slots(7)], gate7[:], MULT)
-        round_on_gpsimd(rounded04, 3, raw23[0])
-        round_on_scalar(rounded04, 4, raw23[1])
+        nc.gpsimd.tensor_tensor(gated7[:], y7[:], gate7[:], MULT)
+        round_on_scalar(rounded04, 3, raw23[1])
         nc.scalar.activation(window_s[:].indirect(slot_list(7 * C, C)), gated7[:], COPY)
         gate56 = load_gate(5, 2, RAW01 - 1024)
         gate04 = load_gate(0, 5, RAW01 + 3072)
-        w4, w0, w1, w2 = quantize_w(rounded04, 0, 4, "4012")
-        (w3,) = quantize_w(rounded04, 4, 1, "3", RAW23)
+        rounded2 = placed("rounded2", [P, 1, N, PACK], BF16, GATE7)
+        round_on_vector(rounded2, 0, raw23[0])
+        w4, w0, w1, w3 = quantize_w(rounded04, 0, 4, "4013", Y7)
+        (w2,) = quantize_w(rounded2, 0, 1, "2")
 
         ys = placed("ys", [P, SPLIT], F32)
         acc_shared = bank("acc_shared01", 0)
@@ -208,7 +213,7 @@ def tile_moe_shr_lin_silu_kernel(tc, x_words, x_scales, w, b, gate, offs, out):
         expert(2, 4, w2, words23, scales03[:, slots(2)])
         expert(3, 5, w3, words23, scales03[:, slots(3)])
 
-        expert(4, 6, w4, words45, scales45[:, slots(0)])
+        expert(4, 6, w4, words45, scales03[:, slots(4)])
 
         product(5, 1, gate56[:, slots(0)])
         nc.vector.tensor_tensor(window_s[:].indirect(slot_list(6 * C, C)), y[:, slots(6)], gate56[:, slots(1)], MULT)

@@ -26,7 +26,7 @@ LIST_COLUMN = 16
 BANK = 512
 ALIGN = 64
 FIRST_ROW = 112
-RAW67, RAW01, GATE7, Y7 = 0, 6144, 16384, 18432
+RAW67, RAW01, GATE7, Y7, RAW23 = 0, 4096, 8192, 10240, 12288
 SPLIT = 704
 STORE_WIDTHS = (256, 384, 384, 384, 384, 256)
 assert sum(STORE_WIDTHS) == T
@@ -137,10 +137,8 @@ def tile_moe_shr_lin_silu_kernel(tc, x_words, x_scales, w, b, gate, offs, out):
         nc.sync.dma_start(token_words[:, : T // 2], words_hbm[:, : T // 2])
         raw5 = load_w(5, 1)
         nc.sync.dma_start(token_words[:, T // 2 :], words_hbm[:, T // 2 :])
-        gate7 = load_gate(7, 1, GATE7)
         raw4 = load_w(4, 1)
         raw01 = load_w(0, 2, RAW01)
-        raw23 = load_w(2, 2)
 
         picked = placed("picked", [P, 5 * C], U8)
         nc.vector.tensor_copy(picked[:], spread_scales[:].indirect(slot_list(0, 5 * C)))
@@ -149,6 +147,10 @@ def tile_moe_shr_lin_silu_kernel(tc, x_words, x_scales, w, b, gate, offs, out):
             nc.sync.dma_start(
                 scales03[r:P:QUADRANT, :].bitcast(I32), picked[FIRST_ROW + r : P : SCALE_ROWS, :].bitcast(I32)
             )
+        raw23 = load_w(2, 2, RAW23)
+        gate7 = load_gate(7, 1, GATE7)
+        gate04 = load_gate(0, 5)
+        gate56 = load_gate(5, 2)
         scales5 = gather_scales(5, 1)
         rounded867 = placed("rounded867", [P, 3, N, PACK], BF16)
         for i, raw in enumerate(raw8 + raw67):
@@ -183,8 +185,8 @@ def tile_moe_shr_lin_silu_kernel(tc, x_words, x_scales, w, b, gate, offs, out):
         expert(6, 5, w6, words67, scales67[:, slots(0)])
         words45 = gather_words(4, 2)
         expert(5, 7, w5, words45, scales5[:])
-        words03 = gather_words(0, 4)
-        words01, words23 = words03[:, slots(0, 2)], words03[:, slots(2, 2)]
+        words01 = gather_words(0, 2)
+        words23 = gather_words(2, 2)
 
         rounded04 = placed("rounded04", [P, 4, N, PACK], BF16)
         for i, raw in enumerate(raw4 + raw01):
@@ -193,16 +195,14 @@ def tile_moe_shr_lin_silu_kernel(tc, x_words, x_scales, w, b, gate, offs, out):
         nc.gpsimd.tensor_tensor(gated7[:], y7[:], gate7[:], MULT)
         round_on_scalar(rounded04, 3, raw23[1])
         nc.scalar.activation(window_s[:].indirect(slot_list(7 * C, C)), gated7[:], COPY)
-        gate56 = load_gate(5, 2, RAW01 - 1024)
-        gate04 = load_gate(0, 5, RAW01 + 3072)
         rounded2 = placed("rounded2", [P, 1, N, PACK], BF16, GATE7)
         round_on_vector(rounded2, 0, raw23[0])
         w4, w0, w1, w3 = quantize_w(rounded04, 0, 4, "4013", Y7)
         (w2,) = quantize_w(rounded2, 0, 1, "2")
 
-        ys = placed("ys", [P, SPLIT], F32)
+        ys = placed("ys", [P, SPLIT], F32, RAW23)
         acc_shared = bank("acc_shared01", 0)
-        sums(acc_shared[:], w8, words01, scales03[:, slots(0, 2)])
+        sums(acc_shared[:], w8, words01[:], scales03[:, slots(0, 2)])
         silu(ys[:, :BANK], acc_shared[:], E)
         acc_rest = bank("acc_shared2", 1)
         sums(acc_rest[:, :128], w8, words23[:, :128], scales03[:, BANK : BANK + 128])

@@ -26,7 +26,7 @@ LIST_COLUMN = 16
 BANK = 512
 ALIGN = 64
 FIRST_ROW = 112
-RAW67, RAW01, GATE7, Y7, RAW23 = 0, 4096, 8192, 10240, 12288
+RAW67, RAW2, RAW01 = 0, 4096, 8192
 SPLIT = 704
 STORE_WIDTHS = (256, 384, 384, 384, 384, 256)
 assert sum(STORE_WIDTHS) == T
@@ -137,8 +137,9 @@ def tile_moe_shr_lin_silu_kernel(tc, x_words, x_scales, w, b, gate, offs, out):
         nc.sync.dma_start(token_words[:, : T // 2], words_hbm[:, : T // 2])
         raw5 = load_w(5, 1)
         nc.sync.dma_start(token_words[:, T // 2 :], words_hbm[:, T // 2 :])
-        raw4 = load_w(4, 1)
-        raw01 = load_w(0, 2, RAW01)
+        raw34 = load_w(3, 2)
+        gate7 = load_gate(7, 1)
+        raw2 = load_w(2, 1, RAW2)
 
         picked = placed("picked", [P, 5 * C], U8)
         nc.vector.tensor_copy(picked[:], spread_scales[:].indirect(slot_list(0, 5 * C)))
@@ -147,10 +148,10 @@ def tile_moe_shr_lin_silu_kernel(tc, x_words, x_scales, w, b, gate, offs, out):
             nc.sync.dma_start(
                 scales03[r:P:QUADRANT, :].bitcast(I32), picked[FIRST_ROW + r : P : SCALE_ROWS, :].bitcast(I32)
             )
-        raw23 = load_w(2, 2, RAW23)
-        gate7 = load_gate(7, 1, GATE7)
-        gate04 = load_gate(0, 5)
+        raw01 = load_w(0, 2, RAW01)
+        gate34 = load_gate(3, 2)
         gate56 = load_gate(5, 2)
+        gate02 = load_gate(0, 3)
         scales5 = gather_scales(5, 1)
         rounded867 = placed("rounded867", [P, 3, N, PACK], BF16)
         for i, raw in enumerate(raw8 + raw67):
@@ -170,37 +171,38 @@ def tile_moe_shr_lin_silu_kernel(tc, x_words, x_scales, w, b, gate, offs, out):
         def expert(e, number, stationary, words, scales):
             acc = bank("acc%d" % e, number)
             sums(acc[:, :C], stationary, words[:, slots(e % 2)], scales)
-            silu(y7[:] if e == 7 else y[:, slots(e)], acc[:, :C], e)
+            silu(y[:, slots(e)], acc[:, :C], e)
 
         def product(first, count, gate_part):
             nc.vector.tensor_tensor(gated[:, slots(first, count)], y[:, slots(first, count)], gate_part, MULT)
 
-        y = placed("y", [P, 7 * C], F32)
-        y7 = placed("y7", [P, C], F32, Y7)
+        y = placed("y", [P, T], F32)
         gated = placed("gated", [P, T], F32)
-        for quarter in range(4):
+        for quarter in range(3):
             shared_tokens(quarter)
         words67 = gather_words(6, 2)
         expert(7, 4, w7, words67, scales67[:, slots(1)])
         expert(6, 5, w6, words67, scales67[:, slots(0)])
+        shared_tokens(3)
         words45 = gather_words(4, 2)
         expert(5, 7, w5, words45, scales5[:])
         words01 = gather_words(0, 2)
         words23 = gather_words(2, 2)
 
-        rounded04 = placed("rounded04", [P, 4, N, PACK], BF16)
-        for i, raw in enumerate(raw4 + raw01):
-            round_on_gpsimd(rounded04, i, raw)
-        gated7 = placed("gated7", [P, C], F32, RAW01 + 1024)
-        nc.gpsimd.tensor_tensor(gated7[:], y7[:], gate7[:], MULT)
-        round_on_scalar(rounded04, 3, raw23[1])
+        rounded14 = placed("rounded14", [P, 4, N, PACK], BF16)
+        round_on_gpsimd(rounded14, 3, raw34[1])
+        round_on_gpsimd(rounded14, 1, raw2[0])
+        gated7 = placed("gated7", [P, C], F32, RAW2)
+        nc.gpsimd.tensor_tensor(gated7[:], y[:, slots(7)], gate7[:], MULT)
+        round_on_gpsimd(rounded14, 0, raw01[1])
+        round_on_scalar(rounded14, 2, raw34[0])
         nc.scalar.activation(window_s[:].indirect(slot_list(7 * C, C)), gated7[:], COPY)
-        rounded2 = placed("rounded2", [P, 1, N, PACK], BF16, GATE7)
-        round_on_vector(rounded2, 0, raw23[0])
-        w4, w0, w1, w3 = quantize_w(rounded04, 0, 4, "4013", Y7)
-        (w2,) = quantize_w(rounded2, 0, 1, "2")
+        rounded0 = placed("rounded0", [P, 1, N, PACK], BF16)
+        round_on_vector(rounded0, 0, raw01[0])
+        w1, w2, w3, w4 = quantize_w(rounded14, 0, 4, "14")
+        (w0,) = quantize_w(rounded0, 0, 1, "0", RAW01)
 
-        ys = placed("ys", [P, SPLIT], F32, RAW23)
+        ys = placed("ys", [P, SPLIT], F32, RAW01 + 512)
         acc_shared = bank("acc_shared01", 0)
         sums(acc_shared[:], w8, words01[:], scales03[:, slots(0, 2)])
         silu(ys[:, :BANK], acc_shared[:], E)
@@ -208,17 +210,17 @@ def tile_moe_shr_lin_silu_kernel(tc, x_words, x_scales, w, b, gate, offs, out):
         sums(acc_rest[:, :128], w8, words23[:, :128], scales03[:, BANK : BANK + 128])
         sums(acc_rest[:, 128:192], w8, words23[:, 128:192], scales03[:, BANK + 128 : SPLIT])
         silu(ys[:, BANK:], acc_rest[:, : SPLIT - BANK], E)
-        expert(0, 2, w0, words01, scales03[:, slots(0)])
         expert(1, 3, w1, words01, scales03[:, slots(1)])
         expert(2, 4, w2, words23, scales03[:, slots(2)])
+        expert(0, 2, w0, words01, scales03[:, slots(0)])
         expert(3, 5, w3, words23, scales03[:, slots(3)])
 
         expert(4, 6, w4, words45, scales03[:, slots(4)])
 
         product(5, 1, gate56[:, slots(0)])
         nc.vector.tensor_tensor(window_s[:].indirect(slot_list(6 * C, C)), y[:, slots(6)], gate56[:, slots(1)], MULT)
-        product(0, 3, gate04[:, slots(0, 3)])
-        product(3, 2, gate04[:, slots(3, 2)])
+        product(0, 3, gate02[:])
+        product(3, 2, gate34[:])
         scalar_scatter(5 * C, C)
         nc.vector.tensor_tensor(window_v[:].indirect(slot_list(0, SPLIT)), gated[:, :SPLIT], ys[:], ADD)
         scalar_scatter(SPLIT, 288)

@@ -26,7 +26,7 @@ LIST_COLUMN = 16
 BANK = 512
 ALIGN = 64
 FIRST_ROW = 112
-RAW67, RAW2, RAW01 = 0, 4096, 8192
+RAW0, RAW1 = 0, 2048
 SPLIT = 704
 STORE_WIDTHS = (256, 384, 384, 384, 384, 256)
 assert sum(STORE_WIDTHS) == T
@@ -65,9 +65,6 @@ def tile_moe_shr_lin_silu_kernel(tc, x_words, x_scales, w, b, gate, offs, out):
                 rounded[:, i].rearrange("p (c i) j -> p c j i", i=RUN),
                 raw.rearrange("p j (c i) -> p c j i", i=RUN),
             )
-
-        def round_on_vector(rounded, i, raw):
-            nc.vector.tensor_copy(rounded[:, i], raw.rearrange("p j n -> p n j"))
 
         def round_on_gpsimd(rounded, i, raw):
             nc.gpsimd.tensor_scalar(rounded[:, i], raw.rearrange("p j n -> p n j"), 1.0, 0.0, MULT, ADD)
@@ -131,15 +128,15 @@ def tile_moe_shr_lin_silu_kernel(tc, x_words, x_scales, w, b, gate, offs, out):
         nc.gpsimd.memset(window_s[:], 0.0)
         window_v = placed("window_v", [P, T], F32)
 
-        raw67 = load_w(6, 2, RAW67)
+        raw57 = load_w(5, 3)
         token_words = placed("token_words", [P, T], I32)
         words_hbm = x_words[0].rearrange("p t r -> p (t r)").bitcast(I32)
         nc.sync.dma_start(token_words[:, : T // 2], words_hbm[:, : T // 2])
-        raw5 = load_w(5, 1)
         nc.sync.dma_start(token_words[:, T // 2 :], words_hbm[:, T // 2 :])
+        raw2 = load_w(2, 1)
         raw34 = load_w(3, 2)
+        raw0 = load_w(0, 1, RAW0)
         gate7 = load_gate(7, 1)
-        raw2 = load_w(2, 1, RAW2)
 
         picked = placed("picked", [P, 5 * C], U8)
         nc.vector.tensor_copy(picked[:], spread_scales[:].indirect(slot_list(0, 5 * C)))
@@ -148,19 +145,18 @@ def tile_moe_shr_lin_silu_kernel(tc, x_words, x_scales, w, b, gate, offs, out):
             nc.sync.dma_start(
                 scales03[r:P:QUADRANT, :].bitcast(I32), picked[FIRST_ROW + r : P : SCALE_ROWS, :].bitcast(I32)
             )
-        raw01 = load_w(0, 2, RAW01)
+        raw1 = load_w(1, 1, RAW1)
         gate34 = load_gate(3, 2)
         gate56 = load_gate(5, 2)
         gate02 = load_gate(0, 3)
-        scales5 = gather_scales(5, 1)
-        rounded867 = placed("rounded867", [P, 3, N, PACK], BF16)
-        for i, raw in enumerate(raw8 + raw67):
-            round_on_scalar(rounded867, i, raw)
-        w8, w6, w7 = quantize_w(rounded867, 0, 3, "867")
-        scales67 = gather_scales(6, 2, RAW67)
-        rounded5 = placed("rounded5", [P, 1, N, PACK], BF16)
-        round_on_scalar(rounded5, 0, raw5[0])
-        (w5,) = quantize_w(rounded5, 0, 1, "5")
+        rounded8 = placed("rounded8", [P, 1, N, PACK], BF16)
+        round_on_scalar(rounded8, 0, raw8[0])
+        (w8,) = quantize_w(rounded8, 0, 1, "8")
+        scales57 = gather_scales(5, 3)
+        rounded57 = placed("rounded57", [P, 3, N, PACK], BF16)
+        for i, raw in enumerate(raw57):
+            round_on_scalar(rounded57, i, raw)
+        w5, w6, w7 = quantize_w(rounded57, 0, 3, "57")
 
         def shared_tokens(quarter):
             cols = slice(quarter * BANK, (quarter + 1) * BANK)
@@ -178,31 +174,30 @@ def tile_moe_shr_lin_silu_kernel(tc, x_words, x_scales, w, b, gate, offs, out):
 
         y = placed("y", [P, T], F32)
         gated = placed("gated", [P, T], F32)
-        for quarter in range(3):
+        for quarter in range(4):
             shared_tokens(quarter)
         words67 = gather_words(6, 2)
-        expert(7, 4, w7, words67, scales67[:, slots(1)])
-        expert(6, 5, w6, words67, scales67[:, slots(0)])
-        shared_tokens(3)
+        expert(7, 4, w7, words67, scales57[:, slots(2)])
+        expert(6, 5, w6, words67, scales57[:, slots(1)])
+        rounded14 = placed("rounded14", [P, 4, N, PACK], BF16)
+        round_on_scalar(rounded14, 2, raw34[0])
         words45 = gather_words(4, 2)
-        expert(5, 7, w5, words45, scales5[:])
+        expert(5, 7, w5, words45, scales57[:, slots(0)])
         words01 = gather_words(0, 2)
         words23 = gather_words(2, 2)
 
-        rounded14 = placed("rounded14", [P, 4, N, PACK], BF16)
-        round_on_gpsimd(rounded14, 3, raw34[1])
         round_on_gpsimd(rounded14, 1, raw2[0])
-        gated7 = placed("gated7", [P, C], F32, RAW2)
-        nc.gpsimd.tensor_tensor(gated7[:], y[:, slots(7)], gate7[:], MULT)
-        round_on_gpsimd(rounded14, 0, raw01[1])
-        round_on_scalar(rounded14, 2, raw34[0])
-        nc.scalar.activation(window_s[:].indirect(slot_list(7 * C, C)), gated7[:], COPY)
         rounded0 = placed("rounded0", [P, 1, N, PACK], BF16)
-        round_on_vector(rounded0, 0, raw01[0])
+        round_on_gpsimd(rounded0, 0, raw0[0])
+        gated7 = placed("gated7", [P, C], F32, RAW0)
+        nc.gpsimd.tensor_tensor(gated7[:], y[:, slots(7)], gate7[:], MULT)
+        round_on_gpsimd(rounded14, 0, raw1[0])
+        round_on_scalar(rounded14, 3, raw34[1])
+        nc.scalar.activation(window_s[:].indirect(slot_list(7 * C, C)), gated7[:], COPY)
         w1, w2, w3, w4 = quantize_w(rounded14, 0, 4, "14")
-        (w0,) = quantize_w(rounded0, 0, 1, "0", RAW01)
+        (w0,) = quantize_w(rounded0, 0, 1, "0", RAW1)
 
-        ys = placed("ys", [P, SPLIT], F32, RAW01 + 512)
+        ys = placed("ys", [P, SPLIT], F32, RAW1 + 512)
         acc_shared = bank("acc_shared01", 0)
         sums(acc_shared[:], w8, words01[:], scales03[:, slots(0, 2)])
         silu(ys[:, :BANK], acc_shared[:], E)

@@ -26,7 +26,7 @@ LIST_COLUMN = 16
 BANK = 512
 ALIGN = 64
 FIRST_ROW = 112
-RAW0, RAW1 = 0, 2048
+RAW34, RAW1 = 0, 4096
 SPLIT = 704
 STORE_WIDTHS = (256, 384, 384, 384, 384, 256)
 assert sum(STORE_WIDTHS) == T
@@ -134,8 +134,8 @@ def tile_moe_shr_lin_silu_kernel(tc, x_words, x_scales, w, b, gate, offs, out):
         nc.sync.dma_start(token_words[:, : T // 2], words_hbm[:, : T // 2])
         nc.sync.dma_start(token_words[:, T // 2 :], words_hbm[:, T // 2 :])
         raw2 = load_w(2, 1)
-        raw34 = load_w(3, 2)
-        raw0 = load_w(0, 1, RAW0)
+        raw34 = load_w(3, 2, RAW34)
+        raw0 = load_w(0, 1)
         gate7 = load_gate(7, 1)
 
         picked = placed("picked", [P, 5 * C], U8)
@@ -179,20 +179,23 @@ def tile_moe_shr_lin_silu_kernel(tc, x_words, x_scales, w, b, gate, offs, out):
         words67 = gather_words(6, 2)
         expert(7, 4, w7, words67, scales57[:, slots(2)])
         expert(6, 5, w6, words67, scales57[:, slots(1)])
-        rounded14 = placed("rounded14", [P, 4, N, PACK], BF16)
-        round_on_scalar(rounded14, 2, raw34[0])
+        ys6 = placed("ys6", [P, C], F32)
+        acc6 = bank("acc_shared6", 6)
+        sums(acc6[:, :C], w8, words67[:, slots(0)], scales57[:, slots(1)])
+        silu(ys6[:], acc6[:, :C], E)
+        rounded0 = placed("rounded0", [P, 1, N, PACK], BF16)
+        round_on_scalar(rounded0, 0, raw0[0])
         words45 = gather_words(4, 2)
         expert(5, 7, w5, words45, scales57[:, slots(0)])
         words01 = gather_words(0, 2)
         words23 = gather_words(2, 2)
 
-        round_on_gpsimd(rounded14, 1, raw2[0])
-        rounded0 = placed("rounded0", [P, 1, N, PACK], BF16)
-        round_on_gpsimd(rounded0, 0, raw0[0])
-        gated7 = placed("gated7", [P, C], F32, RAW0)
+        rounded14 = placed("rounded14", [P, 4, N, PACK], BF16)
+        for i, raw in enumerate(raw2 + raw34):
+            round_on_gpsimd(rounded14, 1 + i, raw)
+        gated7 = placed("gated7", [P, C], F32, RAW34)
         nc.gpsimd.tensor_tensor(gated7[:], y[:, slots(7)], gate7[:], MULT)
         round_on_gpsimd(rounded14, 0, raw1[0])
-        round_on_scalar(rounded14, 3, raw34[1])
         nc.scalar.activation(window_s[:].indirect(slot_list(7 * C, C)), gated7[:], COPY)
         w1, w2, w3, w4 = quantize_w(rounded14, 0, 4, "14")
         (w0,) = quantize_w(rounded0, 0, 1, "0", RAW1)
@@ -212,8 +215,9 @@ def tile_moe_shr_lin_silu_kernel(tc, x_words, x_scales, w, b, gate, offs, out):
 
         expert(4, 6, w4, words45, scales03[:, slots(4)])
 
+        product(6, 1, gate56[:, slots(1)])
         product(5, 1, gate56[:, slots(0)])
-        nc.vector.tensor_tensor(window_s[:].indirect(slot_list(6 * C, C)), y[:, slots(6)], gate56[:, slots(1)], MULT)
+        nc.vector.tensor_tensor(window_v[:].indirect(slot_list(6 * C, C)), gated[:, slots(6)], ys6[:], ADD)
         product(0, 3, gate02[:])
         product(3, 2, gate34[:])
         scalar_scatter(5 * C, C)

@@ -26,8 +26,8 @@ LIST_COLUMN = 16
 BANK = 512
 ALIGN = 64
 FIRST_ROW = 112
-RAW34, RAW1 = 0, 4096
-SPLIT = 704
+RAW4, RAW1 = 0, 2048
+SPLIT = 672
 STORE_WIDTHS = (256, 384, 384, 384, 384, 256)
 assert sum(STORE_WIDTHS) == T
 
@@ -134,7 +134,7 @@ def tile_moe_shr_lin_silu_kernel(tc, x_words, x_scales, w, b, gate, offs, out):
         nc.sync.dma_start(token_words[:, : T // 2], words_hbm[:, : T // 2])
         nc.sync.dma_start(token_words[:, T // 2 :], words_hbm[:, T // 2 :])
         raw2 = load_w(2, 1)
-        raw34 = load_w(3, 2, RAW34)
+        raw3 = load_w(3, 1)
         raw0 = load_w(0, 1)
         gate7 = load_gate(7, 1)
 
@@ -145,10 +145,11 @@ def tile_moe_shr_lin_silu_kernel(tc, x_words, x_scales, w, b, gate, offs, out):
             nc.sync.dma_start(
                 scales03[r:P:QUADRANT, :].bitcast(I32), picked[FIRST_ROW + r : P : SCALE_ROWS, :].bitcast(I32)
             )
+        raw4 = load_w(4, 1, RAW4)
         raw1 = load_w(1, 1, RAW1)
-        gate34 = load_gate(3, 2)
-        gate56 = load_gate(5, 2)
         gate02 = load_gate(0, 3)
+        gate56 = load_gate(5, 2)
+        gate34 = load_gate(3, 2)
         rounded8 = placed("rounded8", [P, 1, N, PACK], BF16)
         round_on_scalar(rounded8, 0, raw8[0])
         (w8,) = quantize_w(rounded8, 0, 1, "8")
@@ -183,22 +184,22 @@ def tile_moe_shr_lin_silu_kernel(tc, x_words, x_scales, w, b, gate, offs, out):
         acc6 = bank("acc_shared6", 6)
         sums(acc6[:, :C], w8, words67[:, slots(0)], scales57[:, slots(1)])
         silu(ys6[:], acc6[:, :C], E)
-        rounded0 = placed("rounded0", [P, 1, N, PACK], BF16)
-        round_on_scalar(rounded0, 0, raw0[0])
+        rounded_late = placed("rounded_late", [P, 4, N, PACK], BF16)
+        round_on_scalar(rounded_late, 0, raw0[0])
         words45 = gather_words(4, 2)
         expert(5, 7, w5, words45, scales57[:, slots(0)])
         words01 = gather_words(0, 2)
         words23 = gather_words(2, 2)
 
-        rounded14 = placed("rounded14", [P, 4, N, PACK], BF16)
-        for i, raw in enumerate(raw2 + raw34):
-            round_on_gpsimd(rounded14, 1 + i, raw)
-        gated7 = placed("gated7", [P, C], F32, RAW34)
-        nc.gpsimd.tensor_tensor(gated7[:], y[:, slots(7)], gate7[:], MULT)
-        round_on_gpsimd(rounded14, 0, raw1[0])
-        nc.scalar.activation(window_s[:].indirect(slot_list(7 * C, C)), gated7[:], COPY)
-        w1, w2, w3, w4 = quantize_w(rounded14, 0, 4, "14")
-        (w0,) = quantize_w(rounded0, 0, 1, "0", RAW1)
+        for i, raw in enumerate(raw2 + raw3):
+            round_on_gpsimd(rounded_late, 1 + i, raw)
+        nc.gpsimd.tensor_tensor(gated[:, slots(7)], y[:, slots(7)], gate7[:], MULT)
+        round_on_gpsimd(rounded_late, 3, raw4[0])
+        scalar_scatter(7 * C, C)
+        rounded1 = placed("rounded1", [P, 1, N, PACK], BF16, RAW4)
+        nc.vector.tensor_copy(rounded1[:, 0], raw1[0].rearrange("p j n -> p n j"))
+        w0, w2, w3, w4 = quantize_w(rounded_late, 0, 4, "late")
+        (w1,) = quantize_w(rounded1, 0, 1, "1")
 
         ys = placed("ys", [P, SPLIT], F32, RAW1 + 512)
         acc_shared = bank("acc_shared01", 0)
@@ -206,24 +207,23 @@ def tile_moe_shr_lin_silu_kernel(tc, x_words, x_scales, w, b, gate, offs, out):
         silu(ys[:, :BANK], acc_shared[:], E)
         acc_rest = bank("acc_shared2", 1)
         sums(acc_rest[:, :128], w8, words23[:, :128], scales03[:, BANK : BANK + 128])
-        sums(acc_rest[:, 128:192], w8, words23[:, 128:192], scales03[:, BANK + 128 : SPLIT])
+        sums(acc_rest[:, 128:192], w8, words23[:, 128:192], scales03[:, BANK + 128 : BANK + 192])
         silu(ys[:, BANK:], acc_rest[:, : SPLIT - BANK], E)
-        expert(1, 3, w1, words01, scales03[:, slots(1)])
-        expert(2, 4, w2, words23, scales03[:, slots(2)])
-        expert(0, 2, w0, words01, scales03[:, slots(0)])
         expert(3, 5, w3, words23, scales03[:, slots(3)])
-
         expert(4, 6, w4, words45, scales03[:, slots(4)])
+        expert(0, 2, w0, words01, scales03[:, slots(0)])
+        expert(2, 4, w2, words23, scales03[:, slots(2)])
+        expert(1, 3, w1, words01, scales03[:, slots(1)])
 
         product(6, 1, gate56[:, slots(1)])
         product(5, 1, gate56[:, slots(0)])
         nc.vector.tensor_tensor(window_v[:].indirect(slot_list(6 * C, C)), gated[:, slots(6)], ys6[:], ADD)
-        product(0, 3, gate02[:])
         product(3, 2, gate34[:])
+        product(0, 3, gate02[:])
         scalar_scatter(5 * C, C)
         nc.vector.tensor_tensor(window_v[:].indirect(slot_list(0, SPLIT)), gated[:, :SPLIT], ys[:], ADD)
+        scalar_scatter(SPLIT + 288, 320)
         scalar_scatter(SPLIT, 288)
-        scalar_scatter(SPLIT + 288, 288)
 
         total = placed("total", [P, T], F32)
         first = 0

@@ -27,7 +27,7 @@ BANK = 512
 ALIGN = 64
 FIRST_ROW = 112
 RAW4, RAW1 = 0, 2048
-SPLIT = 672
+SPLIT = 704
 STORE_WIDTHS = (256, 384, 384, 384, 384, 256)
 assert sum(STORE_WIDTHS) == T
 
@@ -180,10 +180,6 @@ def tile_moe_shr_lin_silu_kernel(tc, x_words, x_scales, w, b, gate, offs, out):
         words67 = gather_words(6, 2)
         expert(7, 4, w7, words67, scales57[:, slots(2)])
         expert(6, 5, w6, words67, scales57[:, slots(1)])
-        ys6 = placed("ys6", [P, C], F32)
-        acc6 = bank("acc_shared6", 6)
-        sums(acc6[:, :C], w8, words67[:, slots(0)], scales57[:, slots(1)])
-        silu(ys6[:], acc6[:, :C], E)
         rounded_late = placed("rounded_late", [P, 4, N, PACK], BF16)
         round_on_scalar(rounded_late, 0, raw0[0])
         words45 = gather_words(4, 2)
@@ -215,14 +211,13 @@ def tile_moe_shr_lin_silu_kernel(tc, x_words, x_scales, w, b, gate, offs, out):
         expert(2, 4, w2, words23, scales03[:, slots(2)])
         expert(1, 3, w1, words01, scales03[:, slots(1)])
 
-        product(6, 1, gate56[:, slots(1)])
         product(5, 1, gate56[:, slots(0)])
-        nc.vector.tensor_tensor(window_v[:].indirect(slot_list(6 * C, C)), gated[:, slots(6)], ys6[:], ADD)
+        nc.vector.tensor_tensor(window_s[:].indirect(slot_list(6 * C, C)), y[:, slots(6)], gate56[:, slots(1)], MULT)
         product(3, 2, gate34[:])
         product(0, 3, gate02[:])
         scalar_scatter(5 * C, C)
         nc.vector.tensor_tensor(window_v[:].indirect(slot_list(0, SPLIT)), gated[:, :SPLIT], ys[:], ADD)
-        scalar_scatter(SPLIT + 288, 320)
+        scalar_scatter(SPLIT + 288, 288)
         scalar_scatter(SPLIT, 288)
 
         total = placed("total", [P, T], F32)

@@ -26,9 +26,9 @@ LIST_COLUMN = 16
 BANK = 512
 ALIGN = 64
 FIRST_ROW = 112
-RAW4, RAW1 = 0, 2048
+RAW4 = 0
 SPLIT = 704
-STORE_WIDTHS = (256, 384, 384, 384, 384, 256)
+STORE_WIDTHS = (256, 256, 256, 512, 512, 256)
 assert sum(STORE_WIDTHS) == T
 
 
@@ -134,8 +134,8 @@ def tile_moe_shr_lin_silu_kernel(tc, x_words, x_scales, w, b, gate, offs, out):
         nc.sync.dma_start(token_words[:, : T // 2], words_hbm[:, : T // 2])
         nc.sync.dma_start(token_words[:, T // 2 :], words_hbm[:, T // 2 :])
         raw2 = load_w(2, 1)
+        raw01 = load_w(0, 2)
         raw3 = load_w(3, 1)
-        raw0 = load_w(0, 1)
         gate7 = load_gate(7, 1)
 
         picked = placed("picked", [P, 5 * C], U8)
@@ -146,7 +146,6 @@ def tile_moe_shr_lin_silu_kernel(tc, x_words, x_scales, w, b, gate, offs, out):
                 scales03[r:P:QUADRANT, :].bitcast(I32), picked[FIRST_ROW + r : P : SCALE_ROWS, :].bitcast(I32)
             )
         raw4 = load_w(4, 1, RAW4)
-        raw1 = load_w(1, 1, RAW1)
         gate02 = load_gate(0, 3)
         gate56 = load_gate(5, 2)
         gate34 = load_gate(3, 2)
@@ -181,7 +180,7 @@ def tile_moe_shr_lin_silu_kernel(tc, x_words, x_scales, w, b, gate, offs, out):
         expert(7, 4, w7, words67, scales57[:, slots(2)])
         expert(6, 5, w6, words67, scales57[:, slots(1)])
         rounded_late = placed("rounded_late", [P, 4, N, PACK], BF16)
-        round_on_scalar(rounded_late, 0, raw0[0])
+        round_on_scalar(rounded_late, 0, raw01[0])
         words45 = gather_words(4, 2)
         expert(5, 7, w5, words45, scales57[:, slots(0)])
         words01 = gather_words(0, 2)
@@ -191,13 +190,13 @@ def tile_moe_shr_lin_silu_kernel(tc, x_words, x_scales, w, b, gate, offs, out):
             round_on_gpsimd(rounded_late, 1 + i, raw)
         nc.gpsimd.tensor_tensor(gated[:, slots(7)], y[:, slots(7)], gate7[:], MULT)
         round_on_gpsimd(rounded_late, 3, raw4[0])
+        rounded1 = placed("rounded1", [P, 1, N, PACK], BF16)
+        round_on_scalar(rounded1, 0, raw01[1])
         scalar_scatter(7 * C, C)
-        rounded1 = placed("rounded1", [P, 1, N, PACK], BF16, RAW4)
-        nc.vector.tensor_copy(rounded1[:, 0], raw1[0].rearrange("p j n -> p n j"))
         w0, w2, w3, w4 = quantize_w(rounded_late, 0, 4, "late")
-        (w1,) = quantize_w(rounded1, 0, 1, "1")
+        (w1,) = quantize_w(rounded1, 0, 1, "1", RAW4)
 
-        ys = placed("ys", [P, SPLIT], F32, RAW1 + 512)
+        ys = placed("ys", [P, SPLIT], F32, RAW4 + 512)
         acc_shared = bank("acc_shared01", 0)
         sums(acc_shared[:], w8, words01[:], scales03[:, slots(0, 2)])
         silu(ys[:, :BANK], acc_shared[:], E)

@@ -26,8 +26,10 @@ LIST_COLUMN = 16
 BANK = 512
 ALIGN = 64
 FIRST_ROW = 112
-RAW4 = 0
-SPLIT = 704
+RAW4 = 1024
+GATE7 = 8192
+RAW0 = 12288
+SPLIT = 672
 STORE_WIDTHS = (256, 256, 256, 512, 512, 256)
 assert sum(STORE_WIDTHS) == T
 
@@ -112,7 +114,7 @@ def tile_moe_shr_lin_silu_kernel(tc, x_words, x_scales, w, b, gate, offs, out):
         token_scales = placed("token_scales", [P, T], U8)
         nc.gpsimd.memset(token_scales[:].bitcast(I32), 0)
         spread_scales = placed("spread_scales", [P, T], U8)
-        nc.sync.dma_start(spread_scales[FIRST_ROW:P, :].bitcast(I32), x_scales[0].bitcast(I32))
+        nc.scalar.dma_start(spread_scales[FIRST_ROW:P, :].bitcast(I32), x_scales[0].bitcast(I32))
         nc.vector.memset(spread_scales[0:FIRST_ROW, :].bitcast(I32), 0)
         offsets = sbuf.tile([P, E * C // LIST_COLUMN], U16, name="offsets")
         nc.sync.dma_start(offsets[:], offs)
@@ -122,6 +124,8 @@ def tile_moe_shr_lin_silu_kernel(tc, x_words, x_scales, w, b, gate, offs, out):
         warm_up = sbuf.tile([P, 2], F32, name="warm_up")
         nc.vector.memset(warm_up[:, 0:1], 0.0)
         nc.scalar.activation(warm_up[:, 1:2], warm_up[:, 0:1], SILU)
+        one = sbuf.tile([P, 1], F32, name="one")
+        nc.vector.memset(one[:], 1.0)
         bias = sbuf.tile([P, E + 1], F32, name="bias")
         nc.gpsimd.dma_start(bias[:], b)
         window_s = placed("window_s", [P, T], F32)
@@ -134,9 +138,10 @@ def tile_moe_shr_lin_silu_kernel(tc, x_words, x_scales, w, b, gate, offs, out):
         nc.sync.dma_start(token_words[:, : T // 2], words_hbm[:, : T // 2])
         nc.sync.dma_start(token_words[:, T // 2 :], words_hbm[:, T // 2 :])
         raw2 = load_w(2, 1)
-        raw01 = load_w(0, 2)
         raw3 = load_w(3, 1)
-        gate7 = load_gate(7, 1)
+        raw01 = load_w(0, 2, RAW0)
+        gate7 = load_gate(7, 1, GATE7)
+        raw4 = load_w(4, 1, RAW4)
 
         picked = placed("picked", [P, 5 * C], U8)
         nc.vector.tensor_copy(picked[:], spread_scales[:].indirect(slot_list(0, 5 * C)))
@@ -145,7 +150,6 @@ def tile_moe_shr_lin_silu_kernel(tc, x_words, x_scales, w, b, gate, offs, out):
             nc.sync.dma_start(
                 scales03[r:P:QUADRANT, :].bitcast(I32), picked[FIRST_ROW + r : P : SCALE_ROWS, :].bitcast(I32)
             )
-        raw4 = load_w(4, 1, RAW4)
         gate02 = load_gate(0, 3)
         gate56 = load_gate(5, 2)
         gate34 = load_gate(3, 2)
@@ -164,10 +168,10 @@ def tile_moe_shr_lin_silu_kernel(tc, x_words, x_scales, w, b, gate, offs, out):
             sums(acc[:], w8, token_words[:, cols].bitcast(U32), token_scales[:, cols])
             silu(window_v[:, cols], acc[:], E)
 
-        def expert(e, number, stationary, words, scales):
+        def expert(e, number, stationary, words, scales, result=None):
             acc = bank("acc%d" % e, number)
             sums(acc[:, :C], stationary, words[:, slots(e % 2)], scales)
-            silu(y[:, slots(e)], acc[:, :C], e)
+            silu(y[:, slots(e)] if result is None else result, acc[:, :C], e)
 
         def product(first, count, gate_part):
             nc.vector.tensor_tensor(gated[:, slots(first, count)], y[:, slots(first, count)], gate_part, MULT)
@@ -181,22 +185,23 @@ def tile_moe_shr_lin_silu_kernel(tc, x_words, x_scales, w, b, gate, offs, out):
         expert(6, 5, w6, words67, scales57[:, slots(1)])
         rounded_late = placed("rounded_late", [P, 4, N, PACK], BF16)
         round_on_scalar(rounded_late, 0, raw01[0])
+        round_on_scalar(rounded_late, 1, raw01[1])
         words45 = gather_words(4, 2)
-        expert(5, 7, w5, words45, scales57[:, slots(0)])
+        y5 = placed("y5", [P, C], F32, RAW0)
+        expert(5, 7, w5, words45, scales57[:, slots(0)], y5[:])
         words01 = gather_words(0, 2)
         words23 = gather_words(2, 2)
 
         for i, raw in enumerate(raw2 + raw3):
-            round_on_gpsimd(rounded_late, 1 + i, raw)
+            round_on_gpsimd(rounded_late, 2 + i, raw)
         nc.gpsimd.tensor_tensor(gated[:, slots(7)], y[:, slots(7)], gate7[:], MULT)
-        round_on_gpsimd(rounded_late, 3, raw4[0])
-        rounded1 = placed("rounded1", [P, 1, N, PACK], BF16)
-        round_on_scalar(rounded1, 0, raw01[1])
+        rounded4 = placed("rounded4", [P, 1, N, PACK], BF16, GATE7)
+        round_on_gpsimd(rounded4, 0, raw4[0])
         scalar_scatter(7 * C, C)
-        w0, w2, w3, w4 = quantize_w(rounded_late, 0, 4, "late")
-        (w1,) = quantize_w(rounded1, 0, 1, "1", RAW4)
+        w0, w1, w2, w3 = quantize_w(rounded_late, 0, 4, "late", RAW4 - 1024)
+        (w4,) = quantize_w(rounded4, 0, 1, "4")
 
-        ys = placed("ys", [P, SPLIT], F32, RAW4 + 512)
+        ys = placed("ys", [P, SPLIT], F32, RAW4 + 1024)
         acc_shared = bank("acc_shared01", 0)
         sums(acc_shared[:], w8, words01[:], scales03[:, slots(0, 2)])
         silu(ys[:, :BANK], acc_shared[:], E)
@@ -204,20 +209,21 @@ def tile_moe_shr_lin_silu_kernel(tc, x_words, x_scales, w, b, gate, offs, out):
         sums(acc_rest[:, :128], w8, words23[:, :128], scales03[:, BANK : BANK + 128])
         sums(acc_rest[:, 128:192], w8, words23[:, 128:192], scales03[:, BANK + 128 : BANK + 192])
         silu(ys[:, BANK:], acc_rest[:, : SPLIT - BANK], E)
+        expert(0, 2, w0, words01, scales03[:, slots(0)])
+        expert(1, 3, w1, words01, scales03[:, slots(1)])
+        expert(2, 4, w2, words23, scales03[:, slots(2)])
         expert(3, 5, w3, words23, scales03[:, slots(3)])
         expert(4, 6, w4, words45, scales03[:, slots(4)])
-        expert(0, 2, w0, words01, scales03[:, slots(0)])
-        expert(2, 4, w2, words23, scales03[:, slots(2)])
-        expert(1, 3, w1, words01, scales03[:, slots(1)])
 
-        product(5, 1, gate56[:, slots(0)])
+        nc.vector.tensor_tensor(gated[:, slots(5)], y5[:], gate56[:, slots(0)], MULT)
         nc.vector.tensor_tensor(window_s[:].indirect(slot_list(6 * C, C)), y[:, slots(6)], gate56[:, slots(1)], MULT)
-        product(3, 2, gate34[:])
         product(0, 3, gate02[:])
+        product(3, 2, gate34[:])
         scalar_scatter(5 * C, C)
         nc.vector.tensor_tensor(window_v[:].indirect(slot_list(0, SPLIT)), gated[:, :SPLIT], ys[:], ADD)
-        scalar_scatter(SPLIT + 288, 288)
-        scalar_scatter(SPLIT, 288)
+        nc.scalar.activation(
+            window_s[:].indirect(slot_list(SPLIT, 5 * C - SPLIT)), gated[:, SPLIT : 5 * C], COPY, scale=one[:]
+        )
 
         total = placed("total", [P, T], F32)
         first = 0

@@ -26,10 +26,9 @@ LIST_COLUMN = 16
 BANK = 512
 ALIGN = 64
 FIRST_ROW = 112
-RAW4 = 1024
+RAW0 = 1024
 GATE7 = 8192
-RAW0 = 12288
-SPLIT = 672
+SPLIT = 608
 STORE_WIDTHS = (256, 256, 256, 512, 512, 256)
 assert sum(STORE_WIDTHS) == T
 
@@ -137,26 +136,26 @@ def tile_moe_shr_lin_silu_kernel(tc, x_words, x_scales, w, b, gate, offs, out):
         words_hbm = x_words[0].rearrange("p t r -> p (t r)").bitcast(I32)
         nc.sync.dma_start(token_words[:, : T // 2], words_hbm[:, : T // 2])
         nc.sync.dma_start(token_words[:, T // 2 :], words_hbm[:, T // 2 :])
-        raw2 = load_w(2, 1)
+        raw4 = load_w(4, 1)
         raw3 = load_w(3, 1)
-        raw01 = load_w(0, 2, RAW0)
+        raw12 = load_w(1, 2)
         gate7 = load_gate(7, 1, GATE7)
-        raw4 = load_w(4, 1, RAW4)
 
-        picked = placed("picked", [P, 5 * C], U8)
-        nc.vector.tensor_copy(picked[:], spread_scales[:].indirect(slot_list(0, 5 * C)))
-        scales03 = placed("slot_scales0", [P, 5 * C], U8)
+        picked = placed("picked", [P, 6 * C], U8)
+        nc.vector.tensor_copy(picked[:], spread_scales[:].indirect(slot_list(0, 6 * C)))
+        scales05 = placed("slot_scales0", [P, 6 * C], U8)
         for r in range(SCALE_ROWS):
             nc.sync.dma_start(
-                scales03[r:P:QUADRANT, :].bitcast(I32), picked[FIRST_ROW + r : P : SCALE_ROWS, :].bitcast(I32)
+                scales05[r:P:QUADRANT, :].bitcast(I32), picked[FIRST_ROW + r : P : SCALE_ROWS, :].bitcast(I32)
             )
-        gate02 = load_gate(0, 3)
+        raw0 = load_w(0, 1, RAW0)
+        gate24 = load_gate(2, 3)
         gate56 = load_gate(5, 2)
-        gate34 = load_gate(3, 2)
+        gate01 = load_gate(0, 2)
         rounded8 = placed("rounded8", [P, 1, N, PACK], BF16)
         round_on_scalar(rounded8, 0, raw8[0])
         (w8,) = quantize_w(rounded8, 0, 1, "8")
-        scales57 = gather_scales(5, 3)
+        scales67 = gather_scales(6, 2)
         rounded57 = placed("rounded57", [P, 3, N, PACK], BF16)
         for i, raw in enumerate(raw57):
             round_on_scalar(rounded57, i, raw)
@@ -170,7 +169,7 @@ def tile_moe_shr_lin_silu_kernel(tc, x_words, x_scales, w, b, gate, offs, out):
 
         def expert(e, number, stationary, words, scales, result=None):
             acc = bank("acc%d" % e, number)
-            sums(acc[:, :C], stationary, words[:, slots(e % 2)], scales)
+            sums(acc[:, :C], stationary, words, scales)
             silu(y[:, slots(e)] if result is None else result, acc[:, :C], e)
 
         def product(first, count, gate_part):
@@ -181,49 +180,48 @@ def tile_moe_shr_lin_silu_kernel(tc, x_words, x_scales, w, b, gate, offs, out):
         for quarter in range(4):
             shared_tokens(quarter)
         words67 = gather_words(6, 2)
-        expert(7, 4, w7, words67, scales57[:, slots(2)])
-        expert(6, 5, w6, words67, scales57[:, slots(1)])
-        rounded_late = placed("rounded_late", [P, 4, N, PACK], BF16)
-        round_on_scalar(rounded_late, 0, raw01[0])
-        round_on_scalar(rounded_late, 1, raw01[1])
-        words45 = gather_words(4, 2)
-        y5 = placed("y5", [P, C], F32, RAW0)
-        expert(5, 7, w5, words45, scales57[:, slots(0)], y5[:])
-        words01 = gather_words(0, 2)
-        words23 = gather_words(2, 2)
+        expert(7, 4, w7, words67[:, slots(1)], scales67[:, slots(1)])
+        expert(6, 5, w6, words67[:, slots(0)], scales67[:, slots(0)])
+        rounded14 = placed("rounded14", [P, 4, N, PACK], BF16)
+        round_on_scalar(rounded14, 0, raw12[0])
+        round_on_scalar(rounded14, 1, raw12[1])
+        words35 = gather_words(3, 3)
+        words02 = gather_words(0, 3)
 
-        for i, raw in enumerate(raw2 + raw3):
-            round_on_gpsimd(rounded_late, 2 + i, raw)
+        round_on_gpsimd(rounded14, 3, raw4[0])
+        round_on_gpsimd(rounded14, 2, raw3[0])
         nc.gpsimd.tensor_tensor(gated[:, slots(7)], y[:, slots(7)], gate7[:], MULT)
-        rounded4 = placed("rounded4", [P, 1, N, PACK], BF16, GATE7)
-        round_on_gpsimd(rounded4, 0, raw4[0])
+        rounded0 = placed("rounded0", [P, 1, N, PACK], BF16, GATE7 - 512)
+        round_on_gpsimd(rounded0, 0, raw0[0])
         scalar_scatter(7 * C, C)
-        w0, w1, w2, w3 = quantize_w(rounded_late, 0, 4, "late", RAW4 - 1024)
-        (w4,) = quantize_w(rounded4, 0, 1, "4")
+        y5 = placed("y5", [P, C], F32, GATE7 + 512)
+        expert(5, 7, w5, words35[:, slots(2)], scales05[:, slots(5)], y5[:])
+        w1, w2, w3, w4 = quantize_w(rounded14, 0, 4, "14", RAW0 - 1024)
+        (w0,) = quantize_w(rounded0, 0, 1, "0")
 
-        ys = placed("ys", [P, SPLIT], F32, RAW4 + 1024)
-        acc_shared = bank("acc_shared01", 0)
-        sums(acc_shared[:], w8, words01[:], scales03[:, slots(0, 2)])
-        silu(ys[:, :BANK], acc_shared[:], E)
+        ys = placed("ys", [P, 5 * C - SPLIT], F32, RAW0 + 1024)
+        acc_shared = bank("acc_shared34", 0)
+        sums(acc_shared[:], w8, words35[:, slots(0, 2)], scales05[:, slots(3, 2)])
+        silu(ys[:, 3 * C - SPLIT :], acc_shared[:], E)
         acc_rest = bank("acc_shared2", 1)
-        sums(acc_rest[:, :128], w8, words23[:, :128], scales03[:, BANK : BANK + 128])
-        sums(acc_rest[:, 128:192], w8, words23[:, 128:192], scales03[:, BANK + 128 : BANK + 192])
-        silu(ys[:, BANK:], acc_rest[:, : SPLIT - BANK], E)
-        expert(0, 2, w0, words01, scales03[:, slots(0)])
-        expert(1, 3, w1, words01, scales03[:, slots(1)])
-        expert(2, 4, w2, words23, scales03[:, slots(2)])
-        expert(3, 5, w3, words23, scales03[:, slots(3)])
-        expert(4, 6, w4, words45, scales03[:, slots(4)])
+        sums(acc_rest[:, :64], w8, words02[:, 576:640], scales05[:, 576:640])
+        sums(acc_rest[:, 64:192], w8, words02[:, 640:768], scales05[:, 640:768])
+        silu(ys[:, : 3 * C - SPLIT], acc_rest[:, SPLIT - 576 : 192], E)
+        expert(4, 2, w4, words35[:, slots(1)], scales05[:, slots(4)])
+        expert(3, 3, w3, words35[:, slots(0)], scales05[:, slots(3)])
+        expert(2, 4, w2, words02[:, slots(2)], scales05[:, slots(2)])
+        expert(1, 5, w1, words02[:, slots(1)], scales05[:, slots(1)])
+        expert(0, 6, w0, words02[:, slots(0)], scales05[:, slots(0)])
 
-        nc.vector.tensor_tensor(gated[:, slots(5)], y5[:], gate56[:, slots(0)], MULT)
-        nc.vector.tensor_tensor(window_s[:].indirect(slot_list(6 * C, C)), y[:, slots(6)], gate56[:, slots(1)], MULT)
-        product(0, 3, gate02[:])
-        product(3, 2, gate34[:])
-        scalar_scatter(5 * C, C)
-        nc.vector.tensor_tensor(window_v[:].indirect(slot_list(0, SPLIT)), gated[:, :SPLIT], ys[:], ADD)
-        nc.scalar.activation(
-            window_s[:].indirect(slot_list(SPLIT, 5 * C - SPLIT)), gated[:, SPLIT : 5 * C], COPY, scale=one[:]
+        product(6, 1, gate56[:, slots(1)])
+        nc.vector.tensor_tensor(window_s[:].indirect(slot_list(5 * C, C)), y5[:], gate56[:, slots(0)], MULT)
+        product(2, 3, gate24[:])
+        product(0, 2, gate01[:])
+        scalar_scatter(6 * C, C)
+        nc.vector.tensor_tensor(
+            window_v[:].indirect(slot_list(SPLIT, 5 * C - SPLIT)), gated[:, SPLIT : 5 * C], ys[:], ADD
         )
+        nc.scalar.activation(window_s[:].indirect(slot_list(0, SPLIT)), gated[:, :SPLIT], COPY, scale=one[:])
 
         total = placed("total", [P, T], F32)
         first = 0

@@ -27,8 +27,7 @@ BANK = 512
 ALIGN = 64
 FIRST_ROW = 112
 RAW0 = 1024
-GATE7 = 8192
-SPLIT = 608
+SPLIT = 576
 STORE_WIDTHS = (256, 256, 256, 512, 512, 256)
 assert sum(STORE_WIDTHS) == T
 
@@ -131,35 +130,36 @@ def tile_moe_shr_lin_silu_kernel(tc, x_words, x_scales, w, b, gate, offs, out):
         nc.gpsimd.memset(window_s[:], 0.0)
         window_v = placed("window_v", [P, T], F32)
 
-        raw57 = load_w(5, 3)
+        raw67 = load_w(6, 2)
         token_words = placed("token_words", [P, T], I32)
         words_hbm = x_words[0].rearrange("p t r -> p (t r)").bitcast(I32)
         nc.sync.dma_start(token_words[:, : T // 2], words_hbm[:, : T // 2])
         nc.sync.dma_start(token_words[:, T // 2 :], words_hbm[:, T // 2 :])
         raw4 = load_w(4, 1)
+        raw5 = load_w(5, 1)
         raw3 = load_w(3, 1)
         raw12 = load_w(1, 2)
-        gate7 = load_gate(7, 1, GATE7)
+        gate7 = load_gate(7, 1)
 
-        picked = placed("picked", [P, 6 * C], U8)
-        nc.vector.tensor_copy(picked[:], spread_scales[:].indirect(slot_list(0, 6 * C)))
-        scales05 = placed("slot_scales0", [P, 6 * C], U8)
+        picked = placed("picked", [P, 5 * C], U8)
+        nc.vector.tensor_copy(picked[:], spread_scales[:].indirect(slot_list(0, 5 * C)))
+        rounded8 = placed("rounded8", [P, 1, N, PACK], BF16)
+        round_on_scalar(rounded8, 0, raw8[0])
+        (w8,) = quantize_w(rounded8, 0, 1, "8")
+        scales57 = gather_scales(5, 3)
+        scales04 = placed("slot_scales0", [P, 5 * C], U8)
         for r in range(SCALE_ROWS):
             nc.sync.dma_start(
-                scales05[r:P:QUADRANT, :].bitcast(I32), picked[FIRST_ROW + r : P : SCALE_ROWS, :].bitcast(I32)
+                scales04[r:P:QUADRANT, :].bitcast(I32), picked[FIRST_ROW + r : P : SCALE_ROWS, :].bitcast(I32)
             )
         raw0 = load_w(0, 1, RAW0)
         gate24 = load_gate(2, 3)
         gate56 = load_gate(5, 2)
         gate01 = load_gate(0, 2)
-        rounded8 = placed("rounded8", [P, 1, N, PACK], BF16)
-        round_on_scalar(rounded8, 0, raw8[0])
-        (w8,) = quantize_w(rounded8, 0, 1, "8")
-        scales67 = gather_scales(6, 2)
-        rounded57 = placed("rounded57", [P, 3, N, PACK], BF16)
-        for i, raw in enumerate(raw57):
-            round_on_scalar(rounded57, i, raw)
-        w5, w6, w7 = quantize_w(rounded57, 0, 3, "57")
+        rounded67 = placed("rounded67", [P, 2, N, PACK], BF16)
+        round_on_scalar(rounded67, 1, raw67[1])
+        round_on_scalar(rounded67, 0, raw67[0])
+        w6, w7 = quantize_w(rounded67, 0, 2, "67")
 
         def shared_tokens(quarter):
             cols = slice(quarter * BANK, (quarter + 1) * BANK)
@@ -180,44 +180,44 @@ def tile_moe_shr_lin_silu_kernel(tc, x_words, x_scales, w, b, gate, offs, out):
         for quarter in range(4):
             shared_tokens(quarter)
         words67 = gather_words(6, 2)
-        expert(7, 4, w7, words67[:, slots(1)], scales67[:, slots(1)])
-        expert(6, 5, w6, words67[:, slots(0)], scales67[:, slots(0)])
-        rounded14 = placed("rounded14", [P, 4, N, PACK], BF16)
-        round_on_scalar(rounded14, 0, raw12[0])
-        round_on_scalar(rounded14, 1, raw12[1])
+        rounded25 = placed("rounded25", [P, 4, N, PACK], BF16)
+        rounded01 = placed("rounded01", [P, 2, N, PACK], BF16)
+        round_on_scalar(rounded25, 3, raw5[0])
+        expert(7, 4, w7, words67[:, slots(1)], scales57[:, slots(2)])
+        expert(6, 5, w6, words67[:, slots(0)], scales57[:, slots(1)])
+        round_on_scalar(rounded25, 0, raw12[1])
+        round_on_scalar(rounded01, 1, raw12[0])
         words35 = gather_words(3, 3)
         words02 = gather_words(0, 3)
 
-        round_on_gpsimd(rounded14, 3, raw4[0])
-        round_on_gpsimd(rounded14, 2, raw3[0])
+        round_on_gpsimd(rounded25, 2, raw4[0])
+        round_on_gpsimd(rounded25, 1, raw3[0])
         nc.gpsimd.tensor_tensor(gated[:, slots(7)], y[:, slots(7)], gate7[:], MULT)
-        rounded0 = placed("rounded0", [P, 1, N, PACK], BF16, GATE7 - 512)
-        round_on_gpsimd(rounded0, 0, raw0[0])
+        round_on_gpsimd(rounded01, 0, raw0[0])
         scalar_scatter(7 * C, C)
-        y5 = placed("y5", [P, C], F32, GATE7 + 512)
-        expert(5, 7, w5, words35[:, slots(2)], scales05[:, slots(5)], y5[:])
-        w1, w2, w3, w4 = quantize_w(rounded14, 0, 4, "14", RAW0 - 1024)
-        (w0,) = quantize_w(rounded0, 0, 1, "0")
+        w2, w3, w4, w5 = quantize_w(rounded25, 0, 4, "25", RAW0 - 1024)
+        w0, w1 = quantize_w(rounded01, 0, 2, "01")
 
         ys = placed("ys", [P, 5 * C - SPLIT], F32, RAW0 + 1024)
         acc_shared = bank("acc_shared34", 0)
-        sums(acc_shared[:], w8, words35[:, slots(0, 2)], scales05[:, slots(3, 2)])
+        sums(acc_shared[:], w8, words35[:, slots(0, 2)], scales04[:, slots(3, 2)])
         silu(ys[:, 3 * C - SPLIT :], acc_shared[:], E)
         acc_rest = bank("acc_shared2", 1)
-        sums(acc_rest[:, :64], w8, words02[:, 576:640], scales05[:, 576:640])
-        sums(acc_rest[:, 64:192], w8, words02[:, 640:768], scales05[:, 640:768])
+        sums(acc_rest[:, :64], w8, words02[:, 576:640], scales04[:, 576:640])
+        sums(acc_rest[:, 64:192], w8, words02[:, 640:768], scales04[:, 640:768])
         silu(ys[:, : 3 * C - SPLIT], acc_rest[:, SPLIT - 576 : 192], E)
-        expert(4, 2, w4, words35[:, slots(1)], scales05[:, slots(4)])
-        expert(3, 3, w3, words35[:, slots(0)], scales05[:, slots(3)])
-        expert(2, 4, w2, words02[:, slots(2)], scales05[:, slots(2)])
-        expert(1, 5, w1, words02[:, slots(1)], scales05[:, slots(1)])
-        expert(0, 6, w0, words02[:, slots(0)], scales05[:, slots(0)])
+        expert(5, 7, w5, words35[:, slots(2)], scales57[:, slots(0)])
+        expert(4, 2, w4, words35[:, slots(1)], scales04[:, slots(4)])
+        expert(3, 3, w3, words35[:, slots(0)], scales04[:, slots(3)])
+        expert(2, 4, w2, words02[:, slots(2)], scales04[:, slots(2)])
+        expert(1, 5, w1, words02[:, slots(1)], scales04[:, slots(1)])
+        expert(0, 6, w0, words02[:, slots(0)], scales04[:, slots(0)])
 
-        product(6, 1, gate56[:, slots(1)])
-        nc.vector.tensor_tensor(window_s[:].indirect(slot_list(5 * C, C)), y5[:], gate56[:, slots(0)], MULT)
+        nc.vector.tensor_tensor(window_s[:].indirect(slot_list(6 * C, C)), y[:, slots(6)], gate56[:, slots(1)], MULT)
+        product(5, 1, gate56[:, slots(0)])
         product(2, 3, gate24[:])
         product(0, 2, gate01[:])
-        scalar_scatter(6 * C, C)
+        scalar_scatter(5 * C, C)
         nc.vector.tensor_tensor(
             window_v[:].indirect(slot_list(SPLIT, 5 * C - SPLIT)), gated[:, SPLIT : 5 * C], ys[:], ADD
         )

@@ -28,7 +28,7 @@ ALIGN = 64
 FIRST_ROW = 112
 RAW0 = 1024
 SPLIT = 576
-STORE_WIDTHS = (256, 256, 256, 512, 512, 256)
+STORE_WIDTHS = (128, 128, 256, 512, 512, 256, 256)
 assert sum(STORE_WIDTHS) == T
 
 

from contextlib import ExitStack

import concourse.mybir as mybir

K, T, E, C, N = 512, 2048, 8, 256, 128
FLOPS = 2 * K * N * (E * C + T)

F32 = mybir.dt.float32
BF16 = mybir.dt.bfloat16
I32 = mybir.dt.int32
U32 = mybir.dt.uint32
U16 = mybir.dt.uint16
U8 = mybir.dt.uint8
FP8X4 = mybir.dt.float8_e4m3fn_x4
SILU = mybir.ActivationFunctionType.Silu
COPY = mybir.ActivationFunctionType.Copy
MULT = mybir.AluOpType.mult
ADD = mybir.AluOpType.add

P = 128
QUADRANT = 32
SCALE_ROWS = 4
PACK = 4
RUN = 4
LIST_COLUMN = 16
BANK = 512
ALIGN = 64
FIRST_ROW = 112
RAW0 = 1024
SPLIT = 576
STORE_WIDTHS = (128, 128, 256, 512, 512, 256, 256)
assert sum(STORE_WIDTHS) == T


def tile_moe_shr_lin_silu_kernel(tc, x_words, x_scales, w, b, gate, offs, out):
    nc = tc.nc
    with ExitStack() as ctx:
        sbuf = ctx.enter_context(tc.tile_pool(name="sbuf", bufs=1))
        reused = ctx.enter_context(tc.tile_pool(name="reused", bufs=1))
        psum = ctx.enter_context(tc.psum_pool(name="psum", bufs=1))

        def placed(name, shape, dtype, at=None):
            if at is None:
                return sbuf.tile(shape, dtype, name=name, align_bytes=ALIGN)
            return reused.tile(shape, dtype, name=name, offset=at, align_bytes=ALIGN)

        def slots(first, count=1):
            return slice(first * C, (first + count) * C)

        def slot_list(first, count):
            return offsets[:, first // LIST_COLUMN : (first + count) // LIST_COLUMN]

        def load_w(first, count, at=None):
            raw = placed("w_raw%d" % first, [P, count, PACK, N], F32, at)
            nc.sync.dma_start(raw[:], w[first : first + count].rearrange("e (p j) n -> p e j n", j=PACK))
            return [raw[:, e] for e in range(count)]

        def load_gate(first, count, at=None):
            part = placed("gate%d" % first, [P, count * C], F32, at)
            nc.sync.dma_start(part[:], gate[:, slots(first, count)])
            return part

        def round_on_scalar(rounded, i, raw):
            nc.scalar.copy(
                rounded[:, i].rearrange("p (c i) j -> p c j i", i=RUN),
                raw.rearrange("p j (c i) -> p c j i", i=RUN),
            )

        def round_on_gpsimd(rounded, i, raw):
            nc.gpsimd.tensor_scalar(rounded[:, i], raw.rearrange("p j n -> p n j"), 1.0, 0.0, MULT, ADD)

        def quantize_w(rounded, first, count, name, at=None):
            codes = placed("w_words_" + name, [P, count * N], U32, at)
            scales = placed("w_scales_" + name, [P, count * N], U8)
            nc.vector.quantize_mx(
                out=codes[:].bitcast(FP8X4),
                scales=scales[:],
                in_=rounded[:, first : first + count].rearrange("p e n j -> p (e n j)"),
            )
            return [(codes[:, i * N : (i + 1) * N], scales[:, i * N : (i + 1) * N]) for i in range(count)]

        def gather_scales(first, count, at=None):
            picked = placed("slot_scales%d" % first, [P, count * C], U8, at)
            nc.vector.tensor_copy(picked[:], token_scales[:].indirect(slot_list(first * C, count * C)))
            return picked

        def gather_words(first, count, at=None):
            picked = placed("slot_words%d" % first, [P, count * C], U32, at)
            nc.vector.tensor_copy(picked[:], token_words[:].bitcast(U32).indirect(slot_list(first * C, count * C)))
            return picked

        def sums(acc, stationary, words, scales):
            nc.tensor.matmul_mx(
                out=acc,
                lhsT=stationary[0].bitcast(FP8X4),
                lhsT_scale=stationary[1],
                rhs=words.bitcast(FP8X4),
                rhs_scale=scales,
                start=True,
                stop=True,
            )

        def silu(result, acc, e):
            nc.scalar.activation(result, acc, SILU, bias=bias[:, e : e + 1])

        def bank(name, number):
            return psum.tile([P, BANK], F32, name=name, tag="bank%d" % number)

        def scalar_scatter(first, count):
            nc.scalar.activation(window_s[:].indirect(slot_list(first, count)), gated[:, first : first + count], COPY)

        token_scales = placed("token_scales", [P, T], U8)
        nc.gpsimd.memset(token_scales[:].bitcast(I32), 0)
        spread_scales = placed("spread_scales", [P, T], U8)
        nc.scalar.dma_start(spread_scales[FIRST_ROW:P, :].bitcast(I32), x_scales[0].bitcast(I32))
        nc.vector.memset(spread_scales[0:FIRST_ROW, :].bitcast(I32), 0)
        offsets = sbuf.tile([P, E * C // LIST_COLUMN], U16, name="offsets")
        nc.sync.dma_start(offsets[:], offs)
        raw8 = load_w(8, 1)
        for r in range(SCALE_ROWS):
            nc.sync.dma_start(token_scales[r:P:QUADRANT, :].bitcast(I32), x_scales[0, r:16:SCALE_ROWS, :].bitcast(I32))
        warm_up = sbuf.tile([P, 2], F32, name="warm_up")
        nc.vector.memset(warm_up[:, 0:1], 0.0)
        nc.scalar.activation(warm_up[:, 1:2], warm_up[:, 0:1], SILU)
        one = sbuf.tile([P, 1], F32, name="one")
        nc.vector.memset(one[:], 1.0)
        bias = sbuf.tile([P, E + 1], F32, name="bias")
        nc.gpsimd.dma_start(bias[:], b)
        window_s = placed("window_s", [P, T], F32)
        nc.gpsimd.memset(window_s[:], 0.0)
        window_v = placed("window_v", [P, T], F32)

        raw67 = load_w(6, 2)
        token_words = placed("token_words", [P, T], I32)
        words_hbm = x_words[0].rearrange("p t r -> p (t r)").bitcast(I32)
        nc.sync.dma_start(token_words[:, : T // 2], words_hbm[:, : T // 2])
        nc.sync.dma_start(token_words[:, T // 2 :], words_hbm[:, T // 2 :])
        raw4 = load_w(4, 1)
        raw5 = load_w(5, 1)
        raw3 = load_w(3, 1)
        raw12 = load_w(1, 2)
        gate7 = load_gate(7, 1)

        picked = placed("picked", [P, 5 * C], U8)
        nc.vector.tensor_copy(picked[:], spread_scales[:].indirect(slot_list(0, 5 * C)))
        rounded8 = placed("rounded8", [P, 1, N, PACK], BF16)
        round_on_scalar(rounded8, 0, raw8[0])
        (w8,) = quantize_w(rounded8, 0, 1, "8")
        scales57 = gather_scales(5, 3)
        scales04 = placed("slot_scales0", [P, 5 * C], U8)
        for r in range(SCALE_ROWS):
            nc.sync.dma_start(
                scales04[r:P:QUADRANT, :].bitcast(I32), picked[FIRST_ROW + r : P : SCALE_ROWS, :].bitcast(I32)
            )
        raw0 = load_w(0, 1, RAW0)
        gate24 = load_gate(2, 3)
        gate56 = load_gate(5, 2)
        gate01 = load_gate(0, 2)
        rounded67 = placed("rounded67", [P, 2, N, PACK], BF16)
        round_on_scalar(rounded67, 1, raw67[1])
        round_on_scalar(rounded67, 0, raw67[0])
        w6, w7 = quantize_w(rounded67, 0, 2, "67")

        def shared_tokens(quarter):
            cols = slice(quarter * BANK, (quarter + 1) * BANK)
            acc = bank("acc_tokens%d" % quarter, quarter)
            sums(acc[:], w8, token_words[:, cols].bitcast(U32), token_scales[:, cols])
            silu(window_v[:, cols], acc[:], E)

        def expert(e, number, stationary, words, scales, result=None):
            acc = bank("acc%d" % e, number)
            sums(acc[:, :C], stationary, words, scales)
            silu(y[:, slots(e)] if result is None else result, acc[:, :C], e)

        def product(first, count, gate_part):
            nc.vector.tensor_tensor(gated[:, slots(first, count)], y[:, slots(first, count)], gate_part, MULT)

        y = placed("y", [P, T], F32)
        gated = placed("gated", [P, T], F32)
        for quarter in range(4):
            shared_tokens(quarter)
        words67 = gather_words(6, 2)
        rounded25 = placed("rounded25", [P, 4, N, PACK], BF16)
        rounded01 = placed("rounded01", [P, 2, N, PACK], BF16)
        round_on_scalar(rounded25, 3, raw5[0])
        expert(7, 4, w7, words67[:, slots(1)], scales57[:, slots(2)])
        expert(6, 5, w6, words67[:, slots(0)], scales57[:, slots(1)])
        round_on_scalar(rounded25, 0, raw12[1])
        round_on_scalar(rounded01, 1, raw12[0])
        words35 = gather_words(3, 3)
        words02 = gather_words(0, 3)

        round_on_gpsimd(rounded25, 2, raw4[0])
        round_on_gpsimd(rounded25, 1, raw3[0])
        nc.gpsimd.tensor_tensor(gated[:, slots(7)], y[:, slots(7)], gate7[:], MULT)
        round_on_gpsimd(rounded01, 0, raw0[0])
        scalar_scatter(7 * C, C)
        w2, w3, w4, w5 = quantize_w(rounded25, 0, 4, "25", RAW0 - 1024)
        w0, w1 = quantize_w(rounded01, 0, 2, "01")

        ys = placed("ys", [P, 5 * C - SPLIT], F32, RAW0 + 1024)
        acc_shared = bank("acc_shared34", 0)
        sums(acc_shared[:], w8, words35[:, slots(0, 2)], scales04[:, slots(3, 2)])
        silu(ys[:, 3 * C - SPLIT :], acc_shared[:], E)
        acc_rest = bank("acc_shared2", 1)
        sums(acc_rest[:, :64], w8, words02[:, 576:640], scales04[:, 576:640])
        sums(acc_rest[:, 64:192], w8, words02[:, 640:768], scales04[:, 640:768])
        silu(ys[:, : 3 * C - SPLIT], acc_rest[:, SPLIT - 576 : 192], E)
        expert(5, 7, w5, words35[:, slots(2)], scales57[:, slots(0)])
        expert(4, 2, w4, words35[:, slots(1)], scales04[:, slots(4)])
        expert(3, 3, w3, words35[:, slots(0)], scales04[:, slots(3)])
        expert(2, 4, w2, words02[:, slots(2)], scales04[:, slots(2)])
        expert(1, 5, w1, words02[:, slots(1)], scales04[:, slots(1)])
        expert(0, 6, w0, words02[:, slots(0)], scales04[:, slots(0)])

        nc.vector.tensor_tensor(window_s[:].indirect(slot_list(6 * C, C)), y[:, slots(6)], gate56[:, slots(1)], MULT)
        product(5, 1, gate56[:, slots(0)])
        product(2, 3, gate24[:])
        product(0, 2, gate01[:])
        scalar_scatter(5 * C, C)
        nc.vector.tensor_tensor(
            window_v[:].indirect(slot_list(SPLIT, 5 * C - SPLIT)), gated[:, SPLIT : 5 * C], ys[:], ADD
        )
        nc.scalar.activation(window_s[:].indirect(slot_list(0, SPLIT)), gated[:, :SPLIT], COPY, scale=one[:])

        total = placed("total", [P, T], F32)
        first = 0
        for width in STORE_WIDTHS:
            cols = slice(first, first + width)
            nc.vector.tensor_tensor(total[:, cols], window_v[:, cols], window_s[:, cols], ADD)
            nc.sync.dma_start(out[:, cols], total[:, cols])
            first = first + width
